import numpy as np, ml_dtypes
CORES = [24,25,26,27,28,29,30,31]
N = 8
BF = ml_dtypes.bfloat16
def gentries(a):
    return np.ascontiguousarray(a.reshape(8, 16, -1).transpose(0, 2, 1)).reshape(8, -1)
def gtable(e):
    e = np.asarray(e); return np.ascontiguousarray(e.reshape(8, -1, 16).transpose(0, 2, 1)).reshape(128, -1).astype(np.int32)
V, D, SD, L, M, P, RO, ST = 2048, 4, 2, 128, 768, 32, 2, 3
DV, E = D * V, (N - 1) * L
def wire(rng, nm, no, vd, od=None, oa=None):
    if od is None: od = np.argsort(rng.random((N, 8, DV)), axis=2)
    if oa is None: oa = np.argsort(rng.random((N, 8, DV)), axis=2)
    a = np.full((N, 8, DV), -1, np.int64); b = np.full((N, 8, DV), -1, np.int64)
    ni = np.zeros((N, 8), np.int64); nu = np.zeros((N, 8), np.int64)
    for g in range(8):
        for q in range(N):
            for h in range(N - 1):
                r = (q + h + 1) % N; m = int(nm[q, g, h]); n = m + int(no[q, g, h])
                c = DV + D * (h * L + rng.permutation(L)[:n])
                i = int(nu[q, g]); b[q, g, oa[q, g, i:i + n]] = c; nu[q, g] += n
                i = int(ni[r, g]); a[r, g, od[r, g, i:i + m]] = c[:m]; ni[r, g] += m
        for q in range(N):
            i, j = int(ni[q, g]), int(nu[q, g]); n = max(min(DV - i - int(vd[q, g]), DV - j), 0)
            sd = od[q, g, i:i + n]; sa = oa[q, g, j:j + n]; a[q, g, sd] = sa; b[q, g, sa] = sd
    return a, b
def parts(rng):
    x = rng.integers(0, 16, (N, 8, 16, V))
    nm = rng.integers(L // 2, 3 * L // 4, (N, 8, N - 1)); no = rng.integers(0, L // 8 + 1, (N, 8, N - 1))
    vd = rng.integers(M // 2, 3 * M // 2, (N, 8)); p = np.zeros((N, 8, 4 + RO), np.int64)
    p[..., 0] = rng.integers(95, 112, (N, 8)); p[..., 1] = rng.integers(112, 150, (N, 8)); p[..., 2] = rng.integers(130, 147, (N, 8))
    p[..., 3] = 2 * rng.integers(0, 1024, (N, 8)) + 1; p[..., 4:] = rng.integers(0, DV, (N, 8, RO))
    return x, nm, no, vd, p
def pack(x, ab, p):
    return {"x0": np.ascontiguousarray(x.reshape(N, 128, V)).astype(BF), "den": np.stack([gtable(c) for c in ab[0]]), "axo": np.stack([gtable(c) for c in ab[1]]), "par": p.astype(np.int32)}
def setup_inputs(rng):
    x, nm, no, vd, p = parts(rng)
    return pack(x, wire(rng, nm, no, vd), p)
def setup_inputs_caps(rng):
    x, nm, no, vd, p = parts(rng); p[..., 0] = 0; p[..., 1] = 241; p[..., 2] = 241
    nm[:] = rng.choice(np.array([0, 1, L // 2, L - 1, L]), (1, 8, N - 1)); nm[:, 3:5] = L // 2
    no[:] = np.minimum(rng.choice(np.array([0, 1, 7, L]), no.shape), L - nm); no[1, :, 0] = L - nm[1, :, 0]; no[1, 3:5, N - 2] = 5
    nm[:, 5] = 0; no[1:, 5] = L; no[0] = 0
    vd[:] = rng.choice(np.array([0, 1, M - 1, M, M + 1, 2 * M]), (N, 8)); vd[0] = np.array([M, M + 1, M - 1, 0, 1, 2 * M, M, 5])
    return pack(x, wire(rng, nm, no, vd), p)
def setup_inputs_full(rng):
    x, nm, no, vd, p = parts(rng); nm[:] = L; no[:] = 0; vd[:] = 0
    p[..., 0] = rng.integers(105, 136, (N, 8)); p[..., 1] = rng.integers(90, 242, (N, 8)); p[..., 2] = rng.integers(105, 136, (N, 8))
    return pack(x, wire(rng, nm, no, vd), p)
def setup_inputs_alike(rng):
    x, nm, no, vd, p = parts(rng)
    od = np.argsort(rng.random((N, 8, DV)), axis=2); oa = np.argsort(rng.random((N, 8, DV)), axis=2); o = np.arange(DV)
    od[:, 0] = o; oa[:, 0] = o; od[:, 1] = o[::-1]; oa[:, 2] = o[::-1]
    for q in range(N):
        od[q, 3] = (D * rng.permutation(V)[:, None] + np.arange(D)).reshape(-1); oa[q, 3] = (D * rng.permutation(V)[:, None] + np.arange(D)).reshape(-1)
    x[:, 0:4:2] = 2 * rng.integers(0, 8, (N, 2, 1, 1)) + 1; x[:, 1:4:2] = rng.integers(0, 16, (N, 2, 1, V))
    p[:, :4, 0] = 16 * rng.integers(3, 8, (N, 4)); p[:, :4, 1] = 16 * rng.integers(7, 16, (N, 4)); p[:, :4, 2] = 16 * rng.integers(8, 13, (N, 4))
    p[:, 0::4, 3] = 1; p[:, 0::4, 4:] = 0; p[:, 1::4, 3] = 2047; p[:, 1::4, 4:] = DV - 1
    return pack(x, wire(rng, nm, no, vd, od, oa), p)
def setup_inputs_bare(rng):
    x, nm, no, vd, p = parts(rng); g = rng.permutation(8); q = int(rng.integers(0, N))
    nm[:, g[0]] = 0; no[:, g[0]] = 0; vd[:, g[0]] = DV
    nm[:, g[1]] = 0; no[:, g[1]] = rng.integers(0, L + 1, (N, N - 1)); vd[:, g[1]] = M
    vd[:, g[2]] = DV
    p[:, g[3], :3] = np.array([0, 0, 241]); p[:, g[4], :3] = np.array([241, 241, 0])
    nm[q] = 0; no[q] = 0
    return pack(x, wire(rng, nm, no, vd), p)
def setup_inputs_spread(rng):
    x, nm, no, vd, p = parts(rng)
    x = np.minimum((np.exp2(4.2 * rng.random((N, 8, 1, V))) * rng.random(x.shape)).astype(np.int64), 15)
    p[..., :3] = rng.integers(0, 242, (N, 8, 3))
    nm = rng.integers(0, L + 1, nm.shape); no = ((L - nm + 1) * rng.random(nm.shape)).astype(np.int64)
    vd = np.exp2(12.9 * rng.random((N, 8))).astype(np.int64)
    return pack(x, wire(rng, nm, no, vd), p)
def ends(c):
    o = np.full((N, 8, E), -1, np.int64); n, g, i = np.nonzero(c >= DV)
    o[n, g, (c[n, g, i] - DV) >> SD] = i
    return o
def gone(c, f):
    return (c >= DV) & np.take_along_axis(f, np.maximum(c - DV, 0) >> SD, 2)
def check_inputs(d):
    bad = []
    x = np.asarray(d["x0"]).astype(np.float32); p = np.asarray(d["par"]).astype(np.int64)
    if not np.all((x >= 0) & (x <= 15) & (x == np.floor(x))): bad.append("range of x0")
    if not np.all((p[..., :3] >= 0) & (p[..., :3] <= 241)): bad.append("range of the thresholds in par")
    if not np.all((p[..., 3] >= 1) & (p[..., 3] <= 2047) & ((p[..., 3] & 1) == 1)): bad.append("K in par")
    if not np.all((p[..., 4:] >= 0) & (p[..., 4:] < DV)): bad.append("C in par")
    a = np.stack([gentries(c) for c in d["den"]]).astype(np.int64); b = np.stack([gentries(c) for c in d["axo"]]).astype(np.int64)
    out = False
    for k, c in (("den", a), ("axo", b)):
        if not np.all((c >= -1) & (c < DV + D * E) & ((c < DV) | ((c & (D - 1)) == 0))): bad.append("range of " + k); out = True
    if out: return bad
    for k, c, o in (("den", a, b), ("axo", b, a)):
        n, g, i = np.nonzero(c >= DV); key = (n * 8 + g) * E + ((c[n, g, i] - DV) >> SD)
        if np.unique(key).size != key.size: bad.append("a link that stands twice in " + k)
        n, g, i = np.nonzero((c >= 0) & (c < DV))
        if np.any(o[n, g, c[n, g, i]] != i): bad.append("twins of " + k)
    ie, oe = ends(a), ends(b)
    for r in range(N):
        for h in range(1, N):
            z = slice((h - 1) * L, h * L)
            if np.any((ie[r][:, z] >= 0) & (oe[(r - h) % N][:, z] < 0)): bad.append("a link in den that no axonal slot holds")
    return sorted(set(bad))
def reference(x0, den, axo, par):
    x = np.asarray(x0).astype(np.float32).astype(np.int32).reshape(N, 8, 16, V)
    a = np.stack([gentries(c) for c in den]).astype(np.int64); b = np.stack([gentries(c) for c in axo]).astype(np.int64); p = par.astype(np.int64)
    blocks = [(r, (r - h) % N, slice((h - 1) * L, h * L)) for r in range(N) for h in range(1, N)]
    for t in range(RO):
        oe = ends(b)
        for k in range(ST):
            new, far = [], []
            for r in range(N):
                w = [x[r]]
                for h in range(1, N):
                    q = (r - h) % N; i = oe[q][:, (h - 1) * L:h * L]
                    w.append(np.take_along_axis(x[q], np.maximum(i, 0)[:, None, :] >> SD, 2) * (i >= 0)[:, None, :])
                w = np.concatenate(w, axis=2); held = a[r] >= 0
                v = (np.take_along_axis(w, np.maximum(a[r], 0)[:, None, :] >> SD, 2) * held[:, None, :]).reshape(8, 16, V, D)
                if k == ST - 1: far.append(np.where(held.reshape(8, V, D), np.add.reduce(np.abs(v - x[r][..., None]), axis=1), -1))
                new.append((x[r] + np.add.reduce(v, axis=3)) & 15)
            x = np.stack(new).astype(np.int32)
        far = np.stack(far); s = np.add.reduce(x, axis=2)
        best = np.argmax(far, axis=3)
        kd = ((s >= p[..., 2:3])[..., None] & (far >= 0) & (np.arange(D) == best[..., None])).reshape(N, 8, DV)
        ka = ((s < p[..., 0:1])[..., None] & (np.arange(D) == t)).reshape(N, 8, DV) & (b >= 0)
        mb = np.zeros((N, 8, DV + D * E), bool); n, g, i = np.nonzero(kd); mb[n, g, a[n, g, i]] = True
        ma = np.zeros((N, 8, DV + D * E), bool); n, g, i = np.nonzero(ka); ma[n, g, b[n, g, i]] = True
        gi = np.zeros((N, 8, E), bool); go = np.zeros((N, 8, E), bool)
        for r, q, z in blocks:
            gi[r][:, z] = ma[q][:, DV::D][:, z]; go[q][:, z] = mb[r][:, DV::D][:, z]
        a = np.where(kd | ma[..., :DV] | gone(a, gi), -1, a); b = np.where(ka | mb[..., :DV] | gone(b, go), -1, b)
        oe, ie = ends(b), ends(a); opn = np.zeros((N, 8, E), bool)
        for r, q, z in blocks: opn[r][:, z] = (oe[q][:, z] >= 0) & (ie[r][:, z] < 0)
        z0 = (t % (N - 1)) * L
        for r in range(N):
            for g in range(8):
                vac = np.nonzero((a[r, g] < 0) & np.repeat(s[r, g] < p[r, g, 1], D))[0][:M]
                links = np.nonzero(opn[r, g])[0]; o = (p[r, g, 3] * np.arange(DV) + p[r, g, 4 + t]) & (DV - 1); fr = o[b[r, g][o] < 0]
                giv = np.concatenate([DV + D * links, fr]); m = min(len(vac), len(giv)); u = max(m - len(links), 0)
                a[r, g, vac[:m]] = giv[:m]
                b[r, g, fr[:u]] = vac[m - u:m]
                rest = fr[u:u + P]; free = np.nonzero(oe[r, g, z0:z0 + L] < 0)[0]; n = min(len(rest), len(free))
                b[r, g, rest[:n]] = DV + D * (z0 + free[:n])
    return {"yx": x.reshape(N, 128, V).astype(np.float32).astype(BF), "yd": np.stack([gtable(c) for c in a]).astype(np.float32), "ya": np.stack([gtable(c) for c in b]).astype(np.float32)}

@@ -1,0 +1,942 @@
+import math
+from concourse.bass import DstId, RemoteDMATransfer
+from concourse.mybir import AluOpType as Op, AxisListType, ActivationFunctionType as Fn
+
+N = 8
+DTY = {"af": "float32", "ab": "bfloat16", "ai": "int32", "au": "uint16", "ah": "float16"}
+SZ = {"float32": 4, "bfloat16": 2, "int32": 4, "uint16": 2, "float16": 2}
+TOP = {k: 0 for k in DTY}
+OPS = []
+ACC = {}
+GC, SC, PEC, HOP = 1.5, 3.5, 0.5, 90.0
+BIAS, LOOK, LOOKF, ROUNDS = 300.0, 300.0, 0.6, 1500
+ND1, ND2, NC3 = 1024, 896, 4
+
+
+def al(k, n):
+    c = TOP[k]
+    TOP[k] = c + (n + 15) // 16 * 16
+    return (k, c, c + n, 1, None)
+
+
+def F(n): return al("af", n)
+def B(n): return al("ab", n)
+def I(n): return al("ai", n)
+def U(n): return al("au", n)
+def H(n): return al("ah", n)
+def sl(r, a, b, st=1): return (r[0], r[1] + a, r[1] + b, st, r[4])
+def pp(r, p): return (r[0], r[1], r[2], r[3], p)
+def ps(bank, a, b, st=1): return ("p%d" % (bank // 2), 512 * (bank % 2) + a, 512 * (bank % 2) + b, st, None)
+def ind(w, o): return ("ind", w, o)
+def dr(name, a, b, p=None): return (name, a, b, 1, p)
+def isref(x): return isinstance(x, tuple)
+def wid(r): return 16 * wid(r[2]) if r[0] == "ind" else len(range(r[1], r[2], r[3]))
+def ispsum(r): return r[0][0] == "p" and r[0] != "par"
+def size(r): return size(r[1]) if r[0] == "ind" else (4 if ispsum(r) else SZ[DTY[r[0]]])
+def half(*rs): return 0.5 if all(size(r) == 2 for r in rs) else 1.0
+def flt(*rs): return all(ispsum(r) or DTY[(r[1] if r[0] == "ind" else r)[0]] in ("float32", "bfloat16") for r in rs)
+
+
+def ap(T, r):
+    if not isref(r):
+        return r
+    if r[0] == "ind":
+        return ap(T, r[1]).indirect(ap(T, r[2]))
+    cs = slice(r[1], r[2]) if r[3] == 1 else slice(r[1], r[2], r[3])
+    if r[4] is None:
+        return T[r[0]][:, cs]
+    p = r[4]
+    return T[r[0]][(slice(p[0], p[1]) if p[2] == 1 else slice(p[0], p[1], p[2])), cs]
+
+
+def op(q, fn, reads, writes, cost, lat=0.0, kind="c", n=1, after=None):
+    k = len(OPS)
+    rd, wr = [], []
+    for r in reads:
+        if isref(r):
+            rd += [r[1], r[2]] if r[0] == "ind" else [r]
+    for r in writes:
+        if r[0] == "ind":
+            wr.append(r[1])
+            rd.append(r[2])
+        else:
+            wr.append(r)
+    pre = set()
+    for lst, w in ((rd, False), (wr, True)):
+        for r in lst:
+            psum = ispsum(r)
+            for (o, a, b, ow) in ACC.get(r[0], []):
+                hit = a < r[2] and r[1] < b and (w or ow)
+                if psum and (OPS[o]["q"] != q or q == "x") and a // 512 <= (r[2] - 1) // 512 and r[1] // 512 <= (b - 1) // 512:
+                    hit = True
+                if hit:
+                    pre.add(o)
+    if kind == "recv":
+        pre = set()
+    if after is not None:
+        pre.add(after)
+    for lst, w in ((rd, False), (wr, True)):
+        for r in lst:
+            old = ACC.get(r[0], [])
+            if w:
+                old = [x for x in old if not (r[1] <= x[1] and x[2] <= r[2] and r[3] == 1 and r[4] is None)]
+            ACC[r[0]] = old + [(k, r[1], r[2], w)]
+    OPS.append({"q": q, "fn": fn, "pre": pre, "cost": cost, "lat": lat, "kind": kind, "n": n})
+    return k
+
+
+def vcost(out, ins, base):
+    n = wid(out)
+    if out[0] == "ind":
+        return 50 + SC * n
+    if ins[0][0] == "ind":
+        return 50 + GC * n
+    return max(64, base * n)
+
+
+def act(out, a, f=None, bias=None, scale=None, q="a"):
+    def fn(g, T):
+        kw = {}
+        if bias is not None:
+            kw["bias"] = ap(T, bias)
+        if scale is not None:
+            kw["scale"] = ap(T, scale)
+        return g.scalar.activation(ap(T, out), ap(T, a), Fn.Identity if f is None else f, **kw)
+    return op(q, fn, [a, bias, scale], [out], vcost(out, [a], 1.0))
+
+
+def either(fv, cv, out, a, bias, scale, f=None):
+    k = act(out, a, f, bias, scale, q="x")
+    OPS[k]["alt"] = {"a": (OPS[k]["fn"], OPS[k]["cost"]), "v": (fv, cv)}
+    return k
+
+
+def ts(out, a, s1, o0, s2=None, o1=None):
+    def fn(g, T):
+        if s2 is None:
+            return g.vector.tensor_scalar(ap(T, out), ap(T, a), ap(T, s1), None, o0)
+        return g.vector.tensor_scalar(ap(T, out), ap(T, a), ap(T, s1), ap(T, s2), o0, o1)
+    c = vcost(out, [a], half(out, a))
+    if flt(out, a):
+        if s2 is None and o0 == Op.mult:
+            return either(fn, c, out, a, None, s1)
+        if s2 is None and o0 == Op.add:
+            return either(fn, c, out, a, s1, None)
+        if s2 is not None and o0 == Op.mult and o1 == Op.add:
+            return either(fn, c, out, a, s2, s1)
+    return op("v", fn, [a, s1, s2], [out], c)
+
+
+def tt(out, a, b, o):
+    return op("v", lambda g, T: g.vector.tensor_tensor(ap(T, out), ap(T, a), ap(T, b), o), [a, b], [out],
+              vcost(out, [a], 1.0 if ispsum(a) or ispsum(b) else 2.0))
+
+
+def cp(out, a, zero=False):
+    fn = lambda g, T: g.vector.tensor_copy(ap(T, out), ap(T, a))
+    c = vcost(out, [a], half(out, a))
+    if zero:
+        return either(fn, c, out, a, None, None, Fn.Silu)
+    if flt(out, a) and out[0] != "ind":
+        return either(fn, c, out, a, None, None)
+    return op("v", fn, [a], [out], c)
+
+
+def ms(out, c):
+    return op("v", lambda g, T: g.vector.memset(ap(T, out), c), [], [out], vcost(out, [out], half(out)))
+
+
+def scan(out, d0, d1, init, o0, o1):
+    return op("v", lambda g, T: g.vector.tensor_tensor_scan(ap(T, out), ap(T, d0), ap(T, d1), init, o0, o1), [d0, d1], [out], max(64, wid(out)))
+
+
+def red(out, a):
+    return op("v", lambda g, T: g.vector.tensor_reduce(ap(T, out), ap(T, a), AxisListType.X, Op.add), [a], [out], 64)
+
+
+def iota(out, pat, base, cm):
+    def fn(g, T):
+        if out[0] == "ai":
+            return g.iota(ap(T, out), pat, base, cm)
+        return g.iota(ap(T, out), pat, base, cm, allow_small_or_imprecise_dtypes=True)
+    return op("g", fn, [], [out], 130 + 2 * wid(out))
+
+
+def mm(lst, after=None):
+    def fn(g, T):
+        for (o, l, r, st, sp) in lst:
+            x = g.tensor.matmul(ap(T, o), ap(T, l), ap(T, r), st, sp)
+        return x
+    c = sum(max(64, wid(x[2])) * (4 if size(x[2]) == 4 else 1) for x in lst) * PEC
+    return op("p", fn, [x[1] for x in lst] + [x[2] for x in lst] + [x[0] for x in lst if not x[3]], [x[0] for x in lst], c, lat=60, after=after)
+
+
+def dg(out, src, z, st=True, sp=True):
+    n = wid(src)
+    return [(out, sl(z, 15 - b, 143 - b), sl(src, b, n, 16), st and b == 0, sp and b == 15) for b in range(16)]
+
+
+def full(out, l, src):
+    n = wid(src)
+    return [(sl(out, a, min(a + 512, n)), l, sl(src, a, min(a + 512, n)), True, True) for a in range(0, n, 512)]
+
+
+def dma(pairs, lat=2500.0, q="s"):
+    def fn(g, T):
+        e = g.sync if q == "s" else g.scalar
+        return [e.dma_start(ap(T, o), ap(T, i)) for (o, i) in pairs]
+    return op(q, fn, [x[1] for x in pairs], [x[0] for x in pairs], 60.0 * len(pairs), lat=lat, kind="dma", n=len(pairs))
+
+
+def exch(src, dst, w):
+    k = op("g", (src, dst, w), [src], [], 300.0, lat=2500.0, kind="send")
+    op("n", None, [], [dst], 0.0, lat=1500.0 + 8 * w, kind="recv", after=k)
+
+
+def build():
+    add, sub, mul, mx, mn = Op.add, Op.subtract, Op.mult, Op.max, Op.min
+    ge, le, lt, eq = Op.is_ge, Op.is_le, Op.is_lt, Op.is_equal
+    shr, band = Op.arith_shift_right, Op.bitwise_and
+    R8 = (0, 128, 16)
+    CAP = 928
+    axw, dew, axB, pari = I(512), I(512), I(512), I(8)
+    X, Qb = [B(2960), B(2960)], B(2048)
+    WA, WB = F(10240), F(10240)
+    dma([(axw, dr("axo", 0, 512))])
+    dma([(pp(sl(pari, 0, 6), (0, 8, 1)), dr("par", 0, 6))], q="a")
+    dma([(dew, dr("den", 0, 512))], q="a")
+    Dd = B(8192 + 768)
+    dma([(sl(X[0], 0, 2048), dr("x0", 0, 2048))], lat=3500.0)
+    dma([(sl(axB, 32 * i, 32 * i + 32), dr("axo", 0, 512, (i, 128, 16))) for i in range(16)], lat=5000.0)
+    PAY, HELD, RAW = F(512), F(512), F(512)
+    ci, cf = I(16), F(48)
+    col = lambda k: sl(cf, k, k + 1)
+    pc, pi, gb, z15, d0c, sidb, p16, p16b, fr = [col(k) for k in range(9)]
+    iota(sl(ci, 0, 1), [[0, 1]], 0, 1)
+    RI, NI = F(1024), F(512)
+    iota(sl(RI, 0, 160), [[1, 160]], 0, 0)
+    cp(pc, sl(ci, 0, 1))
+    ts(sl(ci, 1, 2), sl(ci, 0, 1), 15, band)
+    cp(pi, sl(ci, 1, 2))
+    tt(gb, pc, pi, sub)
+    iota(NI, [[16, 512]], 0, 1)
+    iota(sl(RI, 160, 1024), [[1, 864]], 160, 0)
+    ts(col(11), gb, -1.0, mul)
+    ts(NI, NI, col(11), add)
+    R128, R144 = sl(RI, 0, 128), sl(RI, 0, 144)
+    ts(z15, gb, 15.0, add)
+    ts(d0c, pi, 0.0, eq)
+    ts(sidb, pi, -511.0, add)
+    ts(p16, pc, 16.0, mul)
+    ts(p16b, pc, 16.0, mul, 16.0, add)
+    up, tmp, tmp2, Mi = [sl(RAW, 128 * k, 128 * k + 128) for k in range(4)]
+    ts(up, R128, z15, le)
+    BO, TRI, TRH = B(128), B(128), B(128)
+    ts(tmp, R128, gb, ge)
+    tt(BO, tmp, up, mul)
+    ts(tmp2, R128, pc, ge)
+    tt(TRI, tmp2, up, mul)
+    Z, Z4, ZP, Z0, Zf, Z0f, BOf = B(144), B(144), B(144), B(144), F(144), F(144), F(128)
+    ts(Z0, R144, z15, eq, d0c, mul)
+    ts(Z, R144, z15, eq)
+    cp(Zf, Z)
+    cp(Z0f, Z0)
+    ts(Z4, Z, 4.0, mul)
+    p2, p2f = B(1), F(1)
+    act(p2, pi, Fn.Exp, scale=math.log(2.0))
+    cp(p2f, p2)
+    ts(ZP, Z, p2f, mul)
+    cp(BOf, BO)
+    ID, IDf, O24, ONES, CJ = B(128), F(128), B(128), B(512), B(512)
+    ts(ID, R128, pc, eq)
+    cp(IDf, ID)
+    ms(O24, 24.0)
+    ms(ONES, 1.0)
+    for j in range(4):
+        ms(sl(CJ, 128 * j, 128 * j + 128), 4.0 - j)
+    WM = {1: ID}
+    for w in (-0.5, -1, 3, 4, 5, 16, 32, 128, 512, 2048):
+        WM[w] = B(128)
+        ts(WM[w], ID, float(w), mul)
+    tt(TRH, TRI, WM[-0.5], sub)
+    I16, MK32 = B(32), F(32)
+    ts(I16, sl(RI, 0, 32), pi, eq)
+    cp(sl(MK32, 0, 16), sl(I16, 0, 16))
+    cp(sl(MK32, 16, 32), sl(I16, 0, 16))
+    EI, I16f = B(2048), F(16)
+    cp(I16f, sl(I16, 0, 16))
+    for i in range(16):
+        ts(sl(EI, 128 * i, 128 * i + 128), BO, sl(I16f, i, i + 1), mul)
+    TM, TO = B(2048), B(512)
+    ts(Mi, R128, 1.0, add)
+    tt(Mi, Mi, up, mul)
+    ts(sl(ci, 2, 3), sl(ci, 0, 1), 3, band)
+    ts(sl(ci, 3, 4), sl(ci, 0, 1), 2, shr, 3, band)
+    ts(fr, sl(ci, 2, 3), 4.0, mul, gb, add)
+    ts(col(9), sl(ci, 3, 4), 12.0, add, gb, add)
+    ts(col(10), fr, 3.0, add)
+    ZQ, ZB = sl(WB, 4096, 4096 + 576), F(576)
+    zq, zb, tm = sl(Dd, 0, 144), sl(Dd, 144, 288), sl(Dd, 512, 1024)
+    ts(zq, R144, col(9), eq)
+    ts(zb, R144, col(10), eq)
+    for j in range(4):
+        ts(col(32 + j), fr, 1.0 + j, add)
+        ts(col(36 + j), sl(ci, 3, 4), float(j), eq)
+        ts(col(40 + j), sl(ci, 2, 3), float(j), eq)
+        ts(sl(ZQ, 144 * j, 144 * j + 144), zq, col(40 + j), mul)
+        ts(sl(ZB, 144 * j, 144 * j + 144), zb, col(36 + j), mul)
+        ts(sl(tm, 128 * j, 128 * j + 128), Mi, col(32 + j), ge)
+    for a in range(4):
+        ts(sl(TO, 128 * a, 128 * a + 128), BO, col(36 + a), mul)
+        for j in range(4):
+            c = 128 * (4 * a + j)
+            ts(sl(TM, c, c + 128), sl(tm, 128 * j, 128 * j + 128), col(36 + a), mul)
+    DUM, LB32, ZR, DUC, CAPS, d9 = F(128), U(32), F(928), F(36), B(576), F(56)
+    DUL = sl(DUM, 0, 56)
+    ts(DUM, sl(NI, 0, 128), 8192.0, add)
+    ts(DUC, sl(NI, 0, 36), float(CAP), add)
+    ts(d9, sl(NI, 0, 56), 897.0, add)
+    ms(ZR, 0.0)
+    ms(CAPS, float(CAP))
+    ti = I(32)
+    cp(ti, sl(NI, 0, 32))
+    ts(ti, ti, 31, band)
+    cp(LB32, ti)
+    parf, B8, B8b, PR = F(8), sl(PAY, 0, 128), sl(PAY, 128, 256), F(8)
+    p8 = (0, 8, 1)
+    cp(pp(sl(parf, 0, 6), p8), pp(sl(pari, 0, 6), p8))
+    ts(B8, R128, p16, ge)
+    ts(B8b, R128, p16b, lt)
+    tt(B8, B8, B8b, mul)
+    mm([(ps(7, 0, 6), pp(B8, p8), pp(sl(parf, 0, 6), p8), True, True)])
+    cp(sl(PR, 0, 6), ps(7, 0, 6))
+    lo, th, hi, Kc = [sl(PR, k, k + 1) for k in range(4)]
+    ts(col(12), lo, -0.5, add)
+    ts(col(13), th, -0.5, add)
+    ts(col(14), hi, -1.0, mul, 0.5, add)
+    for x in X:
+        ms(sl(x, 2944, 2960), 0.0)
+    rot = [0]
+    LI, LH = [I(384), I(384), I(896)], [H(384), H(384), H(896)]
+
+    def lin(xi, fields, bank):
+        n = wid(xi)
+        rot[0] += 1
+        out = ps(bank, 0, n)
+        a, b = LI[rot[0] % 2], LH[rot[0] % 2]
+        for k, (s, m, w) in enumerate(fields):
+            ts(sl(a, k * n, k * n + n), xi, s, shr, m, band)
+        cp(sl(b, 0, n * len(fields)), sl(a, 0, n * len(fields)))
+        mm([(out, WM[w], sl(b, k * n, k * n + n), k == 0, k == len(fields) - 1) for k, (s, m, w) in enumerate(fields)])
+        return out
+    POSA = [(2, 15, 512), (0, 3, 128), (6, 127, 1)]
+    POSB = [(9, 15, 512), (0, 15, 32), (4, 31, 1)]
+    POSW = [(0, 15, 512), (4, 511, 1)]
+
+    TA, BP, t1, t2 = F(512), F(512), F(512), F(512)
+    ts(t1, dew, -1.0, mul, 11776.0, add)
+    for j in range(4):
+        mm([(ps(3, 128 * j, 128 * j + 128), sl(ZQ, 144 * j + 12 - 4 * a, 144 * j + 140 - 4 * a), sl(t1, a, 512, 4), a == 0, a == 3) for a in range(4)])
+    ts(t2, ps(3, 0, 512), 11777.0, lt)
+    tt(TA, ps(3, 0, 512), t2, mul)
+    LW, TAB = [U(32), U(32)], [B(512), B(512)]
+    lsi, tbi = I(512), I(512)
+    for t in range(2):
+        Ct = sl(PR, 4 + t, 5 + t)
+        a, b, c = I(32), I(32), F(32)
+        ts(a, sl(NI, 0, 32), Kc, mul, Ct, add)
+        ts(b, a, 4, shr, 31, band)
+        ts(a, a, 15, band)
+        ts(c, a, 32.0, mul)
+        tt(c, c, b, add)
+        cp(LW[t], c)
+        ts(tbi, NI, Kc, mul, Ct, add)
+        ts(tbi, tbi, 9, shr, 15, band)
+        cp(HELD, tbi)
+        act(TAB[t], HELD, Fn.Exp, scale=-math.log(2.0))
+
+    CB = []
+    for k in range(2):
+        w = (WA, WB)[k]
+        CB.append({"CU": H(592), "Q": F(576) if k else sl(WA, 9696, 10240), "SW": sl(w, 8192, 9696), "CR": H(928), "cl": U(64), "li": U(48),
+                   "st": F(48), "em": F(48)})
+        ms(sl(CB[k]["CU"], 0, 1), 0.0)
+
+    def comp(k, NC, R, Pp, Tp, sb):
+        c = CB[k]
+        CU, Q, SW, CR, A = c["CU"], sl(c["Q"], 0, NC), c["SW"], sl(c["CR"], 0, R), NC // 16
+        dma([(sl(SW, 0, R), sl(ZR, 0, R))])
+        scan(sl(CU, 1, NC + 1), Tp, sl(CAPS, 0, NC), 0.0, add, mn)
+        mm(dg(ps(sb, 0, A), sl(CU, 0, NC), Z0) + dg(ps(sb, 64, 64 + A), sl(CU, 1, NC + 1), Z0))
+        st, em, li = sl(c["st"], 0, A), sl(c["em"], 0, A), sl(c["li"], 0, A)
+        cp(st, ps(sb, 0, A))
+        tt(em, ps(sb, 64, 64 + A), st, le)
+        tt(em, em, sl(DUC, 0, A), mul)
+        tt(em, em, st, mx)
+        cp(li, em)
+        tt(Q, Pp, sl(CU, 0, NC), add)
+        act(ind(sl(SW, 0, CAP + NC), li), sl(RI, 32, 32 + NC), Fn.Silu)
+        scan(CR, sl(SW, 0, R), sl(SW, 0, R), 32.0, mx, mx)
+        cl = sl(c["cl"], 0, R // 16)
+        mm(dg(ps(sb, 128, 128 + R // 16), CR, Z0))
+        ts(cl, ps(sb, 128, 128 + R // 16), -32.0, add)
+        return Q, CR, cl
+
+    OT, IT = F(56), F(56)
+    DB, DA = F(896), F(896)
+    for k, (tw, res) in enumerate(((axw, OT), (dew, IT))):
+        w = (WA, WB)[k]
+        Fl, VAL, OH, IW = sl(Dd, 4096 + 512 * k, 4608 + 512 * k), sl(w, 0, 512), sl(w, 512, 1408), sl(w, 2048, 2048 + 1808)
+        EV = H(896) if k == 0 else LH[2]
+        SID = (DA, DB)[k]
+        b0 = 4 * k
+        ts(Fl, tw, 8192.0, ge)
+        mm([(ps(b0 + 1, 0, 512), BO, Fl, True, True)])
+        mm([(ps(b0, 0, 512), TRH, Fl, True, False), (ps(b0, 0, 512), WM[-0.5], ONES, False, True)])
+        dma([(sl(IW, 0, 912), sl(ZR, 0, 912))])
+        if k == 0:
+            ki, k2 = sl(LI[2], 0, 512), sl(w, 1408, 1920)
+            ts(ki, tw, 2, shr, 127, band)
+            ts(k2, ki, 2.0, mul)
+            ts(VAL, tw, -0.25, mul, 2817.0, add)
+            tt(VAL, VAL, k2, add)
+        else:
+            ts(VAL, tw, 0.25, mul, -2047.0, add)
+        Q, CR, cl = comp(k, 512, 896, ps(b0, 0, 512), ps(b0 + 1, 0, 512), b0 + 2)
+        if k == 0:
+            mm(full(ps(b0, 0, 896), WM[16], CR))
+            act(SID, ps(b0, 0, 896), bias=sidb)
+        tt(OH, ind(Q, cl), sl(RI, 1, 897), eq)
+        tt(EV, ind(VAL, cl), OH, mul)
+        o = ps(b0 + 3, 0, 56)
+        mm(dg(o, EV, Z))
+        z, li = F(56), U(56)
+        ts(z, o, 0.0, eq)
+        tt(z, z, d9, mul)
+        tt(z, o, z, add)
+        cp(li, z)
+        if k == 0:
+            tt(ind(IW, li), OH, SID, mul)
+        else:
+            n33 = sl(w, 1408, 1920)
+            ts(n33, NI, 33.0, add)
+            tt(SID, ind(n33, cl), OH, mul)
+            act(ind(IW, li), SID, Fn.Silu)
+        o = ps(b0 + 2, 256, 312)
+        mm(dg(o, sl(IW, 1, 897), Zf))
+        if k == 0:
+            ui, LO = I(56), U(56)
+            ts(ui, o, -1.0, add, 0.0, mx)
+            ts(ui, ui, 2, shr)
+            cp(LO, ui)
+        act(res, o, Fn.Relu, bias=-32.0 * k)
+
+    ts(BP, axB, 1.0, add)
+    dma([(pp(sl(WA, 0, 8192), R8), TA)])
+    dma([(pp(sl(WB, 0, 8192), R8), BP)])
+
+    SB, LS = B(896), U(512)
+    ACCf, ACCi, Ab = DA, LI[2], B(2048)
+
+    def send_x(k):
+        x = X[k % 2]
+        cp(sl(SB, 0, 448), ind(sl(x, 0, 2048), sl(LO, 0, 28)))
+        cp(sl(SB, 448, 896), ind(sl(x, 0, 2048), sl(LO, 28, 56)))
+        exch(SB, sl(x, 2048, 2944), 128)
+        n = (ND1, ND2, 2048)[k % 3]
+        if k != 3:
+            dma([(sl(Qb, 0, n), sl(x, 0, n))])
+
+    def lst(j, a, b): return sl(LS, 128 * j + a // 16, 128 * j + b // 16)
+
+    def step(k, mod):
+        x, y = X[k % 2], X[(k + 1) % 2]
+        nd = ND2 if mod else ND1
+        for bank, a in enumerate(range(nd, 2048, 512)):
+            b = min(a + 512, 2048)
+            o = ps(bank, 0, b - a)
+            last = mm([(o, ID, sl(x, a, b), True, False)] + ([(o, O24, sl(ONES, 0, b - a), False, False)] if mod else []))
+            for j in range(4):
+                v = sl(Dd, 2048 * j + a, 2048 * j + b)
+                act(v, ind(x, lst(j, a, b)))
+                last = mm([(o, ID, v, False, j == 3)], after=last)
+            if mod:
+                ts(sl(Qb, a, b), o, -7.5, add)
+                tt(sl(y, a, b), o, sl(Qb, a, b), sub)
+            else:
+                cp(sl(y, a, b), o)
+        h = nd // 2
+        for j in range(4):
+            for a in (0, h):
+                acc = sl(ACCf, a, a + h) if mod else sl(Qb, a, a + h)
+                out = acc if j < 3 else (sl(ACCi, a, a + h) if mod else sl(y, a, a + h))
+                tt(out, ind(x, lst(j, a, a + h)), acc if j else sl(Qb, a, a + h), add)
+        if mod:
+            for a in (0, h):
+                ts(sl(ACCi, a, a + h), sl(ACCi, a, a + h), 15, band)
+                cp(sl(y, a, a + h), sl(ACCi, a, a + h))
+
+    CP3 = [(0, 0, 0), (1, 0, 0), (0, 0, 1), (1, 0, 1), (0, 1, 0), (1, 1, 0), (0, 1, 1), (1, 1, 1)][:NC3]
+    KEY = PAY
+    KW, MK, FLk, LK, LM = B(1024), B(1792), sl(Dd, 2048, 3840), U(112), U(112)
+    NK, FT, G1, CT, CG, cmpf = sl(Ab, 0, 512), sl(Ab, 512, 1024), sl(Ab, 1024, 1536), sl(Qb, 0, 768), sl(Qb, 768, 1696), sl(Ab, 1536, 1792)
+    FG, Y1, Y1i, Wc = B(576), t1, axw, F(32)
+    ms(sl(FG, 568, 576), 0.0)
+    SBLs, LBLs = [B(112), B(112)], [B(112), B(112)]
+    WR1, WR2 = HELD, t2
+    mark, high = dict(TOP), dict(TOP)
+
+    for t in range(2):
+        fin = t == 1
+        for a in TOP:
+            high[a] = TOP[a]
+            TOP[a] = mark[a]
+        Ct = sl(PR, 4 + t, 5 + t)
+        k0 = 3 * t
+        ts(lsi, TA, -0.25, mul, 2943.625, add)
+        cp(LS, lsi)
+        if t == 0:
+            send_x(0)
+            step(0, False)
+        send_x(k0 + 1)
+        ts(PAY, TA, -1.0 / 16384, mul, 0.71875, add)
+        act(HELD, TA, Fn.Sign)
+        ms(sl(KW, 512, 1024), 0.0)
+        bt, l1, l2, PABd = I(128), F(128), F(128), F(128)
+        for q in range(4):
+            c = 32 * (4 * q + t)
+            ts(sl(bt, 32 * q, 32 * q + 32), sl(BP, c, c + 32), -1.0, add)
+        o = lin(bt, POSA, 6)
+        tt(PABd, o, DUM, sub)
+        ts(l1, bt, 0.0, ge)
+        ts(l2, bt, 8192.0, lt)
+        tt(l1, l1, l2, mul)
+        tt(PABd, PABd, l1, mul)
+        hd, pd, p1 = [F(56), F(56)], [F(56), F(56)], F(56)
+        for s, (tb, fl) in enumerate(((IT, POSA), (OT, POSB))):
+            a, b, c = I(56), I(56), F(56)
+            ts(a, tb, -1.0, add, 0.0, mx)
+            o = lin(a, fl, 5 + s)
+            cp(a, o)
+            tt(pd[s], o, DUL, sub)
+            act(hd[s], tb, Fn.Sign)
+            ts(b, a, 511, band)
+            ts(sl(LK, 56 * s, 56 * s + 56), b, 512.0 * s, add)
+            ts(a, a, 9, shr)
+            ts(c, hd[s], -16.0, mul, 16.0, add)
+            tt(c, c, a, add)
+            cp(sl(LM, 56 * s, 56 * s + 56), c)
+            cp(sl(MK, 896 * s, 896 * s + 896), ind(I16, sl(LM, 56 * s, 56 * s + 56)))
+        tt(pd[0], pd[0], hd[0], mul)
+        tt(p1, pd[0], DUL, add)
+        nh = F(56)
+        ts(nh, hd[0], -1.0, mul, 1.0, add)
+        step(k0 + 1, True)
+        send_x(k0 + 2)
+        x, y = X[k0 % 2], X[(k0 + 1) % 2]
+        far = ps(4, 0, 512)
+        lf = mm([(far, ID, CJ, True, False), (far, IDf, PAY, False, False)])
+        SL, SBp = ps(5, 0, 128), ps(6, 0, 128)
+        lsb = None
+        for hf in range(2):
+            lx = [mm([(ps(2 * hf + i, 0, 512), WM[5 - sum((hf, j, i) in CP3 for j in range(4))], sl(x, 1024 * hf + 512 * i, 1024 * hf + 512 * i + 512), True, False),
+                      (ps(2 * hf + i, 0, 512), O24, ONES, False, False)]) for i in range(2)]
+            for j in range(4):
+                ab = sl(Ab, 1024 * (j % 2), 1024 * (j % 2) + 1024)
+                for i in range(2):
+                    a = 1024 * hf + 512 * i
+                    d = sl(Dd, 2048 * j + a, 2048 * j + a + 512)
+                    if (hf, j, i) in CP3:
+                        act(d, ind(x, lst(j, a, a + 512)))
+                        mm([(ps(7, 0, 512), ID, d, True, False), (ps(7, 0, 512), WM[-1], sl(x, a, a + 512), False, True)])
+                        act(sl(ab, 512 * i, 512 * i + 512), ps(7, 0, 512), Fn.Abs)
+                    else:
+                        tt(d, ind(x, lst(j, a, a + 512)), sl(Qb, a, a + 512), sub)
+                        act(sl(ab, 512 * i, 512 * i + 512), d, Fn.Abs)
+                    lx[i] = mm([(ps(2 * hf + i, 0, 512), ID, d, False, j == 3)], after=lx[i])
+                c = 128 * j + 64 * hf
+                lf = mm(dg(ps(4, c, c + 64), ab, Z4, False, hf == 1 and j == 3), after=lf)
+            for i in range(2):
+                a = 1024 * hf + 512 * i
+                ts(sl(Qb, a, a + 512), ps(2 * hf + i, 0, 512), -7.5, add)
+                tt(sl(y, a, a + 512), ps(2 * hf + i, 0, 512), sl(Qb, a, a + 512), sub)
+            lsb = mm([(SBp, sl(Z, 15 - ii, 143 - ii), sl(y, 128 * ii, 128 * ii + 128), ii == 0, ii == 15) for ii in range(8 * hf, 8 * hf + 8)], after=lsb)
+            mm(dg(ps(5, 64 * hf, 64 * hf + 64), sl(y, 1024 * hf, 1024 * hf + 1024), Z))
+        if fin:
+            dma([(dr("yx", 0, 2048), sl(y, 0, 2048))])
+        else:
+            send_x(3)
+        kac, nka, la, lau = F(128), F(128), F(128), U(128)
+        for q in range(4):
+            act(sl(nka, 32 * q, 32 * q + 32), ps(6, q, 128, 4), Fn.Sign, bias=col(12), scale=-1.0)
+        act(kac, nka, Fn.Relu)
+        tt(la, kac, PABd, mul)
+        tt(la, la, DUM, add)
+        cp(lau, la)
+        for a in range(0, 128, 32):
+            cp(ind(WA, sl(lau, a, a + 32)), sl(ZR, 0, 512), True)
+        fh, thf, m1, m2, ri, zi, lb, lbu = F(128), F(128), F(256), F(128), I(128), I(128), F(128), U(128)
+        act(fh, SL, Fn.Sign, bias=col(14))
+        act(thf, SL, Fn.Sign, bias=col(13), scale=-1.0)
+        act(fh, fh, Fn.Relu)
+        act(thf, thf, Fn.Relu)
+        tt(KEY, far, HELD, mul)
+        tt(m1, sl(KEY, 0, 256), sl(KEY, 256, 512), mx)
+        tt(m2, sl(m1, 0, 128), sl(m1, 128, 256), mx)
+        tt(m2, m2, fh, mul)
+        for j in range(4):
+            tt(sl(KW, 128 * j, 128 * j + 128), sl(KEY, 128 * j, 128 * j + 128), m2, eq)
+        for q in range(4):
+            c = 512 + 32 * (4 * q + t)
+            cp(sl(KW, c, c + 32), sl(kac, 32 * q, 32 * q + 32))
+        SBL, LBL = SBLs[t], LBLs[t]
+        for s in range(2):
+            tt(sl(FLk, 896 * s, 896 * s + 896), ind(KW, sl(LK, 56 * s, 56 * s + 56)), sl(MK, 896 * s, 896 * s + 896), mul)
+            mm(dg(ps(2 + s, 0, 56), sl(FLk, 896 * s, 896 * s + 896), Z))
+        go, alive = sl(SBL, 0, 112, 2), sl(SBL, 1, 112, 2)
+        cp(go, ps(2, 0, 56))
+        tt(alive, hd[1], ps(3, 0, 56), sub)
+        exch(SBL, LBL, 16)
+        ts(ri, m2, 0.5, mx, 16384.0, mul)
+        o = lin(ri, POSB, 7)
+        ts(zi, ri, 13, shr, 1, band)
+        tt(lb, DUM, zi, mul)
+        tt(lb, o, lb, mx)
+        cp(lbu, lb)
+        for a in range(0, 128, 32):
+            cp(ind(WB, sl(lbu, a, a + 32)), sl(ZR, 0, 512), True)
+        gO, aI = sl(LBL, 0, 112, 2), sl(LBL, 1, 112, 2)
+        a, b, au, bu = F(56), F(56), U(56), U(56)
+        tt(a, aI, pd[0], mul)
+        tt(a, p1, a, sub)
+        cp(au, a)
+        cp(ind(WA, au), sl(ZR, 0, 896), True)
+        tt(b, gO, pd[1], mul)
+        tt(b, b, DUL, add)
+        cp(bu, b)
+        cp(ind(WB, bu), sl(ZR, 0, 896), True)
+        dma([(TA, pp(sl(WA, 0, 8192), R8))])
+        dma([(BP, pp(sl(WB, 0, 8192), R8))])
+        ts(NK, sl(KW, 0, 512), -1.0, mul, 1.0, add)
+        ts(nka, kac, -1.0, mul, 1.0, add)
+        tt(TA, TA, NK, mul)
+        for q in range(4):
+            c = 32 * (4 * q + t)
+            tt(sl(BP, c, c + 32), sl(BP, c, c + 32), sl(nka, 32 * q, 32 * q + 32), mul)
+        if not fin:
+            ts(lsi, TA, -0.25, mul, 2943.625, add)
+            cp(LS, lsi)
+            for j in range(4):
+                for a in range(0, 2048, 512):
+                    cp(sl(Dd, 2048 * j + a, 2048 * j + a + 512), ind(X[1], lst(j, a, a + 512)))
+        z0 = 8 * (6 - t)
+        ng, fre, cs8, Qf, qb = F(56), B(8), F(16), F(8), F(8)
+        ts(ng, gO, -1.0, mul, 1.0, add)
+        tt(ng, ng, alive, mul)
+        ts(fre, sl(ng, z0, z0 + 8), -1.0, mul, 1.0, add)
+        mm([(ps(2, 64, 72), TRI, fre, True, True), (ps(2, 80, 88), BO, fre, True, True)])
+        ms(sl(cs8, 0, 1), 0.0)
+        scan(sl(cs8, 1, 9), ps(2, 80, 88), sl(CAPS, 0, 8), 0.0, add, mn)
+        tt(Qf, ps(2, 64, 72), sl(cs8, 0, 8), add)
+        ts(qb, Qf, -1.0, mul, 0.5, add)
+        for c in range(8):
+            act(sl(cmpf, 32 * c, 32 * c + 32), sl(RI, 0, 32), Fn.Sign, bias=sl(qb, c, c + 1))
+        mm([(ps(3, 64, 96), BO, sl(cmpf, 32 * c, 32 * c + 32), c == 0, c == 7) for c in range(8)])
+        one = 0.0 if fin else 1.0
+        ts(sl(DB, 768, 800), ps(3, 64, 96), 2.0, mul, 8448.0 + 512 * t + one, add)
+        tt(sl(FG, 0, 56), aI, nh, mul)
+        ts(G1, ind(BP, LW[t]), 0.5, lt)
+        mm(dg(ps(6, 0, 32), G1, ZP))
+        ts(Wc, ps(6, 0, 32), 0.5, add)
+        tt(Y1, ind(Wc, LB32), TAB[t], mul)
+        ts(Y1i, Y1, -0.5, add)
+        ts(Y1i, Y1i, 1, band)
+        cp(sl(FG, 56, 568), Y1i)
+        for j in range(4):
+            tt(sl(FT, 128 * j, 128 * j + 128), sl(TA, 128 * j, 128 * j + 128), thf, lt)
+        mm([(ps(1, a, 512, 4), sl(TO, 128 * a, 128 * a + 128), sl(FT, 128 * j, 128 * j + 128), j == 0, j == 3) for a in range(4) for j in range(4)])
+        mm([(ps(0, a, 512, 4), sl(TM, 128 * (4 * a + j), 128 * (4 * a + j) + 128), sl(FT, 128 * j, 128 * j + 128), j == 0, j == 3)
+            for a in range(4) for j in range(4)])
+        if not fin:
+            dma([(pp(sl(WA, 0, 8192), R8), TA)])
+            dma([(pp(sl(WB, 0, 8192), R8), BP)])
+        QT, CRT, clT = comp(0, 512, 768, ps(0, 0, 512), ps(1, 0, 512), 6)
+        mm(full(ps(4, 0, 576), BO, FG))
+        mm(full(ps(2, 0, 576), TRI, FG))
+        QG, CRG, clG = comp(1, 576, 928, ps(2, 0, 576), ps(4, 0, 576), 7)
+        if fin:
+            act(HELD, TA, Fn.Sign)
+            ts(HELD, HELD, 11777.0, mul, -1.0, add)
+            tt(RAW, HELD, TA, sub)
+            for a in range(4):
+                mm([(ps(4, a, 512, 4), sl(ZB, 144 * a + 3 - j, 144 * a + 131 - j), sl(RAW, 128 * j, 128 * j + 128), j == 0, j == 3) for j in range(4)])
+            cp(WR1, ps(4, 0, 512))
+            ts(PAY, BP, -1.0, add)
+            dma([(pp(WR2, (i, 128, 16)), sl(PAY, 32 * i, 32 * i + 32)) for i in range(16)], lat=5000.0)
+            dma([(pp(sl(WA, 0, 8192), R8), WR1)])
+            dma([(pp(sl(WB, 0, 8192), R8), WR2)])
+        tt(CT, ind(QT, clT), sl(RI, 0, 768), le)
+        mm(dg(ps(6, 256, 304), CRT, Z, True, False) + dg(ps(6, 256, 304), CT, Z, False, True))
+        mm([x_ for a, b in ((0, 512), (512, 768)) for x_ in
+            ((ps(0, a, b), BO, sl(CRT, a, b), True, False), (ps(0, a, b), BO, sl(CT, a, b), False, True))])
+        ts(sl(DB, 0, 768), ps(0, 0, 768), -512.0 + one, add)
+        si = I(48)
+        ts(si, ps(6, 256, 304), -512.0, add)
+        o = lin(si, POSW if fin else POSA, 6)
+        cn = F(8)
+        nT, nG, nl, mc, r0 = [sl(cn, k, k + 1) for k in range(5)]
+        ts(nT, sl(CB[0]["CU"], 512, 513), 768.0, mn)
+        cp(nG, sl(CB[1]["CU"], 576, 577))
+        cp(nl, sl(CB[1]["CU"], 56, 57))
+        tt(mc, nT, nG, mn)
+        tt(r0, mc, nl, mx)
+        vA, pa, pau, D48 = F(48), F(48), U(48), sl(DUM, 0, 48)
+        tt(pa, o, D48, sub)
+        ts(vA, sl(NI, 0, 48), mc, lt)
+        tt(pa, pa, vA, mul)
+        tt(pa, pa, D48, add)
+        cp(pau, pa)
+        tt(CG, ind(QG, clG), sl(RI, 0, 928), le)
+        o = ps(7, 256, 314)
+        mm(dg(o, CRG, Z, True, False) + dg(o, CG, Z, False, True))
+        j1, ui, uf, isl, lv = F(58), I(58), F(64), F(48), F(48)
+        o48 = ps(7, 256, 304)
+        ts(j1, o, -1408.0, add, Kc, mul)
+        ts(isl, o48, 1408.0, lt)
+        ts(lv, o48, 4.0, mul, 6144.0, add)
+        ts(ui, j1, Ct, add)
+        ts(ui, ui, 8191, band)
+        u48 = sl(ui, 0, 48)
+        gv, gh, gl = F(48), H(48), H(48)
+        tt(lv, lv, isl, mul)
+        tt(gv, lv, u48, mx)
+        if not fin:
+            gi, gu, pv, pvu, XG = I(48), U(48), F(48), U(48), sl(MK, 0, 768)
+            cp(gi, gv)
+            ts(gi, gi, 2, shr)
+            cp(gu, gi)
+            cp(XG, ind(X[1], gu))
+            o = lin(si, [(0, 3, 2048), (2, 2047, 1)], 6)
+            tt(pv, o, D48, sub)
+            tt(pv, pv, vA, mul)
+            tt(pv, pv, D48, add)
+            cp(pvu, pv)
+            cp(ind(Dd, pvu), XG)
+            for q, bank in enumerate((0, 1, 4, 5)):
+                a = 512 * q
+                mm([(ps(bank, 0, 512), ID, sl(X[1], a, a + 512), True, False)]
+                   + [(ps(bank, 0, 512), ID, sl(Dd, 2048 * j + a, 2048 * j + a + 512), False, j == 3) for j in range(4)])
+                cp(sl(X[0], a, a + 512), ps(bank, 0, 512))
+            gv0, gv = gv, F(48)
+            ts(gv, gv0, -1.0, mul, 11776.0, add)
+        cp(gh, gv)
+        tt(gl, gv, gh, sub)
+        for bk, (a, b) in enumerate(((0, 32), (32, 48))):
+            mm([(ps(2 + bk, i, 16 * (b - a), 16), sl(EI, 128 * i, 128 * i + 128), sl(s_, a, b), s_ is gh, s_ is gl) for i in range(16) for s_ in (gh, gl)])
+            cp(sl(DA, 16 * a, 16 * b), ps(2 + bk, 0, 16 * (b - a)))
+            cp(ind(WA, sl(pau, a, b)), sl(DA, 16 * a, 16 * b))
+        if fin:
+            dma([(dr("yd", 0, 512), pp(sl(WA, 0, 8192), R8))])
+        else:
+            dma([(TA, pp(sl(WA, 0, 8192), R8))])
+        PB_ = POSW if fin else POSB
+        pb, pbu, vb = F(50), U(50), F(50)
+        o = lin(u48, PB_, 7)
+        tt(sl(pb, 0, 48), o, D48, sub)
+        ts(sl(vb, 0, 48), isl, -1.0, mul, 1.0, add)
+        tt(sl(vb, 0, 48), sl(vb, 0, 48), vA, mul)
+        cp(sl(uf, 0, 58), ui)
+        rr, ra, rc, rp, mk, rw, RR, uc, uci, v2 = F(2), I(2), U(2), U(2), F(32), F(32), F(32), F(2), I(2), F(2)
+        ts(rr, sl(NI, 0, 2), r0, add)
+        cp(ra, rr)
+        ts(uci, ra, 4, shr)
+        cp(rc, uci)
+        ts(ra, ra, 15, band)
+        cp(rp, ra)
+        cp(mk, ind(I16, rp))
+        tt(rw, ind(sl(uf, 0, 58), rc), mk, mul)
+        mm([(ps(6, 64, 96), BOf, rw, True, True)])
+        cp(RR, ps(6, 64, 96))
+        tt(rw, RR, MK32, mul)
+        red(sl(uc, 0, 1), sl(rw, 0, 16))
+        red(sl(uc, 1, 2), sl(rw, 16, 32))
+        cp(uci, uc)
+        o = lin(uci, PB_, 6)
+        tt(sl(pb, 48, 50), o, sl(DUM, 48, 50), sub)
+        ts(v2, rr, nG, lt)
+        ts(sl(vb, 48, 50), sl(NI, 0, 2), sl(cs8, 8, 9), lt)
+        tt(sl(vb, 48, 50), sl(vb, 48, 50), v2, mul)
+        for a, b in ((0, 48), (48, 50)):
+            tt(sl(pb, a, b), sl(pb, a, b), sl(vb, a, b), mul)
+            tt(sl(pb, a, b), sl(pb, a, b), sl(DUM, a, b), add)
+            cp(sl(pbu, a, b), sl(pb, a, b))
+        for a, b in ((0, 24), (24, 48), (48, 50)):
+            cp(ind(WB, sl(pbu, a, b)), sl(DB, 16 * a, 16 * b))
+        if fin:
+            dma([(dr("ya", 0, 512), pp(sl(WB, 0, 8192), R8))])
+            for a in TOP:
+                TOP[a] = max(TOP[a], high[a])
+            continue
+        dma([(BP, pp(sl(WB, 0, 8192), R8))])
+        v, w, wu, row = F(56), F(56), U(56), sl(WA, 8192, 9088)
+        ts(v, sl(QG, 0, 56), mc, le)
+        tt(v, v, sl(FG, 0, 56), mul)
+        ts(w, sl(QG, 0, 56), -1.0, add)
+        tt(w, w, v, mul)
+        cp(wu, w)
+        cp(row, ind(sl(DB, 0, 768), wu))
+        mm(dg(ps(7, 64, 120), row, Z0f))
+        tt(w, ps(7, 64, 120), v, mul)
+        tt(IT, IT, aI, mul)
+        ts(v, go, -1.0, mul, 1.0, add)
+        tt(IT, IT, v, mul)
+        tt(IT, IT, w, add)
+        nn, v8, w8, w8u, r8 = F(1), F(8), F(8), U(8), F(128)
+        tt(nn, nG, r0, sub)
+        ts(nn, nn, 32.0, mn)
+        ts(v8, Qf, nn, le)
+        tt(v8, v8, fre, mul)
+        ts(w8, Qf, -1.0, add)
+        tt(w8, w8, v8, mul)
+        cp(w8u, w8)
+        cp(r8, ind(RR, w8u))
+        mm(dg(ps(6, 128, 136), r8, Z0f))
+        ts(w8, ps(6, 128, 136), 1.0, add)
+        tt(w8, w8, v8, mul)
+        tt(OT, OT, ng, mul)
+        tt(sl(OT, z0, z0 + 8), sl(OT, z0, z0 + 8), w8, add)
+
+
+def schedule(noise):
+    n = len(OPS)
+    suc = [[] for _ in range(n)]
+    for k, o in enumerate(OPS):
+        if "alt" in o:
+            o["cost"] = o["alt"]["a"][1]
+        for p in o["pre"]:
+            suc[p].append(k)
+    pr = [0.0] * n
+    for k in range(n - 1, -1, -1):
+        pr[k] = OPS[k]["cost"] + OPS[k]["lat"] + HOP + max([pr[s] for s in suc[k]] + [0.0])
+    pr = [a + b for a, b in zip(pr, noise)]
+    left = [len(o["pre"]) for o in OPS]
+    ready = [0.0] * n
+    free = {}
+    cand = [k for k in range(n) if left[k] == 0]
+    order = []
+    end = 0.0
+    while cand:
+        for k in cand:
+            o = OPS[k]
+            if "alt" in o:
+                e = {q: max(ready[k], free.get(q, 0.0)) + o["alt"][q][1] for q in "av"}
+                o["q"] = "a" if e["a"] <= e["v"] + BIAS else "v"
+                o["fn"], o["cost"] = o["alt"][o["q"]]
+        st = {k: max(ready[k], free.get(OPS[k]["q"], 0.0)) for k in cand}
+        k = min(cand, key=lambda x: (st[x], -pr[x]))
+        q = OPS[k]["q"]
+        while True:
+            bet = [x for x in cand if OPS[x]["q"] == q and pr[x] > pr[k] + LOOK and st[x] < st[k] + LOOKF * OPS[k]["cost"]]
+            if not bet:
+                break
+            k = min(bet, key=lambda x: (st[x], -pr[x]))
+        cand.remove(k)
+        o = OPS[k]
+        free[q] = st[k] + o["cost"]
+        fin = st[k] + o["cost"] + o["lat"] + HOP
+        o["t"] = st[k]
+        end = max(end, fin)
+        order.append(k)
+        for s in suc[k]:
+            ready[s] = max(ready[s], fin)
+            left[s] -= 1
+            if left[s] == 0:
+                cand.append(s)
+    sems, cnt = ["cv", "ca", "cp", "cg"], {}
+    for k in order:
+        o = OPS[k]
+        if o["kind"] == "c":
+            cnt[o["q"]] = cnt.get(o["q"], 0) + 1
+            o["sig"] = ("c" + o["q"], cnt[o["q"]])
+        else:
+            sems.append("%s%d" % (o["kind"][0], k))
+            o["sig"] = (sems[-1], 16 * o["n"] if o["kind"] == "dma" else 2 * (N - 1))
+    snd = [o["t"] for o in OPS if o["kind"] == "send"]
+    return order, sems, end + 0.25 * (sum(snd) - snd[3]), end
+
+
+def search(rounds):
+    n, x = len(OPS), 1
+    best = [0.0] * n
+    plan = schedule(best)[2]
+    for it in range(rounds):
+        new = list(best)
+        for m in range(3):
+            x = (x * 1103515245 + 12345) % 2147483648
+            a = (x >> 8) % n
+            x = (x * 1103515245 + 12345) % 2147483648
+            d = ((x >> 8) % 10000) - 5000.0
+            for k in range(a, min(n, a + 1 + (x >> 4) % 12)):
+                new[k] += d
+        p = schedule(new)[2]
+        if p <= plan:
+            best, plan = new, p
+    return schedule(best)
+
+
+build()
+ORDER, SEMAPHORES, _SCORE, PLAN = search(ROUNDS)
+SCRATCH = {k: ("sbuf", [128, TOP[k]], DTY[k]) for k in DTY}
+for _k in range(4):
+    SCRATCH["p%d" % _k] = ("psum", [128, 1024], "float32")
+
+
+def rank_program(g, core, T, topo):
+    rank = T.rank_of(core)
+    if rank is None:
+        return
+    Q = {"v": g.vector, "a": g.scalar, "p": g.tensor, "g": g, "s": g.sync}
+    seen = {q: {} for q in Q}
+    top = {}
+
+    def wait(q, sig):
+        if seen[q].get(sig[0], 0) < sig[1]:
+            Q[q].wait_ge(T.sem[sig[0]], sig[1])
+            seen[q][sig[0]] = sig[1]
+
+    for k in ORDER:
+        o = OPS[k]
+        q, sig = o["q"], o["sig"]
+        top[sig[0]] = sig[1]
+        if o["kind"] == "recv":
+            continue
+        need = {}
+        for p in o["pre"]:
+            s = OPS[p]["sig"]
+            need[s[0]] = max(need.get(s[0], 0), s[1])
+        for s in need.items():
+            wait(q, s)
+        if o["kind"] == "c":
+            o["fn"](g, T).then_inc(T.sem[sig[0]], 1)
+        elif o["kind"] == "dma":
+            for x in o["fn"](g, T):
+                x.then_inc(T.sem[sig[0]], 16)
+        else:
+            src, dst, w = o["fn"]
+            far, near, trs = 0, 0, []
+            for p in range(N - 1):
+                c = T.cores[(rank - p - 1) % N]
+                en = topo.engines(core, c)
+                if topo.die(c) != topo.die(core):
+                    pick = en[0::2][2 * far:2 * far + 2]
+                    far += 1
+                else:
+                    pick = en[1::2][2 * near:2 * near + 2]
+                    near += 1
+                a = topo.addr(c)
+                trs.append(RemoteDMATransfer(dst_ids=[DstId(rid=a[0], pnc=a[1])], dma_engine_mask=sum(1 << e for e in pick),
+                                             remote_sem=T.sem[OPS[k + 1]["sig"][0]],
+                                             src=ap(T, sl(src, w * p, w * p + w)), dst=ap(T, sl(dst, w * (6 - p), w * (6 - p) + w))))
+            g.remote_dma_fused(trs, local_sem=T.sem[sig[0]])
+    for s in top.items():
+        wait("g", s)

@@ -6,11 +6,10 @@ N = 8
 DTY = {"af": "float32", "ab": "bfloat16", "ai": "int32", "au": "uint16", "ah": "float16"}
 SZ = {"float32": 4, "bfloat16": 2, "int32": 4, "uint16": 2, "float16": 2}
 TOP = {k: 0 for k in DTY}
-OPS = []
-ACC = {}
+OPS, ACC, EXPS, BANK, ALT, LAT = [], {}, [], {}, [], []
 GC, SC, PEC, HOP = 1.5, 3.5, 0.5, 90.0
-BIAS, LOOK, LOOKF, ROUNDS = 300.0, 300.0, 0.6, 1500
-ND1, ND2, NC3 = 1024, 896, 4
+BIAS, SEED, ROUNDS = 300.0, 1, 3000
+ND, NPE, NC3 = [1024, 0, 0, 0, 0, 0], [0, 0, 0, 0, 0, 0], 3
 
 
 def al(k, n):
@@ -74,7 +73,7 @@ def op(q, fn, reads, writes, cost, lat=0.0, kind="c", n=1, after=None):
     if kind == "recv":
         pre = set()
     if after is not None:
-        pre.add(after)
+        pre.update(after if isinstance(after, list) else [after])
     for lst, w in ((rd, False), (wr, True)):
         for r in lst:
             old = ACC.get(r[0], [])
@@ -102,7 +101,10 @@ def act(out, a, f=None, bias=None, scale=None, q="a"):
         if scale is not None:
             kw["scale"] = ap(T, scale)
         return g.scalar.activation(ap(T, out), ap(T, a), Fn.Identity if f is None else f, **kw)
-    return op(q, fn, [a, bias, scale], [out], vcost(out, [a], 1.0))
+    k = op(q, fn, [a, bias, scale], [out], vcost(out, [a], 1.0), after=list(EXPS) if f == Fn.Silu else None)
+    if f == Fn.Exp:
+        EXPS.append(k)
+    return k
 
 
 def either(fv, cv, out, a, bias, scale, f=None):
@@ -124,6 +126,10 @@ def ts(out, a, s1, o0, s2=None, o1=None):
             return either(fn, c, out, a, s1, None)
         if s2 is not None and o0 == Op.mult and o1 == Op.add:
             return either(fn, c, out, a, s2, s1)
+        if s2 == 0.0 and o0 == Op.add and o1 == Op.max:
+            return either(fn, c, out, a, s1, None, Fn.Relu)
+        if s1 == 0.0 and o0 == Op.is_equal and o1 == Op.mult and not isref(s2):
+            return either(fn, c, out, a, s2, -s2, Fn.Relu)
     return op("v", fn, [a, s1, s2], [out], c)
 
 
@@ -132,10 +138,10 @@ def tt(out, a, b, o):
               vcost(out, [a], 1.0 if ispsum(a) or ispsum(b) else 2.0))
 
 
-def cp(out, a, zero=False):
+def cp(out, a, silu=False):
     fn = lambda g, T: g.vector.tensor_copy(ap(T, out), ap(T, a))
     c = vcost(out, [a], half(out, a))
-    if zero:
+    if silu:
         return either(fn, c, out, a, None, None, Fn.Silu)
     if flt(out, a) and out[0] != "ind":
         return either(fn, c, out, a, None, None)
@@ -147,11 +153,8 @@ def ms(out, c):
 
 
 def scan(out, d0, d1, init, o0, o1):
-    return op("v", lambda g, T: g.vector.tensor_tensor_scan(ap(T, out), ap(T, d0), ap(T, d1), init, o0, o1), [d0, d1], [out], max(64, wid(out)))
-
-
-def red(out, a):
-    return op("v", lambda g, T: g.vector.tensor_reduce(ap(T, out), ap(T, a), AxisListType.X, Op.add), [a], [out], 64)
+    return op("v", lambda g, T: g.vector.tensor_tensor_scan(ap(T, out), ap(T, d0), ap(T, d1), init, o0, o1), [d0, d1], [out],
+              max(64, wid(out) * half(out, d0, d1)))
 
 
 def iota(out, pat, base, cm):
@@ -162,13 +165,32 @@ def iota(out, pat, base, cm):
     return op("g", fn, [], [out], 130 + 2 * wid(out))
 
 
+def asel(out, a, pat, cmp, base, cm):
+    return op("g", lambda g, T: g.affine_select(ap(T, out), ap(T, a), pat, cmp, 0.0, base, cm), [a], [out], 170 + 2 * wid(out))
+
+
 def mm(lst, after=None):
     def fn(g, T):
         for (o, l, r, st, sp) in lst:
-            x = g.tensor.matmul(ap(T, o), ap(T, l), ap(T, r), st, sp)
+            x = g.tensor.matmul(ap(T, o), ap(T, l), ap(T, r), st, sp == 1)
         return x
     c = sum(max(64, wid(x[2])) * (4 if size(x[2]) == 4 else 1) for x in lst) * PEC
-    return op("p", fn, [x[1] for x in lst] + [x[2] for x in lst] + [x[0] for x in lst if not x[3]], [x[0] for x in lst], c, lat=60, after=after)
+    pre = [] if after is None else [after]
+    k = len(OPS)
+    for x in lst:
+        b = BANK.setdefault((x[0][0], x[0][1] // 512), {"open": None, "close": None, "starts": []})
+        if x[3]:
+            assert b["open"] is None
+            pre += [b["close"]] if b["close"] is not None else []
+            b["open"] = k
+            b["starts"].append(k)
+        if x[4] == 1:
+            if b["open"] != k:
+                b["close"] = k
+                OPS[b["open"]]["pre"].update(s for s in b["starts"] if s < b["open"])
+            b["open"] = None
+    return op("p", fn, [x[1] for x in lst] + [x[2] for x in lst] + [x[0] for x in lst if not x[3]], [x[0] for x in lst], c, lat=60,
+              after=[p for p in pre if p != k])
 
 
 def dg(out, src, z, st=True, sp=True):
@@ -176,9 +198,9 @@ def dg(out, src, z, st=True, sp=True):
     return [(out, sl(z, 15 - b, 143 - b), sl(src, b, n, 16), st and b == 0, sp and b == 15) for b in range(16)]
 
 
-def full(out, l, src):
+def full(out, l, src, st=True, sp=True):
     n = wid(src)
-    return [(sl(out, a, min(a + 512, n)), l, sl(src, a, min(a + 512, n)), True, True) for a in range(0, n, 512)]
+    return [(sl(out, a, min(a + 512, n)), l, sl(src, a, min(a + 512, n)), st, sp) for a in range(0, n, 512)]
 
 
 def dma(pairs, lat=2500.0, q="s"):
@@ -195,29 +217,34 @@ def exch(src, dst, w):
 
 def build():
     add, sub, mul, mx, mn = Op.add, Op.subtract, Op.mult, Op.max, Op.min
-    ge, le, lt, eq = Op.is_ge, Op.is_le, Op.is_lt, Op.is_equal
+    ge, gt, le, lt, eq, ne = Op.is_ge, Op.is_gt, Op.is_le, Op.is_lt, Op.is_equal, Op.not_equal
     shr, band = Op.arith_shift_right, Op.bitwise_and
     R8 = (0, 128, 16)
     CAP = 928
+    NOL = 8193.0 / 16384
     axw, dew, axB, pari = I(512), I(512), I(512), I(8)
-    X, Qb = [B(2960), B(2960)], B(2048)
-    WA, WB = F(10240), F(10240)
+    XP, Qb = B(5024), B(2048)
+    X, Y3 = [B(2960), sl(XP, 2064, 5024)], sl(XP, 16, 2064)
+    XV, XL = [sl(x, 16, 2064) for x in X], [sl(x, 2064, 2960) for x in X]
+    WA, WB = F(10240), F(10592)
     dma([(axw, dr("axo", 0, 512))])
-    dma([(pp(sl(pari, 0, 6), (0, 8, 1)), dr("par", 0, 6))], q="a")
     dma([(dew, dr("den", 0, 512))], q="a")
-    Dd = B(8192 + 768)
-    dma([(sl(X[0], 0, 2048), dr("x0", 0, 2048))], lat=3500.0)
+    dma([(pp(sl(pari, 0, 6), (i, 128, 16)), dr("par", 0, 6)) for i in range(16)], q="a", lat=3000.0)
+    Dd, Ab = B(8192 + 896), B(2048)
+    dma([(XV[0], dr("x0", 0, 2048))], lat=3500.0)
+    dma([(sl(Y3, 0, ND[0]), dr("x0", 0, ND[0]))], lat=3500.0)
     dma([(sl(axB, 32 * i, 32 * i + 32), dr("axo", 0, 512, (i, 128, 16))) for i in range(16)], lat=5000.0)
     PAY, HELD, RAW = F(512), F(512), F(512)
-    ci, cf = I(16), F(48)
+    ci, cf = I(32), F(48)
     col = lambda k: sl(cf, k, k + 1)
-    pc, pi, gb, z15, d0c, sidb, p16, p16b, fr = [col(k) for k in range(9)]
-    iota(sl(ci, 0, 1), [[0, 1]], 0, 1)
+    cin = lambda k: sl(ci, k, k + 1)
+    pc, pi, gb, z15, d0c, d1c, fr = [col(k) for k in range(7)]
+    iota(cin(0), [[0, 1]], 0, 1)
     RI, NI = F(1024), F(512)
     iota(sl(RI, 0, 160), [[1, 160]], 0, 0)
-    cp(pc, sl(ci, 0, 1))
-    ts(sl(ci, 1, 2), sl(ci, 0, 1), 15, band)
-    cp(pi, sl(ci, 1, 2))
+    cp(pc, cin(0))
+    ts(cin(1), cin(0), 15, band)
+    cp(pi, cin(1))
     tt(gb, pc, pi, sub)
     iota(NI, [[16, 512]], 0, 1)
     iota(sl(RI, 160, 1024), [[1, 864]], 160, 0)
@@ -226,98 +253,106 @@ def build():
     R128, R144 = sl(RI, 0, 128), sl(RI, 0, 144)
     ts(z15, gb, 15.0, add)
     ts(d0c, pi, 0.0, eq)
-    ts(sidb, pi, -511.0, add)
-    ts(p16, pc, 16.0, mul)
-    ts(p16b, pc, 16.0, mul, 16.0, add)
-    up, tmp, tmp2, Mi = [sl(RAW, 128 * k, 128 * k + 128) for k in range(4)]
-    ts(up, R128, z15, le)
-    BO, TRI, TRH = B(128), B(128), B(128)
-    ts(tmp, R128, gb, ge)
-    tt(BO, tmp, up, mul)
-    ts(tmp2, R128, pc, ge)
-    tt(TRI, tmp2, up, mul)
-    Z, Z4, ZP, Z0, Zf, Z0f, BOf = B(144), B(144), B(144), B(144), F(144), F(144), F(128)
-    ts(Z0, R144, z15, eq, d0c, mul)
+    ts(d1c, pi, 1.0, eq)
+    BO, TRI, TRH, BOP, BOm, DLO, up = B(128), B(128), B(128), B(128), B(128), B(128), sl(Dd, 512, 640)
+    ID, IDf, O17, ONES, CJ = B(128), F(128), B(128), B(512), B(512)
+    ms(ONES, 1.0)
+    asel(up, sl(ONES, 0, 128), [[-16, 8], [0, 16]], ge, 0, 1)
+    asel(BO, up, [[16, 8], [0, 16]], ge, 15, -1)
+    asel(TRI, BO, [[1, 128]], ge, 0, -1)
+    Z, Z4, ZP, Z0, Z1, Z32, ZI4, Zq, Z0n = [B(144) for k in range(9)]
+    Z0f, BOf = F(144), F(128)
     ts(Z, R144, z15, eq)
-    cp(Zf, Z)
+    ts(Z0, Z, d0c, mul)
+    ts(Z1, Z, d1c, mul)
+    ts(Z0n, Z0, -32768.0, mul)
     cp(Z0f, Z0)
     ts(Z4, Z, 4.0, mul)
+    ts(Z32, Z, 32.0, mul)
+    ts(Zq, Z, 0.25, mul)
     p2, p2f = B(1), F(1)
     act(p2, pi, Fn.Exp, scale=math.log(2.0))
     cp(p2f, p2)
     ts(ZP, Z, p2f, mul)
     cp(BOf, BO)
-    ID, IDf, O24, ONES, CJ = B(128), F(128), B(128), B(512), B(512)
+    ts(BOP, BO, pi, mul)
+    ts(BOm, BO, -16.0, mul)
     ts(ID, R128, pc, eq)
     cp(IDf, ID)
-    ms(O24, 24.0)
-    ms(ONES, 1.0)
-    for j in range(4):
-        ms(sl(CJ, 128 * j, 128 * j + 128), 4.0 - j)
+    iota(O17, [[0, 128]], 17, 0)
+    iota(CJ, [[-1, 4], [0, 128]], 4, 0)
     WM = {1: ID}
-    for w in (-0.5, -1, 3, 4, 5, 16, 32, 128, 512, 2048):
+    for w in (507904, -0.5, -1, 4, 5, 16, 128, 512, 2048) + ((3,) if NC3 > 4 else ()):
         WM[w] = B(128)
         ts(WM[w], ID, float(w), mul)
     tt(TRH, TRI, WM[-0.5], sub)
-    I16, MK32 = B(32), F(32)
+    I16, NI16 = B(32), B(32)
     ts(I16, sl(RI, 0, 32), pi, eq)
-    cp(sl(MK32, 0, 16), sl(I16, 0, 16))
-    cp(sl(MK32, 16, 32), sl(I16, 0, 16))
-    EI, I16f = B(2048), F(16)
-    cp(I16f, sl(I16, 0, 16))
-    for i in range(16):
-        ts(sl(EI, 128 * i, 128 * i + 128), BO, sl(I16f, i, i + 1), mul)
+    ts(NI16, I16, -16384.0, mul, 16384.0, add)
+    EI = B(2048)
+    for i in range(4):
+        asel(sl(EI, 512 * i, 512 * i + 512), ONES, [[-1, 4], [-16, 8], [0, 16]], eq, -4 * i, 1)
     TM, TO = B(2048), B(512)
-    ts(Mi, R128, 1.0, add)
-    tt(Mi, Mi, up, mul)
-    ts(sl(ci, 2, 3), sl(ci, 0, 1), 3, band)
-    ts(sl(ci, 3, 4), sl(ci, 0, 1), 2, shr, 3, band)
-    ts(fr, sl(ci, 2, 3), 4.0, mul, gb, add)
-    ts(col(9), sl(ci, 3, 4), 12.0, add, gb, add)
+    ts(cin(2), cin(0), 3, band)
+    ts(cin(3), cin(0), 2, shr, 3, band)
+    cp(col(15), cin(3))
+    ts(ZI4, Z, col(15), mul)
+    ts(fr, cin(2), 4.0, mul, gb, add)
+    ts(col(9), cin(3), 12.0, add, gb, add)
     ts(col(10), fr, 3.0, add)
-    ZQ, ZB = sl(WB, 4096, 4096 + 576), F(576)
-    zq, zb, tm = sl(Dd, 0, 144), sl(Dd, 144, 288), sl(Dd, 512, 1024)
+    ZQ, ZB, ZBb = sl(WB, 4096, 4096 + 576), F(576), B(576)
+    zq, zb = sl(Dd, 0, 144), sl(Dd, 144, 288)
     ts(zq, R144, col(9), eq)
     ts(zb, R144, col(10), eq)
     for j in range(4):
-        ts(col(32 + j), fr, 1.0 + j, add)
-        ts(col(36 + j), sl(ci, 3, 4), float(j), eq)
-        ts(col(40 + j), sl(ci, 2, 3), float(j), eq)
+        ts(col(36 + j), cin(3), float(j), eq)
+        ts(col(40 + j), cin(2), float(j), eq)
         ts(sl(ZQ, 144 * j, 144 * j + 144), zq, col(40 + j), mul)
         ts(sl(ZB, 144 * j, 144 * j + 144), zb, col(36 + j), mul)
-        ts(sl(tm, 128 * j, 128 * j + 128), Mi, col(32 + j), ge)
+    cp(ZBb, ZB)
     for a in range(4):
         ts(sl(TO, 128 * a, 128 * a + 128), BO, col(36 + a), mul)
         for j in range(4):
             c = 128 * (4 * a + j)
-            ts(sl(TM, c, c + 128), sl(tm, 128 * j, 128 * j + 128), col(36 + a), mul)
-    DUM, LB32, ZR, DUC, CAPS, d9 = F(128), U(32), F(928), F(36), B(576), F(56)
+            asel(sl(TM, c, c + 128), sl(TO, 128 * a, 128 * a + 128), [[64, 8], [1, 16]], ge, 16 * a - j, -4)
+    DUM, LB32, ZR, DUC, CAPS, d9, d9r = F(128), U(32), F(928), F(36), B(576), F(56), F(56)
     DUL = sl(DUM, 0, 56)
     ts(DUM, sl(NI, 0, 128), 8192.0, add)
     ts(DUC, sl(NI, 0, 36), float(CAP), add)
-    ts(d9, sl(NI, 0, 56), 897.0, add)
+    ts(d9, sl(NI, 0, 56), 912.0, add)
+    ts(d9r, sl(NI, 0, 56), -112.0, add)
     ms(ZR, 0.0)
     ms(CAPS, float(CAP))
     ti = I(32)
     cp(ti, sl(NI, 0, 32))
     ts(ti, ti, 31, band)
     cp(LB32, ti)
-    parf, B8, B8b, PR = F(8), sl(PAY, 0, 128), sl(PAY, 128, 256), F(8)
-    p8 = (0, 8, 1)
-    cp(pp(sl(parf, 0, 6), p8), pp(sl(pari, 0, 6), p8))
-    ts(B8, R128, p16, ge)
-    ts(B8b, R128, p16b, lt)
-    tt(B8, B8, B8b, mul)
-    mm([(ps(7, 0, 6), pp(B8, p8), pp(sl(parf, 0, 6), p8), True, True)])
-    cp(sl(PR, 0, 6), ps(7, 0, 6))
+    PR = F(8)
+    cp(sl(PR, 0, 6), sl(pari, 0, 6))
     lo, th, hi, Kc = [sl(PR, k, k + 1) for k in range(4)]
-    ts(col(12), lo, -0.5, add)
-    ts(col(13), th, -0.5, add)
-    ts(col(14), hi, -1.0, mul, 0.5, add)
-    for x in X:
-        ms(sl(x, 2944, 2960), 0.0)
+    ts(col(16), lo, 16.0, mul)
+    ts(DLO, ID, col(16), mul)
+    ms(sl(X[0], 0, 16), 0.0)
+    ms(sl(X[1], 0, 16), 16.0)
+    ms(sl(XP, 0, 16), 16.0)
+    ts(col(12), Kc, -1.0, mul)
+    ts(cin(5), sl(pari, 3, 4), 7, band)
+    for k, m in ((5, 63), (8, 4095)):
+        ts(cin(k + 1), cin(k), col(12), mul, 2.0, add)
+        ts(cin(k + 1), cin(k + 1), m, band)
+        tt(cin(k + 2), cin(k), cin(k + 1), mul)
+        ts(cin(k + 3), cin(k + 2), m, band)
+    ts(cin(12), cin(11), Kc, mul)
+    ts(cin(12), cin(12), 8191, band)
+    tt(cin(13), cin(11), cin(12), add)
+    ts(cin(13), cin(13), -1.0, add)
+    ts(cin(14), cin(13), 127, band)
+    ts(cin(15), cin(13), 7, shr)
+    cp(sl(cf, 13, 15), sl(ci, 14, 16))
+    kl, kh = col(13), col(14)
     rot = [0]
-    LI, LH = [I(384), I(384), I(896)], [H(384), H(384), H(896)]
+    LI01 = I(768)
+    LI, LH = [sl(LI01, 0, 384), sl(LI01, 384, 768), I(896)], [H(384), H(384), H(896)]
 
     def lin(xi, fields, bank):
         n = wid(xi)
@@ -330,26 +365,23 @@ def build():
         mm([(out, WM[w], sl(b, k * n, k * n + n), k == 0, k == len(fields) - 1) for k, (s, m, w) in enumerate(fields)])
         return out
     POSA = [(2, 15, 512), (0, 3, 128), (6, 127, 1)]
-    POSB = [(9, 15, 512), (0, 15, 32), (4, 31, 1)]
     POSW = [(0, 15, 512), (4, 511, 1)]
 
-    TA, BP, t1, t2 = F(512), F(512), F(512), F(512)
-    ts(t1, dew, -1.0, mul, 11776.0, add)
+    TA, BP, t1 = F(512), F(512), F(512)
+    cp(t1, dew)
     for j in range(4):
-        mm([(ps(3, 128 * j, 128 * j + 128), sl(ZQ, 144 * j + 12 - 4 * a, 144 * j + 140 - 4 * a), sl(t1, a, 512, 4), a == 0, a == 3) for a in range(4)])
-    ts(t2, ps(3, 0, 512), 11777.0, lt)
-    tt(TA, ps(3, 0, 512), t2, mul)
+        last = None
+        for a in range(4):
+            last = mm([(ps(7, 128 * j, 128 * j + 128), sl(ZQ, 144 * j + 12 - 4 * a, 144 * j + 140 - 4 * a), sl(t1, a, 512, 4), a == 0, a == 3)], after=last)
+    ts(TA, ps(7, 0, 512), 1.0, add)
     LW, TAB = [U(32), U(32)], [B(512), B(512)]
-    lsi, tbi = I(512), I(512)
+    lsi, tbi = I(512), sl(LI01, 0, 512)
     for t in range(2):
         Ct = sl(PR, 4 + t, 5 + t)
-        a, b, c = I(32), I(32), F(32)
+        a = I(32)
         ts(a, sl(NI, 0, 32), Kc, mul, Ct, add)
-        ts(b, a, 4, shr, 31, band)
-        ts(a, a, 15, band)
-        ts(c, a, 32.0, mul)
-        tt(c, c, b, add)
-        cp(LW[t], c)
+        ts(a, a, 511, band)
+        cp(LW[t], a)
         ts(tbi, NI, Kc, mul, Ct, add)
         ts(tbi, tbi, 9, shr, 15, band)
         cp(HELD, tbi)
@@ -357,12 +389,11 @@ def build():
 
     CB = []
     for k in range(2):
-        w = (WA, WB)[k]
-        CB.append({"CU": H(592), "Q": F(576) if k else sl(WA, 9696, 10240), "SW": sl(w, 8192, 9696), "CR": H(928), "cl": U(64), "li": U(48),
-                   "st": F(48), "em": F(48)})
+        CB.append({"CU": H(592), "Q": F(576) if k else sl(WA, 9696, 10240), "SW": sl(WB, 9088, 10592) if k else sl(WA, 8192, 9696), "CR": H(928),
+                   "cl": U(64), "li": U(48), "st": F(48), "em": F(48)})
         ms(sl(CB[k]["CU"], 0, 1), 0.0)
 
-    def comp(k, NC, R, Pp, Tp, sb):
+    def comp(k, NC, R, Pp, Tp, sb, silu=True, off=0.0):
         c = CB[k]
         CU, Q, SW, CR, A = c["CU"], sl(c["Q"], 0, NC), c["SW"], sl(c["CR"], 0, R), NC // 16
         dma([(sl(SW, 0, R), sl(ZR, 0, R))])
@@ -374,8 +405,9 @@ def build():
         tt(em, em, sl(DUC, 0, A), mul)
         tt(em, em, st, mx)
         cp(li, em)
-        tt(Q, Pp, sl(CU, 0, NC), add)
-        act(ind(sl(SW, 0, CAP + NC), li), sl(RI, 32, 32 + NC), Fn.Silu)
+        mm(full(Pp, ID, sl(CU, 0, NC), False, True))
+        ts(Q, Pp, off, add)
+        cp(ind(sl(SW, 0, CAP + NC), li), sl(RI, 32, 32 + NC), silu)
         scan(CR, sl(SW, 0, R), sl(SW, 0, R), 32.0, mx, mx)
         cl = sl(c["cl"], 0, R // 16)
         mm(dg(ps(sb, 128, 128 + R // 16), CR, Z0))
@@ -383,107 +415,112 @@ def build():
         return Q, CR, cl
 
     OT, IT = F(56), F(56)
-    DB, DA = F(896), F(896)
+    DB, DA = F(928), F(896)
+    SB, LS = B(896), U(512)
+    ms(sl(DB, 896, 928), 0.0)
     for k, (tw, res) in enumerate(((axw, OT), (dew, IT))):
         w = (WA, WB)[k]
-        Fl, VAL, OH, IW = sl(Dd, 4096 + 512 * k, 4608 + 512 * k), sl(w, 0, 512), sl(w, 512, 1408), sl(w, 2048, 2048 + 1808)
+        Fl, OH = (sl(Dd, 4096, 4608), sl(Ab, 0, 512))[k], (sl(Dd, 6144, 7040), sl(Ab, 1024, 1920))[k]
+        VAL, IW = sl(w, 0, 512), sl(w, 2048, 2048 + 1808)
         EV = H(896) if k == 0 else LH[2]
-        SID = (DA, DB)[k]
+        SID = (DA, sl(DB, 0, 896))[k]
         b0 = 4 * k
         ts(Fl, tw, 8192.0, ge)
         mm([(ps(b0 + 1, 0, 512), BO, Fl, True, True)])
-        mm([(ps(b0, 0, 512), TRH, Fl, True, False), (ps(b0, 0, 512), WM[-0.5], ONES, False, True)])
+        mm([(ps(b0, 0, 512), TRH, Fl, True, False), (ps(b0, 0, 512), WM[-0.5], ONES, False, 2)])
         dma([(sl(IW, 0, 912), sl(ZR, 0, 912))])
-        if k == 0:
-            ki, k2 = sl(LI[2], 0, 512), sl(w, 1408, 1920)
-            ts(ki, tw, 2, shr, 127, band)
-            ts(k2, ki, 2.0, mul)
-            ts(VAL, tw, -0.25, mul, 2817.0, add)
-            tt(VAL, VAL, k2, add)
-        else:
-            ts(VAL, tw, 0.25, mul, -2047.0, add)
-        Q, CR, cl = comp(k, 512, 896, ps(b0, 0, 512), ps(b0 + 1, 0, 512), b0 + 2)
-        if k == 0:
-            mm(full(ps(b0, 0, 896), WM[16], CR))
-            act(SID, ps(b0, 0, 896), bias=sidb)
+        ts(VAL, tw, 0.25, mul, -2032.0, add)
+        Q, CR, cl = comp(k, 512, 896, ps(b0, 0, 512), ps(b0 + 1, 0, 512), b0 + 2, k == 1)
         tt(OH, ind(Q, cl), sl(RI, 1, 897), eq)
         tt(EV, ind(VAL, cl), OH, mul)
         o = ps(b0 + 3, 0, 56)
         mm(dg(o, EV, Z))
         z, li = F(56), U(56)
-        ts(z, o, 0.0, eq)
-        tt(z, z, d9, mul)
-        tt(z, o, z, add)
+        if k == 0:
+            oi, k2 = I(56), F(56)
+            ts(oi, o, -16.0, add)
+            ts(z, o, 0.0, eq)
+            ts(oi, oi, 127, band)
+            tt(z, z, d9r, mul)
+            ts(k2, oi, 2.0, mul, 800.0, add)
+            tt(z, z, o, sub)
+            tt(z, z, k2, add)
+        else:
+            ts(z, o, 0.0, eq)
+            tt(z, z, d9, mul)
+            tt(z, o, z, add)
         cp(li, z)
         if k == 0:
-            tt(ind(IW, li), OH, SID, mul)
-        else:
-            n33 = sl(w, 1408, 1920)
-            ts(n33, NI, 33.0, add)
-            tt(SID, ind(n33, cl), OH, mul)
-            act(ind(IW, li), SID, Fn.Silu)
-        o = ps(b0 + 2, 256, 312)
-        mm(dg(o, sl(IW, 1, 897), Zf))
+            o2, nl0 = ps(2, 256, 312), U(56)
+            last = mm(dg(o2, CR, Zq, True, False))
+            mm(dg(o2, OH, ZI4, False, True), after=last)
+            ts(nl0, o2, -128.0, add)
+            cp(SB, ind(XV[0], nl0))
+            ms(sl(Qb, 16, 912), 0.0)
+            cp(ind(sl(Qb, 0, 1808), li), SB)
+            exch(sl(Qb, 16, 912), XL[0], 128)
+        mm(full(ps(b0, 0, 896), WM[16], CR, True, False) + full(ps(b0, 0, 896), BOP, OH, False, True))
+        ts(SID, ps(b0, 0, 896), -479.0, add)
+        cp(ind(IW, li), SID, True)
+        o = ps(b0 + 2, 320, 376)
+        mm(dg(o, sl(IW, 16, 912), Z0f))
         if k == 0:
             ui, LO = I(56), U(56)
-            ts(ui, o, -1.0, add, 0.0, mx)
+            ts(ui, o, -33.0, add, 0.0, mx)
             ts(ui, ui, 2, shr)
             cp(LO, ui)
-        act(res, o, Fn.Relu, bias=-32.0 * k)
+        ts(res, o, -32.0, add, 0.0, mx)
 
-    ts(BP, axB, 1.0, add)
-    dma([(pp(sl(WA, 0, 8192), R8), TA)])
+    for i in range(16):
+        ts(sl(BP, i, 512, 16), sl(axB, 32 * i, 32 * i + 32), 33.0, add)
+    dma([(pp(sl(WA, 0, 8192), R8), sl(ZR, 0, 512))])
     dma([(pp(sl(WB, 0, 8192), R8), BP)])
 
-    SB, LS = B(896), U(512)
-    ACCf, ACCi, Ab = DA, LI[2], B(2048)
+    ACCf, ACCi = DA, LI[2]
 
     def send_x(k):
-        x = X[k % 2]
-        cp(sl(SB, 0, 448), ind(sl(x, 0, 2048), sl(LO, 0, 28)))
-        cp(sl(SB, 448, 896), ind(sl(x, 0, 2048), sl(LO, 28, 56)))
-        exch(SB, sl(x, 2048, 2944), 128)
-        n = (ND1, ND2, 2048)[k % 3]
-        if k != 3:
-            dma([(sl(Qb, 0, n), sl(x, 0, n))])
+        cp(sl(SB, 0, 448), ind(XV[k % 2], sl(LO, 0, 28)))
+        cp(sl(SB, 448, 896), ind(XV[k % 2], sl(LO, 28, 56)))
+        exch(SB, XL[k % 2], 128)
 
     def lst(j, a, b): return sl(LS, 128 * j + a // 16, 128 * j + b // 16)
 
+    def rem16(y, o, q, pe):
+        ts(q, o, -7.5, add)
+        if pe:
+            mm([(o, WM[-1], q, False, True)])
+            cp(y, o)
+        else:
+            tt(y, o, q, sub)
+
     def step(k, mod):
-        x, y = X[k % 2], X[(k + 1) % 2]
-        nd = ND2 if mod else ND1
+        w, x, y = X[k % 2], XV[k % 2], XV[(k + 1) % 2]
+        nd = ND[k]
         for bank, a in enumerate(range(nd, 2048, 512)):
             b = min(a + 512, 2048)
             o = ps(bank, 0, b - a)
-            last = mm([(o, ID, sl(x, a, b), True, False)] + ([(o, O24, sl(ONES, 0, b - a), False, False)] if mod else []))
+            last = mm([(o, ID, sl(x, a, b), True, False)] + ([(o, O17, sl(ONES, 0, b - a), False, False)] if mod else []))
             for j in range(4):
                 v = sl(Dd, 2048 * j + a, 2048 * j + b)
-                act(v, ind(x, lst(j, a, b)))
-                last = mm([(o, ID, v, False, j == 3)], after=last)
+                cp(v, ind(w, lst(j, a, b)))
+                last = mm([(o, ID, v, False, (j == 3) * (2 if mod and bank < NPE[k] else 1))], after=last)
             if mod:
-                ts(sl(Qb, a, b), o, -7.5, add)
-                tt(sl(y, a, b), o, sl(Qb, a, b), sub)
+                rem16(sl(y, a, b), o, sl(Qb, a, b), bank < NPE[k])
+                dma([(sl(Qb, a, b), sl(y, a, b))])
             else:
                 cp(sl(y, a, b), o)
         h = nd // 2
-        for j in range(4):
+        for j in range(4 if nd else 0):
             for a in (0, h):
-                acc = sl(ACCf, a, a + h) if mod else sl(Qb, a, a + h)
-                out = acc if j < 3 else (sl(ACCi, a, a + h) if mod else sl(y, a, a + h))
-                tt(out, ind(x, lst(j, a, a + h)), acc if j else sl(Qb, a, a + h), add)
-        if mod:
-            for a in (0, h):
-                ts(sl(ACCi, a, a + h), sl(ACCi, a, a + h), 15, band)
-                cp(sl(y, a, a + h), sl(ACCi, a, a + h))
+                acc = sl(Qb, a, a + h)
+                tt(acc if j < 3 else sl(y, a, a + h), ind(w, lst(j, a, a + h)), acc if j else sl(Y3, a, a + h), add)
 
     CP3 = [(0, 0, 0), (1, 0, 0), (0, 0, 1), (1, 0, 1), (0, 1, 0), (1, 1, 0), (0, 1, 1), (1, 1, 1)][:NC3]
-    KEY = PAY
-    KW, MK, FLk, LK, LM = B(1024), B(1792), sl(Dd, 2048, 3840), U(112), U(112)
+    MKE, LK, LM, LO3 = F(896), U(56), U(56), U(56)
     NK, FT, G1, CT, CG, cmpf = sl(Ab, 0, 512), sl(Ab, 512, 1024), sl(Ab, 1024, 1536), sl(Qb, 0, 768), sl(Qb, 768, 1696), sl(Ab, 1536, 1792)
+    VAC, FLk = sl(Ab, 0, 512), sl(Qb, 0, 896)
     FG, Y1, Y1i, Wc = B(576), t1, axw, F(32)
     ms(sl(FG, 568, 576), 0.0)
-    SBLs, LBLs = [B(112), B(112)], [B(112), B(112)]
-    WR1, WR2 = HELD, t2
     mark, high = dict(TOP), dict(TOP)
 
     for t in range(2):
@@ -493,146 +530,222 @@ def build():
             TOP[a] = mark[a]
         Ct = sl(PR, 4 + t, 5 + t)
         k0 = 3 * t
-        ts(lsi, TA, -0.25, mul, 2943.625, add)
+        ts(lsi, TA, 0.25, mul, 15.375 - 8 * t, add)
         cp(LS, lsi)
+        if fin:
+            ts(dew, TA, -32.0, add, 0.0, mx)
+            cp(TA, dew)
+            dma([(pp(sl(WA, 0, 8192), R8), TA)])
+            ts(axB, BP, -32.0, add, 0.0, mx)
+            cp(BP, axB)
+            dma([(pp(sl(WB, 0, 8192), R8), BP)])
         if t == 0:
-            send_x(0)
             step(0, False)
         send_x(k0 + 1)
-        ts(PAY, TA, -1.0 / 16384, mul, 0.71875, add)
-        act(HELD, TA, Fn.Sign)
-        ms(sl(KW, 512, 1024), 0.0)
-        bt, l1, l2, PABd = I(128), F(128), F(128), F(128)
-        for q in range(4):
-            c = 32 * (4 * q + t)
-            ts(sl(bt, 32 * q, 32 * q + 32), sl(BP, c, c + 32), -1.0, add)
-        o = lin(bt, POSA, 6)
-        tt(PABd, o, DUM, sub)
-        ts(l1, bt, 0.0, ge)
-        ts(l2, bt, 8192.0, lt)
-        tt(l1, l1, l2, mul)
-        tt(PABd, PABd, l1, mul)
-        hd, pd, p1 = [F(56), F(56)], [F(56), F(56)], F(56)
-        for s, (tb, fl) in enumerate(((IT, POSA), (OT, POSB))):
-            a, b, c = I(56), I(56), F(56)
-            ts(a, tb, -1.0, add, 0.0, mx)
-            o = lin(a, fl, 5 + s)
-            cp(a, o)
-            tt(pd[s], o, DUL, sub)
-            act(hd[s], tb, Fn.Sign)
-            ts(b, a, 511, band)
-            ts(sl(LK, 56 * s, 56 * s + 56), b, 512.0 * s, add)
-            ts(a, a, 9, shr)
-            ts(c, hd[s], -16.0, mul, 16.0, add)
-            tt(c, c, a, add)
-            cp(sl(LM, 56 * s, 56 * s + 56), c)
-            cp(sl(MK, 896 * s, 896 * s + 896), ind(I16, sl(LM, 56 * s, 56 * s + 56)))
-        tt(pd[0], pd[0], hd[0], mul)
-        tt(p1, pd[0], DUL, add)
-        nh = F(56)
-        ts(nh, hd[0], -1.0, mul, 1.0, add)
+        ts(PAY, TA, 1.0 / 16384, mul, -1.0 / 16384, add)
+        ts(VAC, TA, 0.0, eq, 2048.0, mul)
+        hd0, hd1, nh, pd1, pdj, c, e = [F(56) for k in range(7)]
+        a, b, u, un, uz = [I(56) for k in range(5)]
+        ts(a, IT, -1.0, add, 0.0, mx)
+        ts(nh, IT, 0.5, lt)
+        ts(b, a, 6, shr)
+        cp(LK, b)
+        ts(b, a, 2, shr, 15, band)
+        ts(c, nh, 16.0, mul)
+        tt(c, c, b, mx)
+        cp(LM, c)
+        iota(MKE, [[4, 896]], 8192, 0)
+        tt(MKE, ind(NI16, LM), MKE, add)
+        ts(u, OT, -1.0, add, 0.0, mx)
+        tt(pd1, u, DUL, sub)
+        ts(un, u, 2, shr)
+        ts(uz, u, 3, band)
+        if not fin:
+            ts(hd1, OT, 0.5, ge, 16.0, mul)
+            ts(e, uz, 0.0, eq, 2064.0, mul)
+            tt(e, e, un, add)
+            tt(e, e, hd1, add)
+            cp(LO3, e)
+            ts(dew, TA, 0.25, mul, 0.125, add)
+            ts(RAW, lsi, 2065.0, mul, -30960.0, add)
+            ts(HELD, dew, 2064.0, mul)
+            tt(RAW, RAW, HELD, sub)
+        else:
+            ts(hd0, IT, 0.5, ge)
+            ts(hd1, OT, 0.5, ge)
+            cp(LO3, un)
+            ts(e, uz, 1.0, eq)
+            tt(e, e, hd1, mul)
+            pd0, p1 = F(56), F(56)
+            o = lin(a, POSA, 5)
+            tt(pd0, o, DUL, sub)
+            tt(pd0, pd0, hd0, mul)
+            tt(p1, pd0, DUL, add)
+            bt, l1, l2, PABd = I(128), F(128), F(128), F(128)
+            ts(bt, sl(BP, t, 512, 4), -1.0, add)
+            o = lin(bt, POSA, 6)
+            tt(PABd, o, DUM, sub)
+            ts(l1, bt, 0.0, ge)
+            ts(l2, bt, 8192.0, lt)
+            tt(l1, l1, l2, mul)
+            tt(PABd, PABd, l1, mul)
+            ms(sl(XP, 0, 512), 0.0)
+            for q in range(4):
+                last = None
+                for j in range(4):
+                    last = mm([(ps(4, q, 512, 4), sl(ZB, 144 * q + 3 - j, 144 * q + 131 - j), sl(TA, 128 * j, 128 * j + 128), j == 0, j == 3)], after=last)
+            cp(HELD, ps(4, 0, 512))
+        j0, j1_, j2 = I(56), I(56), I(56)
+        ts(j0, u, Ct, sub)
+        ts(j0, j0, 8191, band)
+        ts(j1_, j0, kh, mul)
+        ts(j1_, j1_, 63, band)
+        ts(j2, j0, kl, mul)
+        ts(j1_, j1_, 128.0, mul)
+        tt(j2, j2, j1_, add)
+        o = lin(j2, POSW, 5)
+        tt(pdj, o, DUL, sub)
         step(k0 + 1, True)
         send_x(k0 + 2)
-        x, y = X[k0 % 2], X[(k0 + 1) % 2]
+        w, x, y = X[k0 % 2], XV[k0 % 2], (XV[0] if fin else Y3)
         far = ps(4, 0, 512)
-        lf = mm([(far, ID, CJ, True, False), (far, IDf, PAY, False, False)])
+        lf = mm([(far, ID, CJ, True, False), (far, WM[-1], VAC, False, False), (far, IDf, PAY, False, False)])
         SL, SBp = ps(5, 0, 128), ps(6, 0, 128)
         lsb = None
         for hf in range(2):
             lx = [mm([(ps(2 * hf + i, 0, 512), WM[5 - sum((hf, j, i) in CP3 for j in range(4))], sl(x, 1024 * hf + 512 * i, 1024 * hf + 512 * i + 512), True, False),
-                      (ps(2 * hf + i, 0, 512), O24, ONES, False, False)]) for i in range(2)]
+                      (ps(2 * hf + i, 0, 512), O17, ONES, False, False)]) for i in range(2)]
             for j in range(4):
                 ab = sl(Ab, 1024 * (j % 2), 1024 * (j % 2) + 1024)
                 for i in range(2):
                     a = 1024 * hf + 512 * i
                     d = sl(Dd, 2048 * j + a, 2048 * j + a + 512)
                     if (hf, j, i) in CP3:
-                        act(d, ind(x, lst(j, a, a + 512)))
+                        act(d, ind(w, lst(j, a, a + 512)))
                         mm([(ps(7, 0, 512), ID, d, True, False), (ps(7, 0, 512), WM[-1], sl(x, a, a + 512), False, True)])
                         act(sl(ab, 512 * i, 512 * i + 512), ps(7, 0, 512), Fn.Abs)
                     else:
-                        tt(d, ind(x, lst(j, a, a + 512)), sl(Qb, a, a + 512), sub)
+                        tt(d, ind(w, lst(j, a, a + 512)), sl(Qb, a, a + 512), sub)
                         act(sl(ab, 512 * i, 512 * i + 512), d, Fn.Abs)
-                    lx[i] = mm([(ps(2 * hf + i, 0, 512), ID, d, False, j == 3)], after=lx[i])
+                    lx[i] = mm([(ps(2 * hf + i, 0, 512), ID, d, False, (j == 3) * (2 if 2 * hf + i < NPE[k0 + 2] else 1))], after=lx[i])
                 c = 128 * j + 64 * hf
                 lf = mm(dg(ps(4, c, c + 64), ab, Z4, False, hf == 1 and j == 3), after=lf)
             for i in range(2):
                 a = 1024 * hf + 512 * i
-                ts(sl(Qb, a, a + 512), ps(2 * hf + i, 0, 512), -7.5, add)
-                tt(sl(y, a, a + 512), ps(2 * hf + i, 0, 512), sl(Qb, a, a + 512), sub)
-            lsb = mm([(SBp, sl(Z, 15 - ii, 143 - ii), sl(y, 128 * ii, 128 * ii + 128), ii == 0, ii == 15) for ii in range(8 * hf, 8 * hf + 8)], after=lsb)
+                rem16(sl(y, a, a + 512), ps(2 * hf + i, 0, 512), sl(Qb, a, a + 512), 2 * hf + i < NPE[k0 + 2])
             mm(dg(ps(5, 64 * hf, 64 * hf + 64), sl(y, 1024 * hf, 1024 * hf + 1024), Z))
+            lsb = mm([(SBp, sl(Z, 15 - ii, 143 - ii), sl(y, 128 * ii, 128 * ii + 128), ii == 0, ii == 15) for ii in range(8 * hf, 8 * hf + 8)], after=lsb)
         if fin:
-            dma([(dr("yx", 0, 2048), sl(y, 0, 2048))])
+            dma([(dr("yx", 0, 2048), y)])
+            dma([(pp(sl(Dd, 0, 8192), R8), sl(XP, 0, 512))])
+        h2, m1, m2, dk, thf, nka, tp = F(256), F(256), F(128), F(128), F(128), F(128), F(128)
+        ri, pay, zi, lb, lbu = I(128), I(128), I(128), F(128), U(128)
+        ts(dk, SL, hi, lt, 1000.0 + NOL, mul)
+        if fin:
+            ts(thf, SL, th, lt)
         else:
-            send_x(3)
-        kac, nka, la, lau = F(128), F(128), F(128), U(128)
-        for q in range(4):
-            act(sl(nka, 32 * q, 32 * q + 32), ps(6, q, 128, 4), Fn.Sign, bias=col(12), scale=-1.0)
-        act(kac, nka, Fn.Relu)
-        tt(la, kac, PABd, mul)
-        tt(la, la, DUM, add)
-        cp(lau, la)
-        for a in range(0, 128, 32):
-            cp(ind(WA, sl(lau, a, a + 32)), sl(ZR, 0, 512), True)
-        fh, thf, m1, m2, ri, zi, lb, lbu = F(128), F(128), F(256), F(128), I(128), I(128), F(128), U(128)
-        act(fh, SL, Fn.Sign, bias=col(14))
-        act(thf, SL, Fn.Sign, bias=col(13), scale=-1.0)
-        act(fh, fh, Fn.Relu)
-        act(thf, thf, Fn.Relu)
-        tt(KEY, far, HELD, mul)
-        tt(m1, sl(KEY, 0, 256), sl(KEY, 256, 512), mx)
+            ts(thf, SL, th, ge, -1e9, mul)
+        ts(nka, SBp, lo, ge)
+        cp(h2, ps(4, 256, 512))
+        tt(m1, ps(4, 0, 256), h2, mx)
         tt(m2, sl(m1, 0, 128), sl(m1, 128, 256), mx)
-        tt(m2, m2, fh, mul)
-        for j in range(4):
-            tt(sl(KW, 128 * j, 128 * j + 128), sl(KEY, 128 * j, 128 * j + 128), m2, eq)
-        for q in range(4):
-            c = 512 + 32 * (4 * q + t)
-            cp(sl(KW, c, c + 32), sl(kac, 32 * q, 32 * q + 32))
-        SBL, LBL = SBLs[t], LBLs[t]
-        for s in range(2):
-            tt(sl(FLk, 896 * s, 896 * s + 896), ind(KW, sl(LK, 56 * s, 56 * s + 56)), sl(MK, 896 * s, 896 * s + 896), mul)
-            mm(dg(ps(2 + s, 0, 56), sl(FLk, 896 * s, 896 * s + 896), Z))
-        go, alive = sl(SBL, 0, 112, 2), sl(SBL, 1, 112, 2)
-        cp(go, ps(2, 0, 56))
-        tt(alive, hd[1], ps(3, 0, 56), sub)
-        exch(SBL, LBL, 16)
-        ts(ri, m2, 0.5, mx, 16384.0, mul)
-        o = lin(ri, POSB, 7)
+        tt(m2, m2, dk, mx)
+        ts(ri, m2, NOL, mx, 16384.0, mul)
+        ts(pay, ri, 16383, band)
+        for q in range(2):
+            tt(sl(FLk, 448 * q, 448 * q + 448), ind(pay, sl(LK, 28 * q, 28 * q + 28)), sl(MKE, 448 * q, 448 * q + 448), eq)
         ts(zi, ri, 13, shr, 1, band)
+        ts(ri, ri, 8191, band)
         tt(lb, DUM, zi, mul)
-        tt(lb, o, lb, mx)
+        tt(lb, lb, ri, mx)
         cp(lbu, lb)
         for a in range(0, 128, 32):
-            cp(ind(WB, sl(lbu, a, a + 32)), sl(ZR, 0, 512), True)
-        gO, aI = sl(LBL, 0, 112, 2), sl(LBL, 1, 112, 2)
-        a, b, au, bu = F(56), F(56), U(56), U(56)
-        tt(a, aI, pd[0], mul)
-        tt(a, p1, a, sub)
-        cp(au, a)
-        cp(ind(WA, au), sl(ZR, 0, 896), True)
-        tt(b, gO, pd[1], mul)
+            cp(ind(sl(WB, 0, 10240), sl(lbu, a, a + 32)), sl(ZR, 0, 512), True)
+        ts(tp, pay, 1.0, add)
+        for j in range(4):
+            tt(sl(NK, 128 * j, 128 * j + 128), sl(TA, 128 * j, 128 * j + 128), tp, ne)
+        dma([(BP, pp(sl(WB, 0, 8192), R8))])
+        tt(sl(BP, t, 512, 4), sl(BP, t, 512, 4), nka, mul)
+        gq, ng, b, bu, bj, bju = F(56), F(56), F(56), U(56), F(56), U(56)
+        if not fin:
+            for q in range(4):
+                a = 512 * q
+                mm([(ps(q, 0, 512), BOm, sl(y, a, a + 512), True, False), (ps(q, 0, 512), DLO, ONES, False, True)])
+                tt(sl(XV[1], a, a + 512), ps(q, 0, 512), sl(y, a, a + 512), mx)
+                ts(sl(XV[1], a, a + 512), sl(XV[1], a, a + 512), 16.0, mn)
+            cp(sl(SB, 0, 448), ind(sl(XP, 0, 4128), sl(LO3, 0, 28)))
+            cp(sl(SB, 448, 896), ind(sl(XP, 0, 4128), sl(LO3, 28, 56)))
+            for q in range(2):
+                a = 448 * q
+                mm([(ps(2 + q, 0, 448), sl(Z32, 14, 142), sl(FLk, a, a + 448), True, False), (ps(2 + q, 0, 448), ID, sl(SB, a, a + 448), False, True)])
+                cp(sl(SB, a, a + 448), ps(2 + q, 0, 448))
+            exch(SB, XL[1], 128)
+            go, alive, gO, aI = F(56), F(56), F(56), F(56)
+            mm(dg(ps(6, 128, 184), SB, Z0) + dg(ps(6, 192, 248), FLk, Z))
+            ts(alive, ps(6, 128, 184), 16.0, lt)
+            cp(go, ps(6, 192, 248))
+            tt(HELD, RAW, NK, mul)
+            cp(LS, HELD)
+            mm(dg(ps(7, 0, 56), XL[1], Z1))
+            ts(gO, ps(7, 0, 56), 32.0, ge)
+            mm(dg(ps(6, 256, 312), XL[1], Z0))
+            ts(aI, ps(6, 256, 312), 16.0, lt)
+            FLp = ps(0, 0, 512)
+            lf = mm([(FLp, WM[507904], ONES, True, False)])
+            for hf in range(2):
+                for j in range(4):
+                    for a in (1024 * hf, 1024 * hf + 512):
+                        cp(sl(Dd, 2048 * j + a, 2048 * j + a + 512), ind(XP, lst(j, a, a + 512)))
+                    c = 128 * j + 64 * hf
+                    lf = mm(dg(ps(0, c, c + 64), sl(Dd, 2048 * j + 1024 * hf, 2048 * j + 1024 * hf + 1024), Z0n, False, hf == 1 and j == 3), after=lf)
+        else:
+            kac, la, lau = F(128), F(128), U(128)
+            ts(kac, SBp, lo, lt)
+            tt(la, kac, PABd, mul)
+            tt(la, la, DUM, add)
+            cp(lau, la)
+            for a in range(0, 128, 32):
+                cp(ind(WA, sl(lau, a, a + 32)), sl(ZR, 0, 512), True)
+            SBL, LBL, lw = B(112), B(112), F(56)
+            go, alive = sl(SBL, 0, 112, 2), sl(SBL, 1, 112, 2)
+            cp(sl(SB, 0, 448), ind(y, sl(LO3, 0, 28)))
+            cp(sl(SB, 448, 896), ind(y, sl(LO3, 28, 56)))
+            mm(dg(ps(3, 0, 56), SB, Z))
+            ts(lw, ps(3, 0, 56), lo, lt)
+            tt(lw, lw, e, mul)
+            tt(alive, hd1, lw, sub)
+            mm(dg(ps(2, 0, 56), FLk, Z))
+            cp(go, ps(2, 0, 56))
+            exch(SBL, LBL, 16)
+            gO, aI = sl(LBL, 0, 112, 2), sl(LBL, 1, 112, 2)
+            a, au = F(56), U(56)
+            tt(a, aI, pd0, mul)
+            tt(a, p1, a, sub)
+            cp(au, a)
+            cp(ind(sl(WA, 0, 9088), au), sl(ZR, 0, 896), True)
+            dma([(TA, pp(sl(WA, 0, 8192), R8))])
+            tt(NK, TA, NK, mn)
+        tt(gq, gO, alive, mul)
+        tt(bj, gq, pdj, mul)
+        tt(bj, bj, DUL, add)
+        cp(bju, bj)
+        LJ = sl(Qb, 1536, 2048)
+        if fin:
+            cp(ind(Dd, sl(bju, 0, 28)), sl(ONES, 0, 448))
+            cp(ind(Dd, sl(bju, 28, 56)), sl(ONES, 0, 448))
+            dma([(LJ, pp(sl(Dd, 0, 8192), R8))])
+        else:
+            cp(ind(sl(WA, 0, 9088), bju), sl(RI, 32, 928), True)
+            dma([(PAY, pp(sl(WA, 0, 8192), R8))])
+            act(LJ, PAY, Fn.Sign)
+            dma([(pp(sl(WB, 0, 8192), R8), BP)])
+        tt(ng, alive, gq, sub)
+        tt(b, gO, pd1, mul)
         tt(b, b, DUL, add)
         cp(bu, b)
-        cp(ind(WB, bu), sl(ZR, 0, 896), True)
-        dma([(TA, pp(sl(WA, 0, 8192), R8))])
-        dma([(BP, pp(sl(WB, 0, 8192), R8))])
-        ts(NK, sl(KW, 0, 512), -1.0, mul, 1.0, add)
-        ts(nka, kac, -1.0, mul, 1.0, add)
-        tt(TA, TA, NK, mul)
-        for q in range(4):
-            c = 32 * (4 * q + t)
-            tt(sl(BP, c, c + 32), sl(BP, c, c + 32), sl(nka, 32 * q, 32 * q + 32), mul)
-        if not fin:
-            ts(lsi, TA, -0.25, mul, 2943.625, add)
-            cp(LS, lsi)
-            for j in range(4):
-                for a in range(0, 2048, 512):
-                    cp(sl(Dd, 2048 * j + a, 2048 * j + a + 512), ind(X[1], lst(j, a, a + 512)))
+        cp(ind(sl(WB, 0, 9088), bu), sl(ZR, 0, 896), True)
         z0 = 8 * (6 - t)
-        ng, fre, cs8, Qf, qb = F(56), B(8), F(16), F(8), F(8)
-        ts(ng, gO, -1.0, mul, 1.0, add)
-        tt(ng, ng, alive, mul)
+        fre, cs8, Qf, qb, nlv = B(8), F(16), F(8), F(8), F(32)
         ts(fre, sl(ng, z0, z0 + 8), -1.0, mul, 1.0, add)
         mm([(ps(2, 64, 72), TRI, fre, True, True), (ps(2, 80, 88), BO, fre, True, True)])
         ms(sl(cs8, 0, 1), 0.0)
@@ -642,41 +755,50 @@ def build():
         for c in range(8):
             act(sl(cmpf, 32 * c, 32 * c + 32), sl(RI, 0, 32), Fn.Sign, bias=sl(qb, c, c + 1))
         mm([(ps(3, 64, 96), BO, sl(cmpf, 32 * c, 32 * c + 32), c == 0, c == 7) for c in range(8)])
-        one = 0.0 if fin else 1.0
-        ts(sl(DB, 768, 800), ps(3, 64, 96), 2.0, mul, 8448.0 + 512 * t + one, add)
+        one = 0.0 if fin else 33.0
+        ts(nlv, ps(3, 64, 96), 2.0, mul, 8448.0 + 512 * t + one, add)
         tt(sl(FG, 0, 56), aI, nh, mul)
-        ts(G1, ind(BP, LW[t]), 0.5, lt)
+        act(G1, ind(BP, LW[t]), Fn.Sign, bias=0.5 if fin else 32.5, scale=-1.0)
         mm(dg(ps(6, 0, 32), G1, ZP))
-        ts(Wc, ps(6, 0, 32), 0.5, add)
+        ts(Wc, ps(6, 0, 32), 0.5, mul, 32768.0, add)
         tt(Y1, ind(Wc, LB32), TAB[t], mul)
         ts(Y1i, Y1, -0.5, add)
         ts(Y1i, Y1i, 1, band)
         cp(sl(FG, 56, 568), Y1i)
+        for bank, l in ((4, BO), (2, TRI)):
+            mm([(ps(bank, 0, 512), l, sl(FG, 0, 512), True, False), (ps(bank, 56, 512), l, sl(LJ, 0, 456), False, 1 + (bank == 2)),
+                (ps(bank, 512, 576), l, sl(FG, 512, 576), True, False), (ps(bank, 512, 568), l, sl(LJ, 456, 512), False, 1 + (bank == 2))])
         for j in range(4):
-            tt(sl(FT, 128 * j, 128 * j + 128), sl(TA, 128 * j, 128 * j + 128), thf, lt)
-        mm([(ps(1, a, 512, 4), sl(TO, 128 * a, 128 * a + 128), sl(FT, 128 * j, 128 * j + 128), j == 0, j == 3) for a in range(4) for j in range(4)])
-        mm([(ps(0, a, 512, 4), sl(TM, 128 * (4 * a + j), 128 * (4 * a + j) + 128), sl(FT, 128 * j, 128 * j + 128), j == 0, j == 3)
-            for a in range(4) for j in range(4)])
+            if fin:
+                tt(sl(FT, 128 * j, 128 * j + 128), sl(NK, 128 * j, 128 * j + 128), thf, lt)
+            else:
+                tt(sl(FT, 128 * j, 128 * j + 128), ps(0, 128 * j, 128 * j + 128), thf, lt)
         if not fin:
+            ts(TA, TA, 32.0, add)
+            tt(TA, FLp, TA, mn)
             dma([(pp(sl(WA, 0, 8192), R8), TA)])
-            dma([(pp(sl(WB, 0, 8192), R8), BP)])
-        QT, CRT, clT = comp(0, 512, 768, ps(0, 0, 512), ps(1, 0, 512), 6)
-        mm(full(ps(4, 0, 576), BO, FG))
-        mm(full(ps(2, 0, 576), TRI, FG))
+        for a in range(4):
+            mm([(ps(1, a, 512, 4), sl(TO, 128 * a, 128 * a + 128), sl(FT, 128 * j, 128 * j + 128), j == 0, j == 3) for j in range(4)])
+        last = mm([(ps(0, 0, 512), WM[-0.5], ONES, True, False)])
+        for a in range(4):
+            last = mm([(ps(0, a, 512, 4), sl(TM, 128 * (4 * a + j), 128 * (4 * a + j) + 128), sl(FT, 128 * j, 128 * j + 128), False, 2 * (a + j == 6))
+                       for j in range(4)], after=last)
         QG, CRG, clG = comp(1, 576, 928, ps(2, 0, 576), ps(4, 0, 576), 7)
+        QT, CRT, clT = comp(0, 512, 768, ps(0, 0, 512), ps(1, 0, 512), 6, True, 0.5)
         if fin:
-            act(HELD, TA, Fn.Sign)
-            ts(HELD, HELD, 11777.0, mul, -1.0, add)
-            tt(RAW, HELD, TA, sub)
             for a in range(4):
-                mm([(ps(4, a, 512, 4), sl(ZB, 144 * a + 3 - j, 144 * a + 131 - j), sl(RAW, 128 * j, 128 * j + 128), j == 0, j == 3) for j in range(4)])
-            cp(WR1, ps(4, 0, 512))
-            ts(PAY, BP, -1.0, add)
-            dma([(pp(WR2, (i, 128, 16)), sl(PAY, 32 * i, 32 * i + 32)) for i in range(16)], lat=5000.0)
-            dma([(pp(sl(WA, 0, 8192), R8), WR1)])
-            dma([(pp(sl(WB, 0, 8192), R8), WR2)])
+                mm([(ps(4, a, 512, 4), sl(ZBb, 144 * a + 3 - j, 144 * a + 131 - j), sl(NK, 128 * j, 128 * j + 128), j == 0, j == 3) for j in range(4)])
+            tt(HELD, ps(4, 0, 512), HELD, mul)
+            ts(HELD, HELD, -1.0, add)
+            dma([(pp(sl(WA, 0, 8192), R8), HELD)])
+            dma([(PAY, pp(sl(WB, 0, 8192), R8))])
+            tt(sl(PAY, t, 512, 4), sl(PAY, t, 512, 4), nka, mul)
+            for i in range(16):
+                ts(sl(BP, 32 * i, 32 * i + 32), sl(PAY, i, 512, 16), -1.0, add)
+            dma([(pp(sl(WB, 512 * i, 512 * i + 512), R8), sl(BP, 32 * i, 32 * i + 32)) for i in range(16)], lat=5000.0)
         tt(CT, ind(QT, clT), sl(RI, 0, 768), le)
-        mm(dg(ps(6, 256, 304), CRT, Z, True, False) + dg(ps(6, 256, 304), CT, Z, False, True))
+        last = mm(dg(ps(6, 256, 304), CRT, Z, True, False))
+        mm(dg(ps(6, 256, 304), CT, Z, False, True), after=last)
         mm([x_ for a, b in ((0, 512), (512, 768)) for x_ in
             ((ps(0, a, b), BO, sl(CRT, a, b), True, False), (ps(0, a, b), BO, sl(CT, a, b), False, True))])
         ts(sl(DB, 0, 768), ps(0, 0, 768), -512.0 + one, add)
@@ -684,13 +806,19 @@ def build():
         ts(si, ps(6, 256, 304), -512.0, add)
         o = lin(si, POSW if fin else POSA, 6)
         cn = F(8)
-        nT, nG, nl, mc, r0 = [sl(cn, k, k + 1) for k in range(5)]
+        nT, nG, nl, mc, r0, lim, l2 = [sl(cn, k, k + 1) for k in range(7)]
         ts(nT, sl(CB[0]["CU"], 512, 513), 768.0, mn)
         cp(nG, sl(CB[1]["CU"], 576, 577))
         cp(nl, sl(CB[1]["CU"], 56, 57))
         tt(mc, nT, nG, mn)
         tt(r0, mc, nl, mx)
-        vA, pa, pau, D48 = F(48), F(48), U(48), sl(DUM, 0, 48)
+        ts(l2, sl(cs8, 8, 9), 32.0, mn, r0, add)
+        tt(lim, l2, nG, mn)
+        rr, rru = F(2), U(2)
+        ts(rr, sl(NI, 0, 2), r0, add)
+        cp(rru, rr)
+        cp(ind(DB, rru), nlv)
+        vA, pa, pau, D48, D58 = F(48), F(48), U(48), sl(DUM, 0, 48), sl(DUM, 0, 58)
         tt(pa, o, D48, sub)
         ts(vA, sl(NI, 0, 48), mc, lt)
         tt(pa, pa, vA, mul)
@@ -698,8 +826,9 @@ def build():
         cp(pau, pa)
         tt(CG, ind(QG, clG), sl(RI, 0, 928), le)
         o = ps(7, 256, 314)
-        mm(dg(o, CRG, Z, True, False) + dg(o, CG, Z, False, True))
-        j1, ui, uf, isl, lv = F(58), I(58), F(64), F(48), F(48)
+        last = mm(dg(o, CRG, Z, True, False))
+        mm(dg(o, CG, Z, False, True), after=last)
+        j1, ui, isl, lv = F(58), I(58), F(48), F(48)
         o48 = ps(7, 256, 304)
         ts(j1, o, -1408.0, add, Kc, mul)
         ts(isl, o48, 1408.0, lt)
@@ -711,11 +840,13 @@ def build():
         tt(lv, lv, isl, mul)
         tt(gv, lv, u48, mx)
         if not fin:
-            gi, gu, pv, pvu, XG = I(48), U(48), F(48), U(48), sl(MK, 0, 768)
+            gi, gf, gu, pv, pvu, XG = I(48), F(48), U(48), F(48), U(48), sl(SB, 0, 768)
             cp(gi, gv)
             ts(gi, gi, 2, shr)
-            cp(gu, gi)
-            cp(XG, ind(X[1], gu))
+            ts(gf, isl, 2064.0, mul, 16.0, add)
+            tt(gf, gf, gi, add)
+            cp(gu, gf)
+            cp(XG, ind(XP, gu))
             o = lin(si, [(0, 3, 2048), (2, 2047, 1)], 6)
             tt(pv, o, D48, sub)
             tt(pv, pv, vA, mul)
@@ -724,30 +855,39 @@ def build():
             cp(ind(Dd, pvu), XG)
             for q, bank in enumerate((0, 1, 4, 5)):
                 a = 512 * q
-                mm([(ps(bank, 0, 512), ID, sl(X[1], a, a + 512), True, False)]
-                   + [(ps(bank, 0, 512), ID, sl(Dd, 2048 * j + a, 2048 * j + a + 512), False, j == 3) for j in range(4)])
-                cp(sl(X[0], a, a + 512), ps(bank, 0, 512))
+                last = mm([(ps(bank, 0, 512), ID, sl(Y3, a, a + 512), True, False)])
+                mm([(ps(bank, 0, 512), ID, sl(Dd, 2048 * j + a, 2048 * j + a + 512), False, j == 3) for j in range(4)], after=last)
+                cp(sl(XV[0], a, a + 512), ps(bank, 0, 512))
             gv0, gv = gv, F(48)
-            ts(gv, gv0, -1.0, mul, 11776.0, add)
+            ts(gv, gv0, 33.0, add)
         cp(gh, gv)
         tt(gl, gv, gh, sub)
         for bk, (a, b) in enumerate(((0, 32), (32, 48))):
             mm([(ps(2 + bk, i, 16 * (b - a), 16), sl(EI, 128 * i, 128 * i + 128), sl(s_, a, b), s_ is gh, s_ is gl) for i in range(16) for s_ in (gh, gl)])
             cp(sl(DA, 16 * a, 16 * b), ps(2 + bk, 0, 16 * (b - a)))
-            cp(ind(WA, sl(pau, a, b)), sl(DA, 16 * a, 16 * b))
+            cp(ind(WA, sl(pau, a, b)), sl(DA, 16 * a, 16 * b), not fin)
         if fin:
             dma([(dr("yd", 0, 512), pp(sl(WA, 0, 8192), R8))])
         else:
             dma([(TA, pp(sl(WA, 0, 8192), R8))])
-        PB_ = POSW if fin else POSB
-        pb, pbu, vb = F(50), U(50), F(50)
-        o = lin(u48, PB_, 7)
-        tt(sl(pb, 0, 48), o, D48, sub)
-        ts(sl(vb, 0, 48), isl, -1.0, mul, 1.0, add)
-        tt(sl(vb, 0, 48), sl(vb, 0, 48), vA, mul)
+        pb, pbu, vb, v2 = F(58), U(58), F(58), F(58)
+        ts(vb, sl(NI, 0, 58), nl, ge)
+        ts(v2, sl(NI, 0, 58), lim, lt)
+        tt(vb, vb, v2, mul)
+        tt(pb, lin(ui, POSW, 7) if fin else ui, D58, sub)
+        tt(pb, pb, vb, mul)
+        tt(pb, pb, D58, add)
+        cp(pbu, pb)
+        for a, b in ((0, 30), (30, 58)):
+            cp(ind(sl(WB, 0, 9120), sl(pbu, a, b)), sl(DB, 16 * a, 16 * b), not fin)
+        if fin:
+            dma([(dr("ya", 0, 512), pp(sl(WB, 0, 8192), R8))])
+            for a in TOP:
+                TOP[a] = max(TOP[a], high[a])
+            continue
+        dma([(BP, pp(sl(WB, 0, 8192), R8))])
+        uf, ra, rc, rp, mk, rw, RR, uci = F(64), I(2), U(2), U(2), F(32), F(32), F(32), I(2)
         cp(sl(uf, 0, 58), ui)
-        rr, ra, rc, rp, mk, rw, RR, uc, uci, v2 = F(2), I(2), U(2), U(2), F(32), F(32), F(32), F(2), I(2), F(2)
-        ts(rr, sl(NI, 0, 2), r0, add)
         cp(ra, rr)
         ts(uci, ra, 4, shr)
         cp(rc, uci)
@@ -757,28 +897,7 @@ def build():
         tt(rw, ind(sl(uf, 0, 58), rc), mk, mul)
         mm([(ps(6, 64, 96), BOf, rw, True, True)])
         cp(RR, ps(6, 64, 96))
-        tt(rw, RR, MK32, mul)
-        red(sl(uc, 0, 1), sl(rw, 0, 16))
-        red(sl(uc, 1, 2), sl(rw, 16, 32))
-        cp(uci, uc)
-        o = lin(uci, PB_, 6)
-        tt(sl(pb, 48, 50), o, sl(DUM, 48, 50), sub)
-        ts(v2, rr, nG, lt)
-        ts(sl(vb, 48, 50), sl(NI, 0, 2), sl(cs8, 8, 9), lt)
-        tt(sl(vb, 48, 50), sl(vb, 48, 50), v2, mul)
-        for a, b in ((0, 48), (48, 50)):
-            tt(sl(pb, a, b), sl(pb, a, b), sl(vb, a, b), mul)
-            tt(sl(pb, a, b), sl(pb, a, b), sl(DUM, a, b), add)
-            cp(sl(pbu, a, b), sl(pb, a, b))
-        for a, b in ((0, 24), (24, 48), (48, 50)):
-            cp(ind(WB, sl(pbu, a, b)), sl(DB, 16 * a, 16 * b))
-        if fin:
-            dma([(dr("ya", 0, 512), pp(sl(WB, 0, 8192), R8))])
-            for a in TOP:
-                TOP[a] = max(TOP[a], high[a])
-            continue
-        dma([(BP, pp(sl(WB, 0, 8192), R8))])
-        v, w, wu, row = F(56), F(56), U(56), sl(WA, 8192, 9088)
+        v, w, wu, row = F(56), F(56), U(56), MKE
         ts(v, sl(QG, 0, 56), mc, le)
         tt(v, v, sl(FG, 0, 56), mul)
         ts(w, sl(QG, 0, 56), -1.0, add)
@@ -786,7 +905,8 @@ def build():
         cp(wu, w)
         cp(row, ind(sl(DB, 0, 768), wu))
         mm(dg(ps(7, 64, 120), row, Z0f))
-        tt(w, ps(7, 64, 120), v, mul)
+        ts(w, ps(7, 64, 120), -32.0, add)
+        tt(w, w, v, mul)
         tt(IT, IT, aI, mul)
         ts(v, go, -1.0, mul, 1.0, add)
         tt(IT, IT, v, mul)
@@ -807,85 +927,112 @@ def build():
         tt(sl(OT, z0, z0 + 8), sl(OT, z0, z0 + 8), w8, add)
 
 
-def schedule(noise):
+def after_pos(lst, t):
+    a, b = 0, len(lst)
+    while a < b:
+        m = (a + b) // 2
+        if lst[m] <= t:
+            a = m + 1
+        else:
+            b = m
+    return a
+
+
+def place(pr, pred, succ, back, bias):
     n = len(OPS)
-    suc = [[] for _ in range(n)]
-    for k, o in enumerate(OPS):
-        if "alt" in o:
-            o["cost"] = o["alt"]["a"][1]
-        for p in o["pre"]:
-            suc[p].append(k)
-    pr = [0.0] * n
-    for k in range(n - 1, -1, -1):
-        pr[k] = OPS[k]["cost"] + OPS[k]["lat"] + HOP + max([pr[s] for s in suc[k]] + [0.0])
-    pr = [a + b for a, b in zip(pr, noise)]
-    left = [len(o["pre"]) for o in OPS]
-    ready = [0.0] * n
-    free = {}
-    cand = [k for k in range(n) if left[k] == 0]
-    order = []
-    end = 0.0
-    while cand:
-        for k in cand:
-            o = OPS[k]
-            if "alt" in o:
-                e = {q: max(ready[k], free.get(q, 0.0)) + o["alt"][q][1] for q in "av"}
-                o["q"] = "a" if e["a"] <= e["v"] + BIAS else "v"
-                o["fn"], o["cost"] = o["alt"][o["q"]]
-        st = {k: max(ready[k], free.get(OPS[k]["q"], 0.0)) for k in cand}
-        k = min(cand, key=lambda x: (st[x], -pr[x]))
-        q = OPS[k]["q"]
-        while True:
-            bet = [x for x in cand if OPS[x]["q"] == q and pr[x] > pr[k] + LOOK and st[x] < st[k] + LOOKF * OPS[k]["cost"]]
-            if not bet:
-                break
-            k = min(bet, key=lambda x: (st[x], -pr[x]))
-        cand.remove(k)
-        o = OPS[k]
-        free[q] = st[k] + o["cost"]
-        fin = st[k] + o["cost"] + o["lat"] + HOP
-        o["t"] = st[k]
-        end = max(end, fin)
-        order.append(k)
-        for s in suc[k]:
-            ready[s] = max(ready[s], fin)
+    left = [len(p) for p in pred]
+    ready, st, qq, cc = [0.0] * n, [0.0] * n, [None] * n, [0.0] * n
+    busy = {q: ([], []) for q in "vapgsn"}
+    heap = sorted((pr[k], k) for k in range(n) if left[k] == 0)
+    while heap:
+        k = heap.pop()[1]
+        best = None
+        for q, c in ALT[k]:
+            S, E = busy[q]
+            t = ready[k] + (LAT[k] if back else 0.0)
+            m = len(S)
+            i = m if m == 0 or E[-1] <= t else after_pos(E, t)
+            while i < m and S[i] < t + c:
+                t = E[i]
+                i += 1
+            v = t + c + (bias[k] if q == "v" else 0.0)
+            if best is None or v < best[0]:
+                best = (v, q, c, t, i)
+        v, q, c, t, i = best
+        S, E = busy[q]
+        S.insert(i, t)
+        E.insert(i, t + c)
+        st[k], qq[k], cc[k] = t, q, c
+        f = t + c + (0.0 if back else LAT[k])
+        for s in succ[k]:
+            if f > ready[s]:
+                ready[s] = f
             left[s] -= 1
             if left[s] == 0:
-                cand.append(s)
+                heap.insert(after_pos(heap, (pr[s], s)), (pr[s], s))
+    end = max(st[k] + cc[k] + (0.0 if back else LAT[k]) for k in range(n))
+    return end, st, qq, cc
+
+
+def search(rounds):
+    n = len(OPS)
+    for o in OPS:
+        ALT.append([(q, o["alt"][q][1]) for q in "av"] if "alt" in o else [(o["q"], o["cost"])])
+        LAT.append(o["lat"] + HOP)
+    pred = [sorted(o["pre"]) for o in OPS]
+    succ = [[] for _ in range(n)]
+    for k in range(n):
+        for p in pred[k]:
+            succ[p].append(k)
+    pr = [0.0] * n
+    for k in range(n - 1, -1, -1):
+        pr[k] = ALT[k][0][1] + LAT[k] + max([pr[s] for s in succ[k]] + [0.0])
+    x = [SEED]
+
+    def rnd(m):
+        x[0] = (x[0] * 1103515245 + 12345) % 2147483648
+        return (x[0] >> 8) % m
+
+    def tryit(p, bias):
+        e, st, qq, cc = place(p, pred, succ, False, bias)
+        b = place([st[k] + cc[k] + LAT[k] for k in range(n)], succ, pred, True, bias)
+        p2 = [b[1][k] + b[3][k] for k in range(n)]
+        r = place(p2, pred, succ, False, bias)
+        return (r, p2) if r[0] <= e else ((e, st, qq, cc), p)
+    bias = [BIAS] * n
+    best, bp = tryit(pr, bias)
+    for it in range(rounds):
+        p, nb = list(bp), list(bias)
+        for m in range(2):
+            a, w, d = rnd(n), 1 + rnd(12), rnd(6000) - 3000.0
+            for k in range(a, min(n, a + w)):
+                p[k] += d
+        a, w, d = rnd(n), 1 + rnd(20), (0.0, 300.0, 1000.0, 5000.0, -5000.0)[rnd(5)]
+        for k in range(a, min(n, a + w)):
+            nb[k] = d
+        r, p2 = tryit(p, nb)
+        if r[0] <= best[0]:
+            best, bp, bias = r, p2, nb
+    end, st, qq, cc = best
+    order = sorted(range(n), key=lambda k: (st[k], k))
     sems, cnt = ["cv", "ca", "cp", "cg"], {}
     for k in order:
         o = OPS[k]
+        if "alt" in o:
+            o["q"] = qq[k]
+            o["fn"], o["cost"] = o["alt"][qq[k]]
+        o["t"] = st[k]
         if o["kind"] == "c":
             cnt[o["q"]] = cnt.get(o["q"], 0) + 1
             o["sig"] = ("c" + o["q"], cnt[o["q"]])
         else:
             sems.append("%s%d" % (o["kind"][0], k))
             o["sig"] = (sems[-1], 16 * o["n"] if o["kind"] == "dma" else 2 * (N - 1))
-    snd = [o["t"] for o in OPS if o["kind"] == "send"]
-    return order, sems, end + 0.25 * (sum(snd) - snd[3]), end
-
-
-def search(rounds):
-    n, x = len(OPS), 1
-    best = [0.0] * n
-    plan = schedule(best)[2]
-    for it in range(rounds):
-        new = list(best)
-        for m in range(3):
-            x = (x * 1103515245 + 12345) % 2147483648
-            a = (x >> 8) % n
-            x = (x * 1103515245 + 12345) % 2147483648
-            d = ((x >> 8) % 10000) - 5000.0
-            for k in range(a, min(n, a + 1 + (x >> 4) % 12)):
-                new[k] += d
-        p = schedule(new)[2]
-        if p <= plan:
-            best, plan = new, p
-    return schedule(best)
+    return order, sems, end
 
 
 build()
-ORDER, SEMAPHORES, _SCORE, PLAN = search(ROUNDS)
+ORDER, SEMAPHORES, PLAN = search(ROUNDS)
 SCRATCH = {k: ("sbuf", [128, TOP[k]], DTY[k]) for k in DTY}
 for _k in range(4):
     SCRATCH["p%d" % _k] = ("psum", [128, 1024], "float32")

@@ -7,9 +7,10 @@ DTY = {"af": "float32", "ab": "bfloat16", "ai": "int32", "au": "uint16", "ah": "
 SZ = {"float32": 4, "bfloat16": 2, "int32": 4, "uint16": 2, "float16": 2}
 TOP = {k: 0 for k in DTY}
 OPS, ACC, EXPS, BANK, ALT, LAT = [], {}, [], {}, [], []
-GC, SC, PEC, HOP = 1.5, 3.5, 0.5, 90.0
-BIAS, SEED, ROUNDS = 300.0, 1, 3000
-ND, NPE, NC3 = [1024, 0, 0, 0, 0, 0], [0, 0, 0, 0, 0, 0], 3
+GC, SC, PEC, HOP = 1.45, 3.2, 0.62, 110.0
+OTHER = [{"c": 0.83, "g": 0.75, "s": 0.68, "p": 0.85, "x": 1.0, "w": 1.15}, {"c": 1.16, "g": 1.45, "s": 1.65, "p": 1.25, "x": 1.0, "w": 0.75}]
+BIAS, SEED, ROUNDS = 300.0, 1, 5000
+ND0, NC3 = 1024, 2
 
 
 def al(k, n):
@@ -80,7 +81,14 @@ def op(q, fn, reads, writes, cost, lat=0.0, kind="c", n=1, after=None):
             if w:
                 old = [x for x in old if not (r[1] <= x[1] and x[2] <= r[2] and r[3] == 1 and r[4] is None)]
             ACC[r[0]] = old + [(k, r[1], r[2], w)]
-    OPS.append({"q": q, "fn": fn, "pre": pre, "cost": cost, "lat": lat, "kind": kind, "n": n})
+    ty = "c" if kind == "c" else "x"
+    if q == "p":
+        ty = "p"
+    if reads and isref(reads[0]) and reads[0][0] == "ind":
+        ty = "g"
+    if writes and writes[0][0] == "ind":
+        ty = "s"
+    OPS.append({"q": q, "ty": ty, "fn": fn, "pre": pre, "cost": cost, "lat": lat, "kind": kind, "n": n})
     return k
 
 
@@ -203,16 +211,23 @@ def full(out, l, src, st=True, sp=True):
     return [(sl(out, a, min(a + 512, n)), l, sl(src, a, min(a + 512, n)), st, sp) for a in range(0, n, 512)]
 
 
-def dma(pairs, lat=2500.0, q="s"):
+def dma(pairs, q="s", after=None):
     def fn(g, T):
         e = g.sync if q == "s" else g.scalar
         return [e.dma_start(ap(T, o), ap(T, i)) for (o, i) in pairs]
-    return op(q, fn, [x[1] for x in pairs], [x[0] for x in pairs], 60.0 * len(pairs), lat=lat, kind="dma", n=len(pairs))
+    c = 0.0
+    for (o, i) in pairs:
+        s = o if o[0] in DTY else i
+        z = size(s)
+        by = z * wid(s) * (128 if s[4] is None else len(range(*s[4])))
+        row = min(z * wid(o), z * wid(i))
+        c += max(60.0, -(-by // row // 16) * (30.0 + row / 25.0))
+    return op(q, fn, [x[1] for x in pairs], [x[0] for x in pairs], c, lat=1500.0, kind="dma", n=len(pairs), after=after)
 
 
 def exch(src, dst, w):
-    k = op("g", (src, dst, w), [src], [], 300.0, lat=2500.0, kind="send")
-    op("n", None, [], [dst], 0.0, lat=1500.0 + 8 * w, kind="recv", after=k)
+    k = op("g", (src, dst, w), [src], [], 300.0, lat=900.0, kind="send")
+    op("s", None, [], [dst], 64 * (20.0 + w / 6.0), lat=600.0, kind="recv", after=k)
 
 
 def build():
@@ -227,13 +242,13 @@ def build():
     X, Y3 = [B(2960), sl(XP, 2064, 5024)], sl(XP, 16, 2064)
     XV, XL = [sl(x, 16, 2064) for x in X], [sl(x, 2064, 2960) for x in X]
     WA, WB = F(10240), F(10592)
-    dma([(axw, dr("axo", 0, 512))])
-    dma([(dew, dr("den", 0, 512))], q="a")
-    dma([(pp(sl(pari, 0, 6), (i, 128, 16)), dr("par", 0, 6)) for i in range(16)], q="a", lat=3000.0)
     Dd, Ab = B(8192 + 896), B(2048)
-    dma([(XV[0], dr("x0", 0, 2048))], lat=3500.0)
-    dma([(sl(Y3, 0, ND[0]), dr("x0", 0, ND[0]))], lat=3500.0)
-    dma([(sl(axB, 32 * i, 32 * i + 32), dr("axo", 0, 512, (i, 128, 16))) for i in range(16)], lat=5000.0)
+    dma([(axw, dr("axo", 0, 512))])
+    k = dma([(pp(sl(pari, 0, 6), (i, 128, 16)), dr("par", 0, 6)) for i in range(16)], q="a")
+    dma([(dew, dr("den", 0, 512))], after=k)
+    k = dma([(XV[0], dr("x0", 0, 2048))], after=k)
+    dma([(sl(Y3, 0, ND0), dr("x0", 0, ND0))], after=k)
+    dma([(sl(axB, 32 * i, 32 * i + 32), dr("axo", 0, 512, (i, 128, 16))) for i in range(16)], after=k)
     PAY, HELD, RAW = F(512), F(512), F(512)
     ci, cf = I(32), F(48)
     col = lambda k: sl(cf, k, k + 1)
@@ -254,13 +269,14 @@ def build():
     ts(z15, gb, 15.0, add)
     ts(d0c, pi, 0.0, eq)
     ts(d1c, pi, 1.0, eq)
-    BO, TRI, TRH, BOP, BOm, DLO, up = B(128), B(128), B(128), B(128), B(128), B(128), sl(Dd, 512, 640)
+    BO, TRI, TRH, BOP, BOm, DLO, SH, up = B(128), B(128), B(128), B(128), B(128), B(128), B(128), sl(Dd, 512, 640)
     ID, IDf, O17, ONES, CJ = B(128), F(128), B(128), B(512), B(512)
     ms(ONES, 1.0)
     asel(up, sl(ONES, 0, 128), [[-16, 8], [0, 16]], ge, 0, 1)
     asel(BO, up, [[16, 8], [0, 16]], ge, 15, -1)
     asel(TRI, BO, [[1, 128]], ge, 0, -1)
-    Z, Z4, ZP, Z0, Z1, Z32, ZI4, Zq, Z0n = [B(144) for k in range(9)]
+    asel(SH, BO, [[-1, 128]], eq, -1, 1)
+    Z, Z4, ZP, Z0, Z1, Z32, ZI4, Z0n = [B(144) for k in range(8)]
     Z0f, BOf = F(144), F(128)
     ts(Z, R144, z15, eq)
     ts(Z0, Z, d0c, mul)
@@ -269,7 +285,6 @@ def build():
     cp(Z0f, Z0)
     ts(Z4, Z, 4.0, mul)
     ts(Z32, Z, 32.0, mul)
-    ts(Zq, Z, 0.25, mul)
     p2, p2f = B(1), F(1)
     act(p2, pi, Fn.Exp, scale=math.log(2.0))
     cp(p2f, p2)
@@ -282,7 +297,7 @@ def build():
     iota(O17, [[0, 128]], 17, 0)
     iota(CJ, [[-1, 4], [0, 128]], 4, 0)
     WM = {1: ID}
-    for w in (507904, -0.5, -1, 4, 5, 16, 128, 512, 2048) + ((3,) if NC3 > 4 else ()):
+    for w in (507904, -0.5, -1, 4, 5, 16, 128, 512):
         WM[w] = B(128)
         ts(WM[w], ID, float(w), mul)
     tt(TRH, TRI, WM[-0.5], sub)
@@ -292,7 +307,6 @@ def build():
     EI = B(2048)
     for i in range(4):
         asel(sl(EI, 512 * i, 512 * i + 512), ONES, [[-1, 4], [-16, 8], [0, 16]], eq, -4 * i, 1)
-    TM, TO = B(2048), B(512)
     ts(cin(2), cin(0), 3, band)
     ts(cin(3), cin(0), 2, shr, 3, band)
     cp(col(15), cin(3))
@@ -310,27 +324,27 @@ def build():
         ts(sl(ZQ, 144 * j, 144 * j + 144), zq, col(40 + j), mul)
         ts(sl(ZB, 144 * j, 144 * j + 144), zb, col(36 + j), mul)
     cp(ZBb, ZB)
-    for a in range(4):
-        ts(sl(TO, 128 * a, 128 * a + 128), BO, col(36 + a), mul)
-        for j in range(4):
-            c = 128 * (4 * a + j)
-            asel(sl(TM, c, c + 128), sl(TO, 128 * a, 128 * a + 128), [[64, 8], [1, 16]], ge, 16 * a - j, -4)
     DUM, LB32, ZR, DUC, CAPS, d9, d9r = F(128), U(32), F(928), F(36), B(576), F(56), F(56)
     DUL = sl(DUM, 0, 56)
     ts(DUM, sl(NI, 0, 128), 8192.0, add)
     ts(DUC, sl(NI, 0, 36), float(CAP), add)
     ts(d9, sl(NI, 0, 56), 912.0, add)
     ts(d9r, sl(NI, 0, 56), -112.0, add)
-    ms(ZR, 0.0)
+    iota(ZR, [[0, 928]], 0, 0)
     ms(CAPS, float(CAP))
-    ti = I(32)
-    cp(ti, sl(NI, 0, 32))
-    ts(ti, ti, 31, band)
-    cp(LB32, ti)
     PR = F(8)
     cp(sl(PR, 0, 6), sl(pari, 0, 6))
     lo, th, hi, Kc = [sl(PR, k, k + 1) for k in range(4)]
     ts(col(16), lo, 16.0, mul)
+    ti, tj, tf = I(32), I(32), F(32)
+    cp(ti, sl(NI, 0, 32))
+    ts(tj, ti, 5, shr)
+    ts(ti, ti, 31, band)
+    ts(tj, tj, Kc, mul)
+    ts(tj, tj, 15, band)
+    ts(tf, tj, 32.0, mul)
+    tt(tf, tf, ti, add)
+    cp(LB32, tf)
     ts(DLO, ID, col(16), mul)
     ms(sl(X[0], 0, 16), 0.0)
     ms(sl(X[1], 0, 16), 16.0)
@@ -351,8 +365,7 @@ def build():
     cp(sl(cf, 13, 15), sl(ci, 14, 16))
     kl, kh = col(13), col(14)
     rot = [0]
-    LI01 = I(768)
-    LI, LH = [sl(LI01, 0, 384), sl(LI01, 384, 768), I(896)], [H(384), H(384), H(896)]
+    LI, LH = [I(384), I(384)], [H(384), H(384), H(896)]
 
     def lin(xi, fields, bank):
         n = wid(xi)
@@ -364,6 +377,16 @@ def build():
         cp(sl(b, 0, n * len(fields)), sl(a, 0, n * len(fields)))
         mm([(out, WM[w], sl(b, k * n, k * n + n), k == 0, k == len(fields) - 1) for k, (s, m, w) in enumerate(fields)])
         return out
+
+    def place2(xi, f1, f2, inv, out):
+        n = wid(xi)
+        a, b, c = I(n), I(n), F(n)
+        ts(a, xi, f1[0], shr, f1[1], band)
+        ts(b, xi, f2[0], shr, f2[1], band)
+        ts(c, a, float(f1[2]), mul)
+        tt(c, c, b, add)
+        tt(c, c, inv, mx)
+        cp(out, c)
     POSA = [(2, 15, 512), (0, 3, 128), (6, 127, 1)]
     POSW = [(0, 15, 512), (4, 511, 1)]
 
@@ -374,45 +397,48 @@ def build():
         for a in range(4):
             last = mm([(ps(7, 128 * j, 128 * j + 128), sl(ZQ, 144 * j + 12 - 4 * a, 144 * j + 140 - 4 * a), sl(t1, a, 512, 4), a == 0, a == 3)], after=last)
     ts(TA, ps(7, 0, 512), 1.0, add)
-    LW, TAB = [U(32), U(32)], [B(512), B(512)]
-    lsi, tbi = I(512), sl(LI01, 0, 512)
+    LW, TAB = [U(32), U(32)], [B(96), B(96)]
+    lsi = I(512)
     for t in range(2):
         Ct = sl(PR, 4 + t, 5 + t)
-        a = I(32)
+        a, b, c = I(32), I(32), F(32)
         ts(a, sl(NI, 0, 32), Kc, mul, Ct, add)
+        ts(b, a, 9, shr, 15, band)
         ts(a, a, 511, band)
         cp(LW[t], a)
-        ts(tbi, NI, Kc, mul, Ct, add)
-        ts(tbi, tbi, 9, shr, 15, band)
-        cp(HELD, tbi)
-        act(TAB[t], HELD, Fn.Exp, scale=-math.log(2.0))
+        cp(c, b)
+        act(sl(TAB[t], 0, 32), c, Fn.Exp, scale=-math.log(2.0))
+        act(sl(TAB[t], 32, 64), c, Fn.Exp, scale=math.log(2.0))
+        ts(sl(TAB[t], 64, 96), sl(TAB[t], 0, 32), 65536.0, mul)
 
     CB = []
     for k in range(2):
         CB.append({"CU": H(592), "Q": F(576) if k else sl(WA, 9696, 10240), "SW": sl(WB, 9088, 10592) if k else sl(WA, 8192, 9696), "CR": H(928),
-                   "cl": U(64), "li": U(48), "st": F(48), "em": F(48)})
-        ms(sl(CB[k]["CU"], 0, 1), 0.0)
+                   "cl": U(64), "li": U(48), "st": H(48), "em": F(48), "cb": F(64)})
+        ms(CB[k]["CU"], 0.0)
 
-    def comp(k, NC, R, Pp, Tp, sb, silu=True, off=0.0):
+    def comp(k, NC, R, Pp, Tp, sb, w, base):
         c = CB[k]
         CU, Q, SW, CR, A = c["CU"], sl(c["Q"], 0, NC), c["SW"], sl(c["CR"], 0, R), NC // 16
-        dma([(sl(SW, 0, R), sl(ZR, 0, R))])
+        iota(sl(SW, 0, R), [[0, R]], 0, 0)
         scan(sl(CU, 1, NC + 1), Tp, sl(CAPS, 0, NC), 0.0, add, mn)
-        mm(dg(ps(sb, 0, A), sl(CU, 0, NC), Z0) + dg(ps(sb, 64, 64 + A), sl(CU, 1, NC + 1), Z0))
+        mm(dg(ps(sb, 0, A + 1), sl(CU, 0, NC + 16), Z0))
         st, em, li = sl(c["st"], 0, A), sl(c["em"], 0, A), sl(c["li"], 0, A)
-        cp(st, ps(sb, 0, A))
+        cp(sl(c["st"], 0, A + 1), ps(sb, 0, A + 1))
+        mm([(ps(sb, 64, 64 + A), SH, st, True, False), (ps(sb, 64, 64 + A), sl(Z0, 0, 128), sl(c["st"], 1, A + 1), False, True)])
         tt(em, ps(sb, 64, 64 + A), st, le)
         tt(em, em, sl(DUC, 0, A), mul)
         tt(em, em, st, mx)
         cp(li, em)
         mm(full(Pp, ID, sl(CU, 0, NC), False, True))
-        ts(Q, Pp, off, add)
-        cp(ind(sl(SW, 0, CAP + NC), li), sl(RI, 32, 32 + NC), silu)
+        cp(Q, Pp)
+        cp(ind(sl(SW, 0, CAP + NC), li), sl(RI, 32, 32 + NC), True)
         scan(CR, sl(SW, 0, R), sl(SW, 0, R), 32.0, mx, mx)
-        cl = sl(c["cl"], 0, R // 16)
+        cl, cb = sl(c["cl"], 0, R // 16), sl(c["cb"], 0, R // 16)
         mm(dg(ps(sb, 128, 128 + R // 16), CR, Z0))
         ts(cl, ps(sb, 128, 128 + R // 16), -32.0, add)
-        return Q, CR, cl
+        ts(cb, ps(sb, 128, 128 + R // 16), w, mul, base, add)
+        return Q, CR, cl, cb
 
     OT, IT = F(56), F(56)
     DB, DA = F(928), F(896)
@@ -428,9 +454,9 @@ def build():
         ts(Fl, tw, 8192.0, ge)
         mm([(ps(b0 + 1, 0, 512), BO, Fl, True, True)])
         mm([(ps(b0, 0, 512), TRH, Fl, True, False), (ps(b0, 0, 512), WM[-0.5], ONES, False, 2)])
-        dma([(sl(IW, 0, 912), sl(ZR, 0, 912))])
+        iota(sl(IW, 0, 912), [[0, 912]], 0, 0)
         ts(VAL, tw, 0.25, mul, -2032.0, add)
-        Q, CR, cl = comp(k, 512, 896, ps(b0, 0, 512), ps(b0 + 1, 0, 512), b0 + 2, k == 1)
+        Q, CR, cl, cb = comp(k, 512, 896, ps(b0, 0, 512), ps(b0 + 1, 0, 512), b0 + 2, 4.0, -128.0)
         tt(OH, ind(Q, cl), sl(RI, 1, 897), eq)
         tt(EV, ind(VAL, cl), OH, mul)
         o = ps(b0 + 3, 0, 56)
@@ -452,9 +478,9 @@ def build():
         cp(li, z)
         if k == 0:
             o2, nl0 = ps(2, 256, 312), U(56)
-            last = mm(dg(o2, CR, Zq, True, False))
-            mm(dg(o2, OH, ZI4, False, True), after=last)
-            ts(nl0, o2, -128.0, add)
+            mm(dg(o2, OH, ZI4))
+            tt(cb, o2, cb, add)
+            cp(nl0, cb)
             cp(SB, ind(XV[0], nl0))
             ms(sl(Qb, 16, 912), 0.0)
             cp(ind(sl(Qb, 0, 1808), li), SB)
@@ -476,8 +502,6 @@ def build():
     dma([(pp(sl(WA, 0, 8192), R8), sl(ZR, 0, 512))])
     dma([(pp(sl(WB, 0, 8192), R8), BP)])
 
-    ACCf, ACCi = DA, LI[2]
-
     def send_x(k):
         cp(sl(SB, 0, 448), ind(XV[k % 2], sl(LO, 0, 28)))
         cp(sl(SB, 448, 896), ind(XV[k % 2], sl(LO, 28, 56)))
@@ -485,17 +509,13 @@ def build():
 
     def lst(j, a, b): return sl(LS, 128 * j + a // 16, 128 * j + b // 16)
 
-    def rem16(y, o, q, pe):
+    def rem16(y, o, q):
         ts(q, o, -7.5, add)
-        if pe:
-            mm([(o, WM[-1], q, False, True)])
-            cp(y, o)
-        else:
-            tt(y, o, q, sub)
+        tt(y, o, q, sub)
 
     def step(k, mod):
         w, x, y = X[k % 2], XV[k % 2], XV[(k + 1) % 2]
-        nd = ND[k]
+        nd = 0 if mod else ND0
         for bank, a in enumerate(range(nd, 2048, 512)):
             b = min(a + 512, 2048)
             o = ps(bank, 0, b - a)
@@ -503,9 +523,9 @@ def build():
             for j in range(4):
                 v = sl(Dd, 2048 * j + a, 2048 * j + b)
                 cp(v, ind(w, lst(j, a, b)))
-                last = mm([(o, ID, v, False, (j == 3) * (2 if mod and bank < NPE[k] else 1))], after=last)
+                last = mm([(o, ID, v, False, j == 3)], after=last)
             if mod:
-                rem16(sl(y, a, b), o, sl(Qb, a, b), bank < NPE[k])
+                rem16(sl(y, a, b), o, sl(Qb, a, b))
                 dma([(sl(Qb, a, b), sl(y, a, b))])
             else:
                 cp(sl(y, a, b), o)
@@ -515,11 +535,11 @@ def build():
                 acc = sl(Qb, a, a + h)
                 tt(acc if j < 3 else sl(y, a, a + h), ind(w, lst(j, a, a + h)), acc if j else sl(Y3, a, a + h), add)
 
-    CP3 = [(0, 0, 0), (1, 0, 0), (0, 0, 1), (1, 0, 1), (0, 1, 0), (1, 1, 0), (0, 1, 1), (1, 1, 1)][:NC3]
+    CP3 = [(0, 0, 0), (1, 0, 0), (0, 0, 1), (1, 0, 1)][:NC3]
     MKE, LK, LM, LO3 = F(896), U(56), U(56), U(56)
     NK, FT, G1, CT, CG, cmpf = sl(Ab, 0, 512), sl(Ab, 512, 1024), sl(Ab, 1024, 1536), sl(Qb, 0, 768), sl(Qb, 768, 1696), sl(Ab, 1536, 1792)
     VAC, FLk = sl(Ab, 0, 512), sl(Qb, 0, 896)
-    FG, Y1, Y1i, Wc = B(576), t1, axw, F(32)
+    FG, Y1i, Wc = B(576), axw, F(32)
     ms(sl(FG, 568, 576), 0.0)
     mark, high = dict(TOP), dict(TOP)
 
@@ -627,12 +647,12 @@ def build():
                     else:
                         tt(d, ind(w, lst(j, a, a + 512)), sl(Qb, a, a + 512), sub)
                         act(sl(ab, 512 * i, 512 * i + 512), d, Fn.Abs)
-                    lx[i] = mm([(ps(2 * hf + i, 0, 512), ID, d, False, (j == 3) * (2 if 2 * hf + i < NPE[k0 + 2] else 1))], after=lx[i])
+                    lx[i] = mm([(ps(2 * hf + i, 0, 512), ID, d, False, j == 3)], after=lx[i])
                 c = 128 * j + 64 * hf
                 lf = mm(dg(ps(4, c, c + 64), ab, Z4, False, hf == 1 and j == 3), after=lf)
             for i in range(2):
                 a = 1024 * hf + 512 * i
-                rem16(sl(y, a, a + 512), ps(2 * hf + i, 0, 512), sl(Qb, a, a + 512), 2 * hf + i < NPE[k0 + 2])
+                rem16(sl(y, a, a + 512), ps(2 * hf + i, 0, 512), sl(Qb, a, a + 512))
             mm(dg(ps(5, 64 * hf, 64 * hf + 64), sl(y, 1024 * hf, 1024 * hf + 1024), Z))
             lsb = mm([(SBp, sl(Z, 15 - ii, 143 - ii), sl(y, 128 * ii, 128 * ii + 128), ii == 0, ii == 15) for ii in range(8 * hf, 8 * hf + 8)], after=lsb)
         if fin:
@@ -760,11 +780,18 @@ def build():
         tt(sl(FG, 0, 56), aI, nh, mul)
         act(G1, ind(BP, LW[t]), Fn.Sign, bias=0.5 if fin else 32.5, scale=-1.0)
         mm(dg(ps(6, 0, 32), G1, ZP))
+        W0, wv, wh, wr = F(32), F(32), I(32), I(32)
         ts(Wc, ps(6, 0, 32), 0.5, mul, 32768.0, add)
-        tt(Y1, ind(Wc, LB32), TAB[t], mul)
-        ts(Y1i, Y1, -0.5, add)
-        ts(Y1i, Y1i, 1, band)
-        cp(sl(FG, 56, 568), Y1i)
+        ts(W0, ps(6, 0, 32), 0.5, mul, 32767.5, add)
+        tt(wv, Wc, sl(TAB[t], 0, 32), mul)
+        ts(wh, wv, -0.5, add)
+        tt(wv, wh, sl(TAB[t], 32, 64), mul)
+        tt(wv, W0, wv, sub)
+        tt(wv, wv, sl(TAB[t], 64, 96), mul)
+        tt(wr, wv, wh, add)
+        for s in range(16):
+            ts(sl(Y1i, 32 * s, 32 * s + 32), wr, s, shr, 1, band)
+        cp(sl(FG, 56, 568), ind(Y1i, LB32))
         for bank, l in ((4, BO), (2, TRI)):
             mm([(ps(bank, 0, 512), l, sl(FG, 0, 512), True, False), (ps(bank, 56, 512), l, sl(LJ, 0, 456), False, 1 + (bank == 2)),
                 (ps(bank, 512, 576), l, sl(FG, 512, 576), True, False), (ps(bank, 512, 568), l, sl(LJ, 456, 512), False, 1 + (bank == 2))])
@@ -778,13 +805,12 @@ def build():
             tt(TA, FLp, TA, mn)
             dma([(pp(sl(WA, 0, 8192), R8), TA)])
         for a in range(4):
-            mm([(ps(1, a, 512, 4), sl(TO, 128 * a, 128 * a + 128), sl(FT, 128 * j, 128 * j + 128), j == 0, j == 3) for j in range(4)])
-        last = mm([(ps(0, 0, 512), WM[-0.5], ONES, True, False)])
-        for a in range(4):
-            last = mm([(ps(0, a, 512, 4), sl(TM, 128 * (4 * a + j), 128 * (4 * a + j) + 128), sl(FT, 128 * j, 128 * j + 128), False, 2 * (a + j == 6))
-                       for j in range(4)], after=last)
-        QG, CRG, clG = comp(1, 576, 928, ps(2, 0, 576), ps(4, 0, 576), 7)
-        QT, CRT, clT = comp(0, 512, 768, ps(0, 0, 512), ps(1, 0, 512), 6, True, 0.5)
+            mm([(ps(1, a, 512, 4), sl(ZBb, 144 * a + 3 - j, 144 * a + 131 - j), sl(FT, 128 * j, 128 * j + 128), j == 0, j == 3) for j in range(4)])
+        cp(G1, ps(1, 0, 512))
+        mm([(ps(1, 0, 512), BO, G1, True, True)])
+        mm([(ps(0, 0, 512), TRI, G1, True, 2)])
+        QG, CRG, clG, cbG = comp(1, 576, 928, ps(2, 0, 576), ps(4, 0, 576), 7, 16.0, -1408.0)
+        QT, CRT, clT, cbT = comp(0, 512, 768, ps(0, 0, 512), ps(1, 0, 512), 6, 16.0, -512.0)
         if fin:
             for a in range(4):
                 mm([(ps(4, a, 512, 4), sl(ZBb, 144 * a + 3 - j, 144 * a + 131 - j), sl(NK, 128 * j, 128 * j + 128), j == 0, j == 3) for j in range(4)])
@@ -795,16 +821,14 @@ def build():
             tt(sl(PAY, t, 512, 4), sl(PAY, t, 512, 4), nka, mul)
             for i in range(16):
                 ts(sl(BP, 32 * i, 32 * i + 32), sl(PAY, i, 512, 16), -1.0, add)
-            dma([(pp(sl(WB, 512 * i, 512 * i + 512), R8), sl(BP, 32 * i, 32 * i + 32)) for i in range(16)], lat=5000.0)
+            dma([(pp(sl(WB, 512 * i, 512 * i + 512), R8), sl(BP, 32 * i, 32 * i + 32)) for i in range(16)])
         tt(CT, ind(QT, clT), sl(RI, 0, 768), le)
-        last = mm(dg(ps(6, 256, 304), CRT, Z, True, False))
-        mm(dg(ps(6, 256, 304), CT, Z, False, True), after=last)
+        mm(dg(ps(6, 256, 304), CT, Z))
         mm([x_ for a, b in ((0, 512), (512, 768)) for x_ in
             ((ps(0, a, b), BO, sl(CRT, a, b), True, False), (ps(0, a, b), BO, sl(CT, a, b), False, True))])
         ts(sl(DB, 0, 768), ps(0, 0, 768), -512.0 + one, add)
         si = I(48)
-        ts(si, ps(6, 256, 304), -512.0, add)
-        o = lin(si, POSW if fin else POSA, 6)
+        tt(si, ps(6, 256, 304), cbT, add)
         cn = F(8)
         nT, nG, nl, mc, r0, lim, l2 = [sl(cn, k, k + 1) for k in range(7)]
         ts(nT, sl(CB[0]["CU"], 512, 513), 768.0, mn)
@@ -819,39 +843,36 @@ def build():
         cp(rru, rr)
         cp(ind(DB, rru), nlv)
         vA, pa, pau, D48, D58 = F(48), F(48), U(48), sl(DUM, 0, 48), sl(DUM, 0, 58)
-        tt(pa, o, D48, sub)
-        ts(vA, sl(NI, 0, 48), mc, lt)
-        tt(pa, pa, vA, mul)
-        tt(pa, pa, D48, add)
-        cp(pau, pa)
+        ts(vA, sl(NI, 0, 48), mc, ge)
+        tt(vA, vA, D48, mul)
+        if fin:
+            place2(si, POSW[0], POSW[1], vA, pau)
+        else:
+            tt(pa, lin(si, POSA, 6), vA, mx)
+            cp(pau, pa)
         tt(CG, ind(QG, clG), sl(RI, 0, 928), le)
         o = ps(7, 256, 314)
-        last = mm(dg(o, CRG, Z, True, False))
-        mm(dg(o, CG, Z, False, True), after=last)
-        j1, ui, isl, lv = F(58), I(58), F(48), F(48)
-        o48 = ps(7, 256, 304)
-        ts(j1, o, -1408.0, add, Kc, mul)
-        ts(isl, o48, 1408.0, lt)
-        ts(lv, o48, 4.0, mul, 6144.0, add)
-        ts(ui, j1, Ct, add)
-        ts(ui, ui, 8191, band)
+        mm(dg(o, CG, Z))
+        j1, u0, ui, isl, lv = F(58), I(58), I(58), F(48), F(48)
+        o48 = sl(j1, 0, 48)
+        tt(j1, o, cbG, add)
+        ts(u0, j1, Kc, mul, Ct, add)
+        ts(isl, o48, 0.0, lt)
+        ts(lv, o48, 4.0, mul, 11776.0, add)
+        ts(ui, u0, 8191, band)
         u48 = sl(ui, 0, 48)
         gv, gh, gl = F(48), H(48), H(48)
         tt(lv, lv, isl, mul)
         tt(gv, lv, u48, mx)
         if not fin:
-            gi, gf, gu, pv, pvu, XG = I(48), F(48), U(48), F(48), U(48), sl(SB, 0, 768)
+            gi, gf, gu, pvu, XG = I(48), F(48), U(48), U(48), sl(SB, 0, 768)
             cp(gi, gv)
             ts(gi, gi, 2, shr)
             ts(gf, isl, 2064.0, mul, 16.0, add)
             tt(gf, gf, gi, add)
             cp(gu, gf)
             cp(XG, ind(XP, gu))
-            o = lin(si, [(0, 3, 2048), (2, 2047, 1)], 6)
-            tt(pv, o, D48, sub)
-            tt(pv, pv, vA, mul)
-            tt(pv, pv, D48, add)
-            cp(pvu, pv)
+            place2(si, (0, 3, 2048), (2, 2047, 1), vA, pvu)
             cp(ind(Dd, pvu), XG)
             for q, bank in enumerate((0, 1, 4, 5)):
                 a = 512 * q
@@ -871,13 +892,15 @@ def build():
         else:
             dma([(TA, pp(sl(WA, 0, 8192), R8))])
         pb, pbu, vb, v2 = F(58), U(58), F(58), F(58)
-        ts(vb, sl(NI, 0, 58), nl, ge)
-        ts(v2, sl(NI, 0, 58), lim, lt)
-        tt(vb, vb, v2, mul)
-        tt(pb, lin(ui, POSW, 7) if fin else ui, D58, sub)
-        tt(pb, pb, vb, mul)
-        tt(pb, pb, D58, add)
-        cp(pbu, pb)
+        ts(vb, sl(NI, 0, 58), nl, lt)
+        ts(v2, sl(NI, 0, 58), lim, ge)
+        tt(vb, vb, v2, mx)
+        tt(vb, vb, D58, mul)
+        if fin:
+            place2(u0, POSW[0], POSW[1], vb, pbu)
+        else:
+            tt(pb, ui, vb, mx)
+            cp(pbu, pb)
         for a, b in ((0, 30), (30, 58)):
             cp(ind(sl(WB, 0, 9120), sl(pbu, a, b)), sl(DB, 16 * a, 16 * b), not fin)
         if fin:
@@ -911,7 +934,7 @@ def build():
         ts(v, go, -1.0, mul, 1.0, add)
         tt(IT, IT, v, mul)
         tt(IT, IT, w, add)
-        nn, v8, w8, w8u, r8 = F(1), F(8), F(8), U(8), F(128)
+        nn, v8, w8, w8u, r8, r8h, r8l = F(1), F(8), F(8), U(8), F(128), H(128), H(128)
         tt(nn, nG, r0, sub)
         ts(nn, nn, 32.0, mn)
         ts(v8, Qf, nn, le)
@@ -920,7 +943,9 @@ def build():
         tt(w8, w8, v8, mul)
         cp(w8u, w8)
         cp(r8, ind(RR, w8u))
-        mm(dg(ps(6, 128, 136), r8, Z0f))
+        cp(r8h, r8)
+        tt(r8l, r8, r8h, sub)
+        mm(dg(ps(6, 128, 136), r8h, Z0, True, False) + dg(ps(6, 128, 136), r8l, Z0, False, True))
         ts(w8, ps(6, 128, 136), 1.0, add)
         tt(w8, w8, v8, mul)
         tt(OT, OT, ng, mul)
@@ -988,6 +1013,7 @@ def search(rounds):
     for k in range(n - 1, -1, -1):
         pr[k] = ALT[k][0][1] + LAT[k] + max([pr[s] for s in succ[k]] + [0.0])
     x = [SEED]
+    ty = [o["ty"] for o in OPS]
 
     def rnd(m):
         x[0] = (x[0] * 1103515245 + 12345) % 2147483648
@@ -999,8 +1025,26 @@ def search(rounds):
         p2 = [b[1][k] + b[3][k] for k in range(n)]
         r = place(p2, pred, succ, False, bias)
         return (r, p2) if r[0] <= e else ((e, st, qq, cc), p)
+
+    def score(r):
+        st, qq, cc = r[1], r[2], r[3]
+        order = sorted(range(n), key=lambda k: st[k])
+        tot = r[0]
+        for m in OTHER:
+            free, fin = {q: 0.0 for q in "vapgsn"}, [0.0] * n
+            for k in order:
+                t = free[qq[k]]
+                for p in pred[k]:
+                    if fin[p] > t:
+                        t = fin[p]
+                t += cc[k] * m[ty[k]]
+                free[qq[k]] = t
+                fin[k] = t + LAT[k]
+            tot += max(fin) * m["w"]
+        return tot
     bias = [BIAS] * n
     best, bp = tryit(pr, bias)
+    bs = score(best)
     for it in range(rounds):
         p, nb = list(bp), list(bias)
         for m in range(2):
@@ -1011,13 +1055,19 @@ def search(rounds):
         for k in range(a, min(n, a + w)):
             nb[k] = d
         r, p2 = tryit(p, nb)
-        if r[0] <= best[0]:
-            best, bp, bias = r, p2, nb
+        if r[0] <= best[0] + 1500:
+            s = score(r)
+            if s <= bs:
+                best, bp, bias, bs = r, p2, nb, s
     end, st, qq, cc = best
     order = sorted(range(n), key=lambda k: (st[k], k))
-    sems, cnt = ["cv", "ca", "cp", "cg"], {}
+    sems, cnt, got = ["cv", "ca", "cp", "cg"], {}, None
     for k in order:
         o = OPS[k]
+        if o["kind"] == "recv":
+            got = k
+        elif o["kind"] == "dma" and got is not None:
+            o["pre"].add(got)
         if "alt" in o:
             o["q"] = qq[k]
             o["fn"], o["cost"] = o["alt"][qq[k]]

import math
from concourse.bass import DstId, RemoteDMATransfer
from concourse.mybir import AluOpType as Op, AxisListType, ActivationFunctionType as Fn

N = 8
DTY = {"af": "float32", "ab": "bfloat16", "ai": "int32", "au": "uint16", "ah": "float16"}
SZ = {"float32": 4, "bfloat16": 2, "int32": 4, "uint16": 2, "float16": 2}
TOP = {k: 0 for k in DTY}
OPS, ACC, EXPS, BANK, ALT, LAT = [], {}, [], {}, [], []
GC, SC, PEC, HOP = 1.45, 3.2, 0.62, 110.0
OTHER = [{"c": 0.83, "g": 0.75, "s": 0.68, "p": 0.85, "x": 1.0, "w": 1.15}, {"c": 1.16, "g": 1.45, "s": 1.65, "p": 1.25, "x": 1.0, "w": 0.75}]
BIAS, SEED, ROUNDS = 300.0, 1, 5000
ND0, NC3 = 1024, 2


def al(k, n):
    c = TOP[k]
    TOP[k] = c + (n + 15) // 16 * 16
    return (k, c, c + n, 1, None)


def F(n): return al("af", n)
def B(n): return al("ab", n)
def I(n): return al("ai", n)
def U(n): return al("au", n)
def H(n): return al("ah", n)
def sl(r, a, b, st=1): return (r[0], r[1] + a, r[1] + b, st, r[4])
def pp(r, p): return (r[0], r[1], r[2], r[3], p)
def ps(bank, a, b, st=1): return ("p%d" % (bank // 2), 512 * (bank % 2) + a, 512 * (bank % 2) + b, st, None)
def ind(w, o): return ("ind", w, o)
def dr(name, a, b, p=None): return (name, a, b, 1, p)
def isref(x): return isinstance(x, tuple)
def wid(r): return 16 * wid(r[2]) if r[0] == "ind" else len(range(r[1], r[2], r[3]))
def ispsum(r): return r[0][0] == "p" and r[0] != "par"
def size(r): return size(r[1]) if r[0] == "ind" else (4 if ispsum(r) else SZ[DTY[r[0]]])
def half(*rs): return 0.5 if all(size(r) == 2 for r in rs) else 1.0
def flt(*rs): return all(ispsum(r) or DTY[(r[1] if r[0] == "ind" else r)[0]] in ("float32", "bfloat16") for r in rs)


def ap(T, r):
    if not isref(r):
        return r
    if r[0] == "ind":
        return ap(T, r[1]).indirect(ap(T, r[2]))
    cs = slice(r[1], r[2]) if r[3] == 1 else slice(r[1], r[2], r[3])
    if r[4] is None:
        return T[r[0]][:, cs]
    p = r[4]
    return T[r[0]][(slice(p[0], p[1]) if p[2] == 1 else slice(p[0], p[1], p[2])), cs]


def op(q, fn, reads, writes, cost, lat=0.0, kind="c", n=1, after=None):
    k = len(OPS)
    rd, wr = [], []
    for r in reads:
        if isref(r):
            rd += [r[1], r[2]] if r[0] == "ind" else [r]
    for r in writes:
        if r[0] == "ind":
            wr.append(r[1])
            rd.append(r[2])
        else:
            wr.append(r)
    pre = set()
    for lst, w in ((rd, False), (wr, True)):
        for r in lst:
            psum = ispsum(r)
            for (o, a, b, ow) in ACC.get(r[0], []):
                hit = a < r[2] and r[1] < b and (w or ow)
                if psum and (OPS[o]["q"] != q or q == "x") and a // 512 <= (r[2] - 1) // 512 and r[1] // 512 <= (b - 1) // 512:
                    hit = True
                if hit:
                    pre.add(o)
    if kind == "recv":
        pre = set()
    if after is not None:
        pre.update(after if isinstance(after, list) else [after])
    for lst, w in ((rd, False), (wr, True)):
        for r in lst:
            old = ACC.get(r[0], [])
            if w:
                old = [x for x in old if not (r[1] <= x[1] and x[2] <= r[2] and r[3] == 1 and r[4] is None)]
            ACC[r[0]] = old + [(k, r[1], r[2], w)]
    ty = "c" if kind == "c" else "x"
    if q == "p":
        ty = "p"
    if reads and isref(reads[0]) and reads[0][0] == "ind":
        ty = "g"
    if writes and writes[0][0] == "ind":
        ty = "s"
    OPS.append({"q": q, "ty": ty, "fn": fn, "pre": pre, "cost": cost, "lat": lat, "kind": kind, "n": n})
    return k


def vcost(out, ins, base):
    n = wid(out)
    if out[0] == "ind":
        return 50 + SC * n
    if ins[0][0] == "ind":
        return 50 + GC * n
    return max(64, base * n)


def act(out, a, f=None, bias=None, scale=None, q="a"):
    def fn(g, T):
        kw = {}
        if bias is not None:
            kw["bias"] = ap(T, bias)
        if scale is not None:
            kw["scale"] = ap(T, scale)
        return g.scalar.activation(ap(T, out), ap(T, a), Fn.Identity if f is None else f, **kw)
    k = op(q, fn, [a, bias, scale], [out], vcost(out, [a], 1.0), after=list(EXPS) if f == Fn.Silu else None)
    if f == Fn.Exp:
        EXPS.append(k)
    return k


def either(fv, cv, out, a, bias, scale, f=None):
    k = act(out, a, f, bias, scale, q="x")
    OPS[k]["alt"] = {"a": (OPS[k]["fn"], OPS[k]["cost"]), "v": (fv, cv)}
    return k


def ts(out, a, s1, o0, s2=None, o1=None):
    def fn(g, T):
        if s2 is None:
            return g.vector.tensor_scalar(ap(T, out), ap(T, a), ap(T, s1), None, o0)
        return g.vector.tensor_scalar(ap(T, out), ap(T, a), ap(T, s1), ap(T, s2), o0, o1)
    c = vcost(out, [a], half(out, a))
    if flt(out, a):
        if s2 is None and o0 == Op.mult:
            return either(fn, c, out, a, None, s1)
        if s2 is None and o0 == Op.add:
            return either(fn, c, out, a, s1, None)
        if s2 is not None and o0 == Op.mult and o1 == Op.add:
            return either(fn, c, out, a, s2, s1)
        if s2 == 0.0 and o0 == Op.add and o1 == Op.max:
            return either(fn, c, out, a, s1, None, Fn.Relu)
        if s1 == 0.0 and o0 == Op.is_equal and o1 == Op.mult and not isref(s2):
            return either(fn, c, out, a, s2, -s2, Fn.Relu)
    return op("v", fn, [a, s1, s2], [out], c)


def tt(out, a, b, o):
    return op("v", lambda g, T: g.vector.tensor_tensor(ap(T, out), ap(T, a), ap(T, b), o), [a, b], [out],
              vcost(out, [a], 1.0 if ispsum(a) or ispsum(b) else 2.0))


def cp(out, a, silu=False):
    fn = lambda g, T: g.vector.tensor_copy(ap(T, out), ap(T, a))
    c = vcost(out, [a], half(out, a))
    if silu:
        return either(fn, c, out, a, None, None, Fn.Silu)
    if flt(out, a) and out[0] != "ind":
        return either(fn, c, out, a, None, None)
    return op("v", fn, [a], [out], c)


def ms(out, c):
    return op("v", lambda g, T: g.vector.memset(ap(T, out), c), [], [out], vcost(out, [out], half(out)))


def scan(out, d0, d1, init, o0, o1):
    return op("v", lambda g, T: g.vector.tensor_tensor_scan(ap(T, out), ap(T, d0), ap(T, d1), init, o0, o1), [d0, d1], [out],
              max(64, wid(out) * half(out, d0, d1)))


def iota(out, pat, base, cm):
    def fn(g, T):
        if out[0] == "ai":
            return g.iota(ap(T, out), pat, base, cm)
        return g.iota(ap(T, out), pat, base, cm, allow_small_or_imprecise_dtypes=True)
    return op("g", fn, [], [out], 130 + 2 * wid(out))


def asel(out, a, pat, cmp, base, cm):
    return op("g", lambda g, T: g.affine_select(ap(T, out), ap(T, a), pat, cmp, 0.0, base, cm), [a], [out], 170 + 2 * wid(out))


def mm(lst, after=None):
    def fn(g, T):
        for (o, l, r, st, sp) in lst:
            x = g.tensor.matmul(ap(T, o), ap(T, l), ap(T, r), st, sp == 1)
        return x
    c = sum(max(64, wid(x[2])) * (4 if size(x[2]) == 4 else 1) for x in lst) * PEC
    pre = [] if after is None else [after]
    k = len(OPS)
    for x in lst:
        b = BANK.setdefault((x[0][0], x[0][1] // 512), {"open": None, "close": None, "starts": []})
        if x[3]:
            assert b["open"] is None
            pre += [b["close"]] if b["close"] is not None else []
            b["open"] = k
            b["starts"].append(k)
        if x[4] == 1:
            if b["open"] != k:
                b["close"] = k
                OPS[b["open"]]["pre"].update(s for s in b["starts"] if s < b["open"])
            b["open"] = None
    return op("p", fn, [x[1] for x in lst] + [x[2] for x in lst] + [x[0] for x in lst if not x[3]], [x[0] for x in lst], c, lat=60,
              after=[p for p in pre if p != k])


def dg(out, src, z, st=True, sp=True):
    n = wid(src)
    return [(out, sl(z, 15 - b, 143 - b), sl(src, b, n, 16), st and b == 0, sp and b == 15) for b in range(16)]


def full(out, l, src, st=True, sp=True):
    n = wid(src)
    return [(sl(out, a, min(a + 512, n)), l, sl(src, a, min(a + 512, n)), st, sp) for a in range(0, n, 512)]


def dma(pairs, q="s", after=None):
    def fn(g, T):
        e = g.sync if q == "s" else g.scalar
        return [e.dma_start(ap(T, o), ap(T, i)) for (o, i) in pairs]
    c = 0.0
    for (o, i) in pairs:
        s = o if o[0] in DTY else i
        z = size(s)
        by = z * wid(s) * (128 if s[4] is None else len(range(*s[4])))
        row = min(z * wid(o), z * wid(i))
        c += max(60.0, -(-by // row // 16) * (30.0 + row / 25.0))
    return op(q, fn, [x[1] for x in pairs], [x[0] for x in pairs], c, lat=1500.0, kind="dma", n=len(pairs), after=after)


def exch(src, dst, w):
    k = op("g", (src, dst, w), [src], [], 300.0, lat=900.0, kind="send")
    op("s", None, [], [dst], 64 * (20.0 + w / 6.0), lat=600.0, kind="recv", after=k)


def build():
    add, sub, mul, mx, mn = Op.add, Op.subtract, Op.mult, Op.max, Op.min
    ge, gt, le, lt, eq, ne = Op.is_ge, Op.is_gt, Op.is_le, Op.is_lt, Op.is_equal, Op.not_equal
    shr, band = Op.arith_shift_right, Op.bitwise_and
    R8 = (0, 128, 16)
    CAP = 928
    NOL = 8193.0 / 16384
    axw, dew, axB, pari = I(512), I(512), I(512), I(8)
    XP, Qb = B(5024), B(2048)
    X, Y3 = [B(2960), sl(XP, 2064, 5024)], sl(XP, 16, 2064)
    XV, XL = [sl(x, 16, 2064) for x in X], [sl(x, 2064, 2960) for x in X]
    WA, WB = F(10240), F(10592)
    Dd, Ab = B(8192 + 896), B(2048)
    dma([(axw, dr("axo", 0, 512))])
    k = dma([(pp(sl(pari, 0, 6), (i, 128, 16)), dr("par", 0, 6)) for i in range(16)], q="a")
    dma([(dew, dr("den", 0, 512))], after=k)
    k = dma([(XV[0], dr("x0", 0, 2048))], after=k)
    dma([(sl(Y3, 0, ND0), dr("x0", 0, ND0))], after=k)
    dma([(sl(axB, 32 * i, 32 * i + 32), dr("axo", 0, 512, (i, 128, 16))) for i in range(16)], after=k)
    PAY, HELD, RAW = F(512), F(512), F(512)
    ci, cf = I(32), F(48)
    col = lambda k: sl(cf, k, k + 1)
    cin = lambda k: sl(ci, k, k + 1)
    pc, pi, gb, z15, d0c, d1c, fr = [col(k) for k in range(7)]
    iota(cin(0), [[0, 1]], 0, 1)
    RI, NI = F(1024), F(512)
    iota(sl(RI, 0, 160), [[1, 160]], 0, 0)
    cp(pc, cin(0))
    ts(cin(1), cin(0), 15, band)
    cp(pi, cin(1))
    tt(gb, pc, pi, sub)
    iota(NI, [[16, 512]], 0, 1)
    iota(sl(RI, 160, 1024), [[1, 864]], 160, 0)
    ts(col(11), gb, -1.0, mul)
    ts(NI, NI, col(11), add)
    R128, R144 = sl(RI, 0, 128), sl(RI, 0, 144)
    ts(z15, gb, 15.0, add)
    ts(d0c, pi, 0.0, eq)
    ts(d1c, pi, 1.0, eq)
    BO, TRI, TRH, BOP, BOm, DLO, SH, up = B(128), B(128), B(128), B(128), B(128), B(128), B(128), sl(Dd, 512, 640)
    ID, IDf, O17, ONES, CJ = B(128), F(128), B(128), B(512), B(512)
    ms(ONES, 1.0)
    asel(up, sl(ONES, 0, 128), [[-16, 8], [0, 16]], ge, 0, 1)
    asel(BO, up, [[16, 8], [0, 16]], ge, 15, -1)
    asel(TRI, BO, [[1, 128]], ge, 0, -1)
    asel(SH, BO, [[-1, 128]], eq, -1, 1)
    Z, Z4, ZP, Z0, Z1, Z32, ZI4, Z0n = [B(144) for k in range(8)]
    Z0f, BOf = F(144), F(128)
    ts(Z, R144, z15, eq)
    ts(Z0, Z, d0c, mul)
    ts(Z1, Z, d1c, mul)
    ts(Z0n, Z0, -32768.0, mul)
    cp(Z0f, Z0)
    ts(Z4, Z, 4.0, mul)
    ts(Z32, Z, 32.0, mul)
    p2, p2f = B(1), F(1)
    act(p2, pi, Fn.Exp, scale=math.log(2.0))
    cp(p2f, p2)
    ts(ZP, Z, p2f, mul)
    cp(BOf, BO)
    ts(BOP, BO, pi, mul)
    ts(BOm, BO, -16.0, mul)
    ts(ID, R128, pc, eq)
    cp(IDf, ID)
    iota(O17, [[0, 128]], 17, 0)
    iota(CJ, [[-1, 4], [0, 128]], 4, 0)
    WM = {1: ID}
    for w in (507904, -0.5, -1, 4, 5, 16, 128, 512):
        WM[w] = B(128)
        ts(WM[w], ID, float(w), mul)
    tt(TRH, TRI, WM[-0.5], sub)
    I16, NI16 = B(32), B(32)
    ts(I16, sl(RI, 0, 32), pi, eq)
    ts(NI16, I16, -16384.0, mul, 16384.0, add)
    EI = B(2048)
    for i in range(4):
        asel(sl(EI, 512 * i, 512 * i + 512), ONES, [[-1, 4], [-16, 8], [0, 16]], eq, -4 * i, 1)
    ts(cin(2), cin(0), 3, band)
    ts(cin(3), cin(0), 2, shr, 3, band)
    cp(col(15), cin(3))
    ts(ZI4, Z, col(15), mul)
    ts(fr, cin(2), 4.0, mul, gb, add)
    ts(col(9), cin(3), 12.0, add, gb, add)
    ts(col(10), fr, 3.0, add)
    ZQ, ZB, ZBb = sl(WB, 4096, 4096 + 576), F(576), B(576)
    zq, zb = sl(Dd, 0, 144), sl(Dd, 144, 288)
    ts(zq, R144, col(9), eq)
    ts(zb, R144, col(10), eq)
    for j in range(4):
        ts(col(36 + j), cin(3), float(j), eq)
        ts(col(40 + j), cin(2), float(j), eq)
        ts(sl(ZQ, 144 * j, 144 * j + 144), zq, col(40 + j), mul)
        ts(sl(ZB, 144 * j, 144 * j + 144), zb, col(36 + j), mul)
    cp(ZBb, ZB)
    DUM, LB32, ZR, DUC, CAPS, d9, d9r = F(128), U(32), F(928), F(36), B(576), F(56), F(56)
    DUL = sl(DUM, 0, 56)
    ts(DUM, sl(NI, 0, 128), 8192.0, add)
    ts(DUC, sl(NI, 0, 36), float(CAP), add)
    ts(d9, sl(NI, 0, 56), 912.0, add)
    ts(d9r, sl(NI, 0, 56), -112.0, add)
    iota(ZR, [[0, 928]], 0, 0)
    ms(CAPS, float(CAP))
    PR = F(8)
    cp(sl(PR, 0, 6), sl(pari, 0, 6))
    lo, th, hi, Kc = [sl(PR, k, k + 1) for k in range(4)]
    ts(col(16), lo, 16.0, mul)
    ti, tj, tf = I(32), I(32), F(32)
    cp(ti, sl(NI, 0, 32))
    ts(tj, ti, 5, shr)
    ts(ti, ti, 31, band)
    ts(tj, tj, Kc, mul)
    ts(tj, tj, 15, band)
    ts(tf, tj, 32.0, mul)
    tt(tf, tf, ti, add)
    cp(LB32, tf)
    ts(DLO, ID, col(16), mul)
    ms(sl(X[0], 0, 16), 0.0)
    ms(sl(X[1], 0, 16), 16.0)
    ms(sl(XP, 0, 16), 16.0)
    ts(col(12), Kc, -1.0, mul)
    ts(cin(5), sl(pari, 3, 4), 7, band)
    for k, m in ((5, 63), (8, 4095)):
        ts(cin(k + 1), cin(k), col(12), mul, 2.0, add)
        ts(cin(k + 1), cin(k + 1), m, band)
        tt(cin(k + 2), cin(k), cin(k + 1), mul)
        ts(cin(k + 3), cin(k + 2), m, band)
    ts(cin(12), cin(11), Kc, mul)
    ts(cin(12), cin(12), 8191, band)
    tt(cin(13), cin(11), cin(12), add)
    ts(cin(13), cin(13), -1.0, add)
    ts(cin(14), cin(13), 127, band)
    ts(cin(15), cin(13), 7, shr)
    cp(sl(cf, 13, 15), sl(ci, 14, 16))
    kl, kh = col(13), col(14)
    rot = [0]
    LI, LH = [I(384), I(384)], [H(384), H(384), H(896)]

    def lin(xi, fields, bank):
        n = wid(xi)
        rot[0] += 1
        out = ps(bank, 0, n)
        a, b = LI[rot[0] % 2], LH[rot[0] % 2]
        for k, (s, m, w) in enumerate(fields):
            ts(sl(a, k * n, k * n + n), xi, s, shr, m, band)
        cp(sl(b, 0, n * len(fields)), sl(a, 0, n * len(fields)))
        mm([(out, WM[w], sl(b, k * n, k * n + n), k == 0, k == len(fields) - 1) for k, (s, m, w) in enumerate(fields)])
        return out

    def place2(xi, f1, f2, inv, out):
        n = wid(xi)
        a, b, c = I(n), I(n), F(n)
        ts(a, xi, f1[0], shr, f1[1], band)
        ts(b, xi, f2[0], shr, f2[1], band)
        ts(c, a, float(f1[2]), mul)
        tt(c, c, b, add)
        tt(c, c, inv, mx)
        cp(out, c)
    POSA = [(2, 15, 512), (0, 3, 128), (6, 127, 1)]
    POSW = [(0, 15, 512), (4, 511, 1)]

    TA, BP, t1 = F(512), F(512), F(512)
    cp(t1, dew)
    for j in range(4):
        last = None
        for a in range(4):
            last = mm([(ps(7, 128 * j, 128 * j + 128), sl(ZQ, 144 * j + 12 - 4 * a, 144 * j + 140 - 4 * a), sl(t1, a, 512, 4), a == 0, a == 3)], after=last)
    ts(TA, ps(7, 0, 512), 1.0, add)
    LW, TAB = [U(32), U(32)], [B(96), B(96)]
    lsi = I(512)
    for t in range(2):
        Ct = sl(PR, 4 + t, 5 + t)
        a, b, c = I(32), I(32), F(32)
        ts(a, sl(NI, 0, 32), Kc, mul, Ct, add)
        ts(b, a, 9, shr, 15, band)
        ts(a, a, 511, band)
        cp(LW[t], a)
        cp(c, b)
        act(sl(TAB[t], 0, 32), c, Fn.Exp, scale=-math.log(2.0))
        act(sl(TAB[t], 32, 64), c, Fn.Exp, scale=math.log(2.0))
        ts(sl(TAB[t], 64, 96), sl(TAB[t], 0, 32), 65536.0, mul)

    CB = []
    for k in range(2):
        CB.append({"CU": H(592), "Q": F(576) if k else sl(WA, 9696, 10240), "SW": sl(WB, 9088, 10592) if k else sl(WA, 8192, 9696), "CR": H(928),
                   "cl": U(64), "li": U(48), "st": H(48), "em": F(48), "cb": F(64)})
        ms(CB[k]["CU"], 0.0)

    def comp(k, NC, R, Pp, Tp, sb, w, base):
        c = CB[k]
        CU, Q, SW, CR, A = c["CU"], sl(c["Q"], 0, NC), c["SW"], sl(c["CR"], 0, R), NC // 16
        iota(sl(SW, 0, R), [[0, R]], 0, 0)
        scan(sl(CU, 1, NC + 1), Tp, sl(CAPS, 0, NC), 0.0, add, mn)
        mm(dg(ps(sb, 0, A + 1), sl(CU, 0, NC + 16), Z0))
        st, em, li = sl(c["st"], 0, A), sl(c["em"], 0, A), sl(c["li"], 0, A)
        cp(sl(c["st"], 0, A + 1), ps(sb, 0, A + 1))
        mm([(ps(sb, 64, 64 + A), SH, st, True, False), (ps(sb, 64, 64 + A), sl(Z0, 0, 128), sl(c["st"], 1, A + 1), False, True)])
        tt(em, ps(sb, 64, 64 + A), st, le)
        tt(em, em, sl(DUC, 0, A), mul)
        tt(em, em, st, mx)
        cp(li, em)
        mm(full(Pp, ID, sl(CU, 0, NC), False, True))
        cp(Q, Pp)
        cp(ind(sl(SW, 0, CAP + NC), li), sl(RI, 32, 32 + NC), True)
        scan(CR, sl(SW, 0, R), sl(SW, 0, R), 32.0, mx, mx)
        cl, cb = sl(c["cl"], 0, R // 16), sl(c["cb"], 0, R // 16)
        mm(dg(ps(sb, 128, 128 + R // 16), CR, Z0))
        ts(cl, ps(sb, 128, 128 + R // 16), -32.0, add)
        ts(cb, ps(sb, 128, 128 + R // 16), w, mul, base, add)
        return Q, CR, cl, cb

    OT, IT = F(56), F(56)
    DB, DA = F(928), F(896)
    SB, LS = B(896), U(512)
    ms(sl(DB, 896, 928), 0.0)
    for k, (tw, res) in enumerate(((axw, OT), (dew, IT))):
        w = (WA, WB)[k]
        Fl, OH = (sl(Dd, 4096, 4608), sl(Ab, 0, 512))[k], (sl(Dd, 6144, 7040), sl(Ab, 1024, 1920))[k]
        VAL, IW = sl(w, 0, 512), sl(w, 2048, 2048 + 1808)
        EV = H(896) if k == 0 else LH[2]
        SID = (DA, sl(DB, 0, 896))[k]
        b0 = 4 * k
        ts(Fl, tw, 8192.0, ge)
        mm([(ps(b0 + 1, 0, 512), BO, Fl, True, True)])
        mm([(ps(b0, 0, 512), TRH, Fl, True, False), (ps(b0, 0, 512), WM[-0.5], ONES, False, 2)])
        iota(sl(IW, 0, 912), [[0, 912]], 0, 0)
        ts(VAL, tw, 0.25, mul, -2032.0, add)
        Q, CR, cl, cb = comp(k, 512, 896, ps(b0, 0, 512), ps(b0 + 1, 0, 512), b0 + 2, 4.0, -128.0)
        tt(OH, ind(Q, cl), sl(RI, 1, 897), eq)
        tt(EV, ind(VAL, cl), OH, mul)
        o = ps(b0 + 3, 0, 56)
        mm(dg(o, EV, Z))
        z, li = F(56), U(56)
        if k == 0:
            oi, k2 = I(56), F(56)
            ts(oi, o, -16.0, add)
            ts(z, o, 0.0, eq)
            ts(oi, oi, 127, band)
            tt(z, z, d9r, mul)
            ts(k2, oi, 2.0, mul, 800.0, add)
            tt(z, z, o, sub)
            tt(z, z, k2, add)
        else:
            ts(z, o, 0.0, eq)
            tt(z, z, d9, mul)
            tt(z, o, z, add)
        cp(li, z)
        if k == 0:
            o2, nl0 = ps(2, 256, 312), U(56)
            mm(dg(o2, OH, ZI4))
            tt(cb, o2, cb, add)
            cp(nl0, cb)
            cp(SB, ind(XV[0], nl0))
            ms(sl(Qb, 16, 912), 0.0)
            cp(ind(sl(Qb, 0, 1808), li), SB)
            exch(sl(Qb, 16, 912), XL[0], 128)
        mm(full(ps(b0, 0, 896), WM[16], CR, True, False) + full(ps(b0, 0, 896), BOP, OH, False, True))
        ts(SID, ps(b0, 0, 896), -479.0, add)
        cp(ind(IW, li), SID, True)
        o = ps(b0 + 2, 320, 376)
        mm(dg(o, sl(IW, 16, 912), Z0f))
        if k == 0:
            ui, LO = I(56), U(56)
            ts(ui, o, -33.0, add, 0.0, mx)
            ts(ui, ui, 2, shr)
            cp(LO, ui)
        ts(res, o, -32.0, add, 0.0, mx)

    for i in range(16):
        ts(sl(BP, i, 512, 16), sl(axB, 32 * i, 32 * i + 32), 33.0, add)
    dma([(pp(sl(WA, 0, 8192), R8), sl(ZR, 0, 512))])
    dma([(pp(sl(WB, 0, 8192), R8), BP)])

    def send_x(k):
        cp(sl(SB, 0, 448), ind(XV[k % 2], sl(LO, 0, 28)))
        cp(sl(SB, 448, 896), ind(XV[k % 2], sl(LO, 28, 56)))
        exch(SB, XL[k % 2], 128)

    def lst(j, a, b): return sl(LS, 128 * j + a // 16, 128 * j + b // 16)

    def rem16(y, o, q):
        ts(q, o, -7.5, add)
        tt(y, o, q, sub)

    def step(k, mod):
        w, x, y = X[k % 2], XV[k % 2], XV[(k + 1) % 2]
        nd = 0 if mod else ND0
        for bank, a in enumerate(range(nd, 2048, 512)):
            b = min(a + 512, 2048)
            o = ps(bank, 0, b - a)
            last = mm([(o, ID, sl(x, a, b), True, False)] + ([(o, O17, sl(ONES, 0, b - a), False, False)] if mod else []))
            for j in range(4):
                v = sl(Dd, 2048 * j + a, 2048 * j + b)
                cp(v, ind(w, lst(j, a, b)))
                last = mm([(o, ID, v, False, j == 3)], after=last)
            if mod:
                rem16(sl(y, a, b), o, sl(Qb, a, b))
                dma([(sl(Qb, a, b), sl(y, a, b))])
            else:
                cp(sl(y, a, b), o)
        h = nd // 2
        for j in range(4 if nd else 0):
            for a in (0, h):
                acc = sl(Qb, a, a + h)
                tt(acc if j < 3 else sl(y, a, a + h), ind(w, lst(j, a, a + h)), acc if j else sl(Y3, a, a + h), add)

    CP3 = [(0, 0, 0), (1, 0, 0), (0, 0, 1), (1, 0, 1)][:NC3]
    MKE, LK, LM, LO3 = F(896), U(56), U(56), U(56)
    NK, FT, G1, CT, CG, cmpf = sl(Ab, 0, 512), sl(Ab, 512, 1024), sl(Ab, 1024, 1536), sl(Qb, 0, 768), sl(Qb, 768, 1696), sl(Ab, 1536, 1792)
    VAC, FLk = sl(Ab, 0, 512), sl(Qb, 0, 896)
    FG, Y1i, Wc = B(576), axw, F(32)
    ms(sl(FG, 568, 576), 0.0)
    mark, high = dict(TOP), dict(TOP)

    for t in range(2):
        fin = t == 1
        for a in TOP:
            high[a] = TOP[a]
            TOP[a] = mark[a]
        Ct = sl(PR, 4 + t, 5 + t)
        k0 = 3 * t
        ts(lsi, TA, 0.25, mul, 15.375 - 8 * t, add)
        cp(LS, lsi)
        if fin:
            ts(dew, TA, -32.0, add, 0.0, mx)
            cp(TA, dew)
            dma([(pp(sl(WA, 0, 8192), R8), TA)])
            ts(axB, BP, -32.0, add, 0.0, mx)
            cp(BP, axB)
            dma([(pp(sl(WB, 0, 8192), R8), BP)])
        if t == 0:
            step(0, False)
        send_x(k0 + 1)
        ts(PAY, TA, 1.0 / 16384, mul, -1.0 / 16384, add)
        ts(VAC, TA, 0.0, eq, 2048.0, mul)
        hd0, hd1, nh, pd1, pdj, c, e = [F(56) for k in range(7)]
        a, b, u, un, uz = [I(56) for k in range(5)]
        ts(a, IT, -1.0, add, 0.0, mx)
        ts(nh, IT, 0.5, lt)
        ts(b, a, 6, shr)
        cp(LK, b)
        ts(b, a, 2, shr, 15, band)
        ts(c, nh, 16.0, mul)
        tt(c, c, b, mx)
        cp(LM, c)
        iota(MKE, [[4, 896]], 8192, 0)
        tt(MKE, ind(NI16, LM), MKE, add)
        ts(u, OT, -1.0, add, 0.0, mx)
        tt(pd1, u, DUL, sub)
        ts(un, u, 2, shr)
        ts(uz, u, 3, band)
        if not fin:
            ts(hd1, OT, 0.5, ge, 16.0, mul)
            ts(e, uz, 0.0, eq, 2064.0, mul)
            tt(e, e, un, add)
            tt(e, e, hd1, add)
            cp(LO3, e)
            ts(dew, TA, 0.25, mul, 0.125, add)
            ts(RAW, lsi, 2065.0, mul, -30960.0, add)
            ts(HELD, dew, 2064.0, mul)
            tt(RAW, RAW, HELD, sub)
        else:
            ts(hd0, IT, 0.5, ge)
            ts(hd1, OT, 0.5, ge)
            cp(LO3, un)
            ts(e, uz, 1.0, eq)
            tt(e, e, hd1, mul)
            pd0, p1 = F(56), F(56)
            o = lin(a, POSA, 5)
            tt(pd0, o, DUL, sub)
            tt(pd0, pd0, hd0, mul)
            tt(p1, pd0, DUL, add)
            bt, l1, l2, PABd = I(128), F(128), F(128), F(128)
            ts(bt, sl(BP, t, 512, 4), -1.0, add)
            o = lin(bt, POSA, 6)
            tt(PABd, o, DUM, sub)
            ts(l1, bt, 0.0, ge)
            ts(l2, bt, 8192.0, lt)
            tt(l1, l1, l2, mul)
            tt(PABd, PABd, l1, mul)
            ms(sl(XP, 0, 512), 0.0)
            for q in range(4):
                last = None
                for j in range(4):
                    last = mm([(ps(4, q, 512, 4), sl(ZB, 144 * q + 3 - j, 144 * q + 131 - j), sl(TA, 128 * j, 128 * j + 128), j == 0, j == 3)], after=last)
            cp(HELD, ps(4, 0, 512))
        j0, j1_, j2 = I(56), I(56), I(56)
        ts(j0, u, Ct, sub)
        ts(j0, j0, 8191, band)
        ts(j1_, j0, kh, mul)
        ts(j1_, j1_, 63, band)
        ts(j2, j0, kl, mul)
        ts(j1_, j1_, 128.0, mul)
        tt(j2, j2, j1_, add)
        o = lin(j2, POSW, 5)
        tt(pdj, o, DUL, sub)
        step(k0 + 1, True)
        send_x(k0 + 2)
        w, x, y = X[k0 % 2], XV[k0 % 2], (XV[0] if fin else Y3)
        far = ps(4, 0, 512)
        lf = mm([(far, ID, CJ, True, False), (far, WM[-1], VAC, False, False), (far, IDf, PAY, False, False)])
        SL, SBp = ps(5, 0, 128), ps(6, 0, 128)
        lsb = None
        for hf in range(2):
            lx = [mm([(ps(2 * hf + i, 0, 512), WM[5 - sum((hf, j, i) in CP3 for j in range(4))], sl(x, 1024 * hf + 512 * i, 1024 * hf + 512 * i + 512), True, False),
                      (ps(2 * hf + i, 0, 512), O17, ONES, False, False)]) for i in range(2)]
            for j in range(4):
                ab = sl(Ab, 1024 * (j % 2), 1024 * (j % 2) + 1024)
                for i in range(2):
                    a = 1024 * hf + 512 * i
                    d = sl(Dd, 2048 * j + a, 2048 * j + a + 512)
                    if (hf, j, i) in CP3:
                        act(d, ind(w, lst(j, a, a + 512)))
                        mm([(ps(7, 0, 512), ID, d, True, False), (ps(7, 0, 512), WM[-1], sl(x, a, a + 512), False, True)])
                        act(sl(ab, 512 * i, 512 * i + 512), ps(7, 0, 512), Fn.Abs)
                    else:
                        tt(d, ind(w, lst(j, a, a + 512)), sl(Qb, a, a + 512), sub)
                        act(sl(ab, 512 * i, 512 * i + 512), d, Fn.Abs)
                    lx[i] = mm([(ps(2 * hf + i, 0, 512), ID, d, False, j == 3)], after=lx[i])
                c = 128 * j + 64 * hf
                lf = mm(dg(ps(4, c, c + 64), ab, Z4, False, hf == 1 and j == 3), after=lf)
            for i in range(2):
                a = 1024 * hf + 512 * i
                rem16(sl(y, a, a + 512), ps(2 * hf + i, 0, 512), sl(Qb, a, a + 512))
            mm(dg(ps(5, 64 * hf, 64 * hf + 64), sl(y, 1024 * hf, 1024 * hf + 1024), Z))
            lsb = mm([(SBp, sl(Z, 15 - ii, 143 - ii), sl(y, 128 * ii, 128 * ii + 128), ii == 0, ii == 15) for ii in range(8 * hf, 8 * hf + 8)], after=lsb)
        if fin:
            dma([(dr("yx", 0, 2048), y)])
            dma([(pp(sl(Dd, 0, 8192), R8), sl(XP, 0, 512))])
        h2, m1, m2, dk, thf, nka, tp = F(256), F(256), F(128), F(128), F(128), F(128), F(128)
        ri, pay, zi, lb, lbu = I(128), I(128), I(128), F(128), U(128)
        ts(dk, SL, hi, lt, 1000.0 + NOL, mul)
        if fin:
            ts(thf, SL, th, lt)
        else:
            ts(thf, SL, th, ge, -1e9, mul)
        ts(nka, SBp, lo, ge)
        cp(h2, ps(4, 256, 512))
        tt(m1, ps(4, 0, 256), h2, mx)
        tt(m2, sl(m1, 0, 128), sl(m1, 128, 256), mx)
        tt(m2, m2, dk, mx)
        ts(ri, m2, NOL, mx, 16384.0, mul)
        ts(pay, ri, 16383, band)
        for q in range(2):
            tt(sl(FLk, 448 * q, 448 * q + 448), ind(pay, sl(LK, 28 * q, 28 * q + 28)), sl(MKE, 448 * q, 448 * q + 448), eq)
        ts(zi, ri, 13, shr, 1, band)
        ts(ri, ri, 8191, band)
        tt(lb, DUM, zi, mul)
        tt(lb, lb, ri, mx)
        cp(lbu, lb)
        for a in range(0, 128, 32):
            cp(ind(sl(WB, 0, 10240), sl(lbu, a, a + 32)), sl(ZR, 0, 512), True)
        ts(tp, pay, 1.0, add)
        for j in range(4):
            tt(sl(NK, 128 * j, 128 * j + 128), sl(TA, 128 * j, 128 * j + 128), tp, ne)
        dma([(BP, pp(sl(WB, 0, 8192), R8))])
        tt(sl(BP, t, 512, 4), sl(BP, t, 512, 4), nka, mul)
        gq, ng, b, bu, bj, bju = F(56), F(56), F(56), U(56), F(56), U(56)
        if not fin:
            for q in range(4):
                a = 512 * q
                mm([(ps(q, 0, 512), BOm, sl(y, a, a + 512), True, False), (ps(q, 0, 512), DLO, ONES, False, True)])
                tt(sl(XV[1], a, a + 512), ps(q, 0, 512), sl(y, a, a + 512), mx)
                ts(sl(XV[1], a, a + 512), sl(XV[1], a, a + 512), 16.0, mn)
            cp(sl(SB, 0, 448), ind(sl(XP, 0, 4128), sl(LO3, 0, 28)))
            cp(sl(SB, 448, 896), ind(sl(XP, 0, 4128), sl(LO3, 28, 56)))
            for q in range(2):
                a = 448 * q
                mm([(ps(2 + q, 0, 448), sl(Z32, 14, 142), sl(FLk, a, a + 448), True, False), (ps(2 + q, 0, 448), ID, sl(SB, a, a + 448), False, True)])
                cp(sl(SB, a, a + 448), ps(2 + q, 0, 448))
            exch(SB, XL[1], 128)
            go, alive, gO, aI = F(56), F(56), F(56), F(56)
            mm(dg(ps(6, 128, 184), SB, Z0) + dg(ps(6, 192, 248), FLk, Z))
            ts(alive, ps(6, 128, 184), 16.0, lt)
            cp(go, ps(6, 192, 248))
            tt(HELD, RAW, NK, mul)
            cp(LS, HELD)
            mm(dg(ps(7, 0, 56), XL[1], Z1))
            ts(gO, ps(7, 0, 56), 32.0, ge)
            mm(dg(ps(6, 256, 312), XL[1], Z0))
            ts(aI, ps(6, 256, 312), 16.0, lt)
            FLp = ps(0, 0, 512)
            lf = mm([(FLp, WM[507904], ONES, True, False)])
            for hf in range(2):
                for j in range(4):
                    for a in (1024 * hf, 1024 * hf + 512):
                        cp(sl(Dd, 2048 * j + a, 2048 * j + a + 512), ind(XP, lst(j, a, a + 512)))
                    c = 128 * j + 64 * hf
                    lf = mm(dg(ps(0, c, c + 64), sl(Dd, 2048 * j + 1024 * hf, 2048 * j + 1024 * hf + 1024), Z0n, False, hf == 1 and j == 3), after=lf)
        else:
            kac, la, lau = F(128), F(128), U(128)
            ts(kac, SBp, lo, lt)
            tt(la, kac, PABd, mul)
            tt(la, la, DUM, add)
            cp(lau, la)
            for a in range(0, 128, 32):
                cp(ind(WA, sl(lau, a, a + 32)), sl(ZR, 0, 512), True)
            SBL, LBL, lw = B(112), B(112), F(56)
            go, alive = sl(SBL, 0, 112, 2), sl(SBL, 1, 112, 2)
            cp(sl(SB, 0, 448), ind(y, sl(LO3, 0, 28)))
            cp(sl(SB, 448, 896), ind(y, sl(LO3, 28, 56)))
            mm(dg(ps(3, 0, 56), SB, Z))
            ts(lw, ps(3, 0, 56), lo, lt)
            tt(lw, lw, e, mul)
            tt(alive, hd1, lw, sub)
            mm(dg(ps(2, 0, 56), FLk, Z))
            cp(go, ps(2, 0, 56))
            exch(SBL, LBL, 16)
            gO, aI = sl(LBL, 0, 112, 2), sl(LBL, 1, 112, 2)
            a, au = F(56), U(56)
            tt(a, aI, pd0, mul)
            tt(a, p1, a, sub)
            cp(au, a)
            cp(ind(sl(WA, 0, 9088), au), sl(ZR, 0, 896), True)
            dma([(TA, pp(sl(WA, 0, 8192), R8))])
            tt(NK, TA, NK, mn)
        tt(gq, gO, alive, mul)
        tt(bj, gq, pdj, mul)
        tt(bj, bj, DUL, add)
        cp(bju, bj)
        LJ = sl(Qb, 1536, 2048)
        if fin:
            cp(ind(Dd, sl(bju, 0, 28)), sl(ONES, 0, 448))
            cp(ind(Dd, sl(bju, 28, 56)), sl(ONES, 0, 448))
            dma([(LJ, pp(sl(Dd, 0, 8192), R8))])
        else:
            cp(ind(sl(WA, 0, 9088), bju), sl(RI, 32, 928), True)
            dma([(PAY, pp(sl(WA, 0, 8192), R8))])
            act(LJ, PAY, Fn.Sign)
            dma([(pp(sl(WB, 0, 8192), R8), BP)])
        tt(ng, alive, gq, sub)
        tt(b, gO, pd1, mul)
        tt(b, b, DUL, add)
        cp(bu, b)
        cp(ind(sl(WB, 0, 9088), bu), sl(ZR, 0, 896), True)
        z0 = 8 * (6 - t)
        fre, cs8, Qf, qb, nlv = B(8), F(16), F(8), F(8), F(32)
        ts(fre, sl(ng, z0, z0 + 8), -1.0, mul, 1.0, add)
        mm([(ps(2, 64, 72), TRI, fre, True, True), (ps(2, 80, 88), BO, fre, True, True)])
        ms(sl(cs8, 0, 1), 0.0)
        scan(sl(cs8, 1, 9), ps(2, 80, 88), sl(CAPS, 0, 8), 0.0, add, mn)
        tt(Qf, ps(2, 64, 72), sl(cs8, 0, 8), add)
        ts(qb, Qf, -1.0, mul, 0.5, add)
        for c in range(8):
            act(sl(cmpf, 32 * c, 32 * c + 32), sl(RI, 0, 32), Fn.Sign, bias=sl(qb, c, c + 1))
        mm([(ps(3, 64, 96), BO, sl(cmpf, 32 * c, 32 * c + 32), c == 0, c == 7) for c in range(8)])
        one = 0.0 if fin else 33.0
        ts(nlv, ps(3, 64, 96), 2.0, mul, 8448.0 + 512 * t + one, add)
        tt(sl(FG, 0, 56), aI, nh, mul)
        act(G1, ind(BP, LW[t]), Fn.Sign, bias=0.5 if fin else 32.5, scale=-1.0)
        mm(dg(ps(6, 0, 32), G1, ZP))
        W0, wv, wh, wr = F(32), F(32), I(32), I(32)
        ts(Wc, ps(6, 0, 32), 0.5, mul, 32768.0, add)
        ts(W0, ps(6, 0, 32), 0.5, mul, 32767.5, add)
        tt(wv, Wc, sl(TAB[t], 0, 32), mul)
        ts(wh, wv, -0.5, add)
        tt(wv, wh, sl(TAB[t], 32, 64), mul)
        tt(wv, W0, wv, sub)
        tt(wv, wv, sl(TAB[t], 64, 96), mul)
        tt(wr, wv, wh, add)
        for s in range(16):
            ts(sl(Y1i, 32 * s, 32 * s + 32), wr, s, shr, 1, band)
        cp(sl(FG, 56, 568), ind(Y1i, LB32))
        for bank, l in ((4, BO), (2, TRI)):
            mm([(ps(bank, 0, 512), l, sl(FG, 0, 512), True, False), (ps(bank, 56, 512), l, sl(LJ, 0, 456), False, 1 + (bank == 2)),
                (ps(bank, 512, 576), l, sl(FG, 512, 576), True, False), (ps(bank, 512, 568), l, sl(LJ, 456, 512), False, 1 + (bank == 2))])
        for j in range(4):
            if fin:
                tt(sl(FT, 128 * j, 128 * j + 128), sl(NK, 128 * j, 128 * j + 128), thf, lt)
            else:
                tt(sl(FT, 128 * j, 128 * j + 128), ps(0, 128 * j, 128 * j + 128), thf, lt)
        if not fin:
            ts(TA, TA, 32.0, add)
            tt(TA, FLp, TA, mn)
            dma([(pp(sl(WA, 0, 8192), R8), TA)])
        for a in range(4):
            mm([(ps(1, a, 512, 4), sl(ZBb, 144 * a + 3 - j, 144 * a + 131 - j), sl(FT, 128 * j, 128 * j + 128), j == 0, j == 3) for j in range(4)])
        cp(G1, ps(1, 0, 512))
        mm([(ps(1, 0, 512), BO, G1, True, True)])
        mm([(ps(0, 0, 512), TRI, G1, True, 2)])
        QG, CRG, clG, cbG = comp(1, 576, 928, ps(2, 0, 576), ps(4, 0, 576), 7, 16.0, -1408.0)
        QT, CRT, clT, cbT = comp(0, 512, 768, ps(0, 0, 512), ps(1, 0, 512), 6, 16.0, -512.0)
        if fin:
            for a in range(4):
                mm([(ps(4, a, 512, 4), sl(ZBb, 144 * a + 3 - j, 144 * a + 131 - j), sl(NK, 128 * j, 128 * j + 128), j == 0, j == 3) for j in range(4)])
            tt(HELD, ps(4, 0, 512), HELD, mul)
            ts(HELD, HELD, -1.0, add)
            dma([(pp(sl(WA, 0, 8192), R8), HELD)])
            dma([(PAY, pp(sl(WB, 0, 8192), R8))])
            tt(sl(PAY, t, 512, 4), sl(PAY, t, 512, 4), nka, mul)
            for i in range(16):
                ts(sl(BP, 32 * i, 32 * i + 32), sl(PAY, i, 512, 16), -1.0, add)
            dma([(pp(sl(WB, 512 * i, 512 * i + 512), R8), sl(BP, 32 * i, 32 * i + 32)) for i in range(16)])
        tt(CT, ind(QT, clT), sl(RI, 0, 768), le)
        mm(dg(ps(6, 256, 304), CT, Z))
        mm([x_ for a, b in ((0, 512), (512, 768)) for x_ in
            ((ps(0, a, b), BO, sl(CRT, a, b), True, False), (ps(0, a, b), BO, sl(CT, a, b), False, True))])
        ts(sl(DB, 0, 768), ps(0, 0, 768), -512.0 + one, add)
        si = I(48)
        tt(si, ps(6, 256, 304), cbT, add)
        cn = F(8)
        nT, nG, nl, mc, r0, lim, l2 = [sl(cn, k, k + 1) for k in range(7)]
        ts(nT, sl(CB[0]["CU"], 512, 513), 768.0, mn)
        cp(nG, sl(CB[1]["CU"], 576, 577))
        cp(nl, sl(CB[1]["CU"], 56, 57))
        tt(mc, nT, nG, mn)
        tt(r0, mc, nl, mx)
        ts(l2, sl(cs8, 8, 9), 32.0, mn, r0, add)
        tt(lim, l2, nG, mn)
        rr, rru = F(2), U(2)
        ts(rr, sl(NI, 0, 2), r0, add)
        cp(rru, rr)
        cp(ind(DB, rru), nlv)
        vA, pa, pau, D48, D58 = F(48), F(48), U(48), sl(DUM, 0, 48), sl(DUM, 0, 58)
        ts(vA, sl(NI, 0, 48), mc, ge)
        tt(vA, vA, D48, mul)
        if fin:
            place2(si, POSW[0], POSW[1], vA, pau)
        else:
            tt(pa, lin(si, POSA, 6), vA, mx)
            cp(pau, pa)
        tt(CG, ind(QG, clG), sl(RI, 0, 928), le)
        o = ps(7, 256, 314)
        mm(dg(o, CG, Z))
        j1, u0, ui, isl, lv = F(58), I(58), I(58), F(48), F(48)
        o48 = sl(j1, 0, 48)
        tt(j1, o, cbG, add)
        ts(u0, j1, Kc, mul, Ct, add)
        ts(isl, o48, 0.0, lt)
        ts(lv, o48, 4.0, mul, 11776.0, add)
        ts(ui, u0, 8191, band)
        u48 = sl(ui, 0, 48)
        gv, gh, gl = F(48), H(48), H(48)
        tt(lv, lv, isl, mul)
        tt(gv, lv, u48, mx)
        if not fin:
            gi, gf, gu, pvu, XG = I(48), F(48), U(48), U(48), sl(SB, 0, 768)
            cp(gi, gv)
            ts(gi, gi, 2, shr)
            ts(gf, isl, 2064.0, mul, 16.0, add)
            tt(gf, gf, gi, add)
            cp(gu, gf)
            cp(XG, ind(XP, gu))
            place2(si, (0, 3, 2048), (2, 2047, 1), vA, pvu)
            cp(ind(Dd, pvu), XG)
            for q, bank in enumerate((0, 1, 4, 5)):
                a = 512 * q
                last = mm([(ps(bank, 0, 512), ID, sl(Y3, a, a + 512), True, False)])
                mm([(ps(bank, 0, 512), ID, sl(Dd, 2048 * j + a, 2048 * j + a + 512), False, j == 3) for j in range(4)], after=last)
                cp(sl(XV[0], a, a + 512), ps(bank, 0, 512))
            gv0, gv = gv, F(48)
            ts(gv, gv0, 33.0, add)
        cp(gh, gv)
        tt(gl, gv, gh, sub)
        for bk, (a, b) in enumerate(((0, 32), (32, 48))):
            mm([(ps(2 + bk, i, 16 * (b - a), 16), sl(EI, 128 * i, 128 * i + 128), sl(s_, a, b), s_ is gh, s_ is gl) for i in range(16) for s_ in (gh, gl)])
            cp(sl(DA, 16 * a, 16 * b), ps(2 + bk, 0, 16 * (b - a)))
            cp(ind(WA, sl(pau, a, b)), sl(DA, 16 * a, 16 * b), not fin)
        if fin:
            dma([(dr("yd", 0, 512), pp(sl(WA, 0, 8192), R8))])
        else:
            dma([(TA, pp(sl(WA, 0, 8192), R8))])
        pb, pbu, vb, v2 = F(58), U(58), F(58), F(58)
        ts(vb, sl(NI, 0, 58), nl, lt)
        ts(v2, sl(NI, 0, 58), lim, ge)
        tt(vb, vb, v2, mx)
        tt(vb, vb, D58, mul)
        if fin:
            place2(u0, POSW[0], POSW[1], vb, pbu)
        else:
            tt(pb, ui, vb, mx)
            cp(pbu, pb)
        for a, b in ((0, 30), (30, 58)):
            cp(ind(sl(WB, 0, 9120), sl(pbu, a, b)), sl(DB, 16 * a, 16 * b), not fin)
        if fin:
            dma([(dr("ya", 0, 512), pp(sl(WB, 0, 8192), R8))])
            for a in TOP:
                TOP[a] = max(TOP[a], high[a])
            continue
        dma([(BP, pp(sl(WB, 0, 8192), R8))])
        uf, ra, rc, rp, mk, rw, RR, uci = F(64), I(2), U(2), U(2), F(32), F(32), F(32), I(2)
        cp(sl(uf, 0, 58), ui)
        cp(ra, rr)
        ts(uci, ra, 4, shr)
        cp(rc, uci)
        ts(ra, ra, 15, band)
        cp(rp, ra)
        cp(mk, ind(I16, rp))
        tt(rw, ind(sl(uf, 0, 58), rc), mk, mul)
        mm([(ps(6, 64, 96), BOf, rw, True, True)])
        cp(RR, ps(6, 64, 96))
        v, w, wu, row = F(56), F(56), U(56), MKE
        ts(v, sl(QG, 0, 56), mc, le)
        tt(v, v, sl(FG, 0, 56), mul)
        ts(w, sl(QG, 0, 56), -1.0, add)
        tt(w, w, v, mul)
        cp(wu, w)
        cp(row, ind(sl(DB, 0, 768), wu))
        mm(dg(ps(7, 64, 120), row, Z0f))
        ts(w, ps(7, 64, 120), -32.0, add)
        tt(w, w, v, mul)
        tt(IT, IT, aI, mul)
        ts(v, go, -1.0, mul, 1.0, add)
        tt(IT, IT, v, mul)
        tt(IT, IT, w, add)
        nn, v8, w8, w8u, r8, r8h, r8l = F(1), F(8), F(8), U(8), F(128), H(128), H(128)
        tt(nn, nG, r0, sub)
        ts(nn, nn, 32.0, mn)
        ts(v8, Qf, nn, le)
        tt(v8, v8, fre, mul)
        ts(w8, Qf, -1.0, add)
        tt(w8, w8, v8, mul)
        cp(w8u, w8)
        cp(r8, ind(RR, w8u))
        cp(r8h, r8)
        tt(r8l, r8, r8h, sub)
        mm(dg(ps(6, 128, 136), r8h, Z0, True, False) + dg(ps(6, 128, 136), r8l, Z0, False, True))
        ts(w8, ps(6, 128, 136), 1.0, add)
        tt(w8, w8, v8, mul)
        tt(OT, OT, ng, mul)
        tt(sl(OT, z0, z0 + 8), sl(OT, z0, z0 + 8), w8, add)


def after_pos(lst, t):
    a, b = 0, len(lst)
    while a < b:
        m = (a + b) // 2
        if lst[m] <= t:
            a = m + 1
        else:
            b = m
    return a


def place(pr, pred, succ, back, bias):
    n = len(OPS)
    left = [len(p) for p in pred]
    ready, st, qq, cc = [0.0] * n, [0.0] * n, [None] * n, [0.0] * n
    busy = {q: ([], []) for q in "vapgsn"}
    heap = sorted((pr[k], k) for k in range(n) if left[k] == 0)
    while heap:
        k = heap.pop()[1]
        best = None
        for q, c in ALT[k]:
            S, E = busy[q]
            t = ready[k] + (LAT[k] if back else 0.0)
            m = len(S)
            i = m if m == 0 or E[-1] <= t else after_pos(E, t)
            while i < m and S[i] < t + c:
                t = E[i]
                i += 1
            v = t + c + (bias[k] if q == "v" else 0.0)
            if best is None or v < best[0]:
                best = (v, q, c, t, i)
        v, q, c, t, i = best
        S, E = busy[q]
        S.insert(i, t)
        E.insert(i, t + c)
        st[k], qq[k], cc[k] = t, q, c
        f = t + c + (0.0 if back else LAT[k])
        for s in succ[k]:
            if f > ready[s]:
                ready[s] = f
            left[s] -= 1
            if left[s] == 0:
                heap.insert(after_pos(heap, (pr[s], s)), (pr[s], s))
    end = max(st[k] + cc[k] + (0.0 if back else LAT[k]) for k in range(n))
    return end, st, qq, cc


def search(rounds):
    n = len(OPS)
    for o in OPS:
        ALT.append([(q, o["alt"][q][1]) for q in "av"] if "alt" in o else [(o["q"], o["cost"])])
        LAT.append(o["lat"] + HOP)
    pred = [sorted(o["pre"]) for o in OPS]
    succ = [[] for _ in range(n)]
    for k in range(n):
        for p in pred[k]:
            succ[p].append(k)
    pr = [0.0] * n
    for k in range(n - 1, -1, -1):
        pr[k] = ALT[k][0][1] + LAT[k] + max([pr[s] for s in succ[k]] + [0.0])
    x = [SEED]
    ty = [o["ty"] for o in OPS]

    def rnd(m):
        x[0] = (x[0] * 1103515245 + 12345) % 2147483648
        return (x[0] >> 8) % m

    def tryit(p, bias):
        e, st, qq, cc = place(p, pred, succ, False, bias)
        b = place([st[k] + cc[k] + LAT[k] for k in range(n)], succ, pred, True, bias)
        p2 = [b[1][k] + b[3][k] for k in range(n)]
        r = place(p2, pred, succ, False, bias)
        return (r, p2) if r[0] <= e else ((e, st, qq, cc), p)

    def score(r):
        st, qq, cc = r[1], r[2], r[3]
        order = sorted(range(n), key=lambda k: st[k])
        tot = r[0]
        for m in OTHER:
            free, fin = {q: 0.0 for q in "vapgsn"}, [0.0] * n
            for k in order:
                t = free[qq[k]]
                for p in pred[k]:
                    if fin[p] > t:
                        t = fin[p]
                t += cc[k] * m[ty[k]]
                free[qq[k]] = t
                fin[k] = t + LAT[k]
            tot += max(fin) * m["w"]
        return tot
    bias = [BIAS] * n
    best, bp = tryit(pr, bias)
    bs = score(best)
    for it in range(rounds):
        p, nb = list(bp), list(bias)
        for m in range(2):
            a, w, d = rnd(n), 1 + rnd(12), rnd(6000) - 3000.0
            for k in range(a, min(n, a + w)):
                p[k] += d
        a, w, d = rnd(n), 1 + rnd(20), (0.0, 300.0, 1000.0, 5000.0, -5000.0)[rnd(5)]
        for k in range(a, min(n, a + w)):
            nb[k] = d
        r, p2 = tryit(p, nb)
        if r[0] <= best[0] + 1500:
            s = score(r)
            if s <= bs:
                best, bp, bias, bs = r, p2, nb, s
    end, st, qq, cc = best
    order = sorted(range(n), key=lambda k: (st[k], k))
    sems, cnt, got = ["cv", "ca", "cp", "cg"], {}, None
    for k in order:
        o = OPS[k]
        if o["kind"] == "recv":
            got = k
        elif o["kind"] == "dma" and got is not None:
            o["pre"].add(got)
        if "alt" in o:
            o["q"] = qq[k]
            o["fn"], o["cost"] = o["alt"][qq[k]]
        o["t"] = st[k]
        if o["kind"] == "c":
            cnt[o["q"]] = cnt.get(o["q"], 0) + 1
            o["sig"] = ("c" + o["q"], cnt[o["q"]])
        else:
            sems.append("%s%d" % (o["kind"][0], k))
            o["sig"] = (sems[-1], 16 * o["n"] if o["kind"] == "dma" else 2 * (N - 1))
    return order, sems, end


build()
ORDER, SEMAPHORES, PLAN = search(ROUNDS)
SCRATCH = {k: ("sbuf", [128, TOP[k]], DTY[k]) for k in DTY}
for _k in range(4):
    SCRATCH["p%d" % _k] = ("psum", [128, 1024], "float32")


def rank_program(g, core, T, topo):
    rank = T.rank_of(core)
    if rank is None:
        return
    Q = {"v": g.vector, "a": g.scalar, "p": g.tensor, "g": g, "s": g.sync}
    seen = {q: {} for q in Q}
    top = {}

    def wait(q, sig):
        if seen[q].get(sig[0], 0) < sig[1]:
            Q[q].wait_ge(T.sem[sig[0]], sig[1])
            seen[q][sig[0]] = sig[1]

    for k in ORDER:
        o = OPS[k]
        q, sig = o["q"], o["sig"]
        top[sig[0]] = sig[1]
        if o["kind"] == "recv":
            continue
        need = {}
        for p in o["pre"]:
            s = OPS[p]["sig"]
            need[s[0]] = max(need.get(s[0], 0), s[1])
        for s in need.items():
            wait(q, s)
        if o["kind"] == "c":
            o["fn"](g, T).then_inc(T.sem[sig[0]], 1)
        elif o["kind"] == "dma":
            for x in o["fn"](g, T):
                x.then_inc(T.sem[sig[0]], 16)
        else:
            src, dst, w = o["fn"]
            far, near, trs = 0, 0, []
            for p in range(N - 1):
                c = T.cores[(rank - p - 1) % N]
                en = topo.engines(core, c)
                if topo.die(c) != topo.die(core):
                    pick = en[0::2][2 * far:2 * far + 2]
                    far += 1
                else:
                    pick = en[1::2][2 * near:2 * near + 2]
                    near += 1
                a = topo.addr(c)
                trs.append(RemoteDMATransfer(dst_ids=[DstId(rid=a[0], pnc=a[1])], dma_engine_mask=sum(1 << e for e in pick),
                                             remote_sem=T.sem[OPS[k + 1]["sig"][0]],
                                             src=ap(T, sl(src, w * p, w * p + w)), dst=ap(T, sl(dst, w * (6 - p), w * (6 - p) + w))))
            g.remote_dma_fused(trs, local_sem=T.sem[sig[0]])
    for s in top.items():
        wait("g", s)
